import numpy as np
import ml_dtypes


def mxq(x, axis, fmt="e4m3"):
    dtype, down = {"e4m3": (ml_dtypes.float8_e4m3fn, 7), "e5m2": (ml_dtypes.float8_e5m2, 14)}[fmt]
    v = np.moveaxis(np.asarray(x, np.float32).astype(ml_dtypes.bfloat16).astype(np.float64), axis, -1)
    blocks = v.reshape(v.shape[:-1] + (-1, 32))
    amax = np.abs(blocks).max(-1, keepdims=True)
    byte = np.maximum(np.where(amax > 0, np.frexp(amax)[1] - 1 + 127, 0) - down, 1)
    scale = np.exp2(byte - 127.0)
    codes = (blocks / scale).astype(np.float32).astype(dtype).astype(np.float64)
    return np.moveaxis((codes * scale).reshape(v.shape), -1, axis)


WIDE = False


def mx_kscale(k):
    if not WIDE:
        return np.ones(k)
    levels = np.array([18, -18])
    if k % 512:
        return np.exp2(np.random.permutation(np.resize(levels, k // 32))).repeat(32)
    a = np.empty((k // 512, 16))
    for p in range(k // 512):
        a[p, :8] = np.random.permutation(np.resize(levels, 8))
        for g in range(8):
            far = levels[np.abs(levels - a[p, g]) >= 10]
            a[p, g + 8] = far[np.random.randint(len(far))]
    return np.exp2(a.ravel()).repeat(32)


def f64(x):
    return np.asarray(x).astype(np.float64)


def striped(idx):
    return np.tile(np.asarray(idx).reshape(-1, 16).T, (8, 1)).astype(np.uint16)


def unstriped(offs):
    return offs[:16].T.reshape(-1).astype(np.int64)


B, N, T, D, R = 1, 512, 2048, 512, 1024


def setup_inputs():
    n = np.random.standard_normal
    idx = np.random.permutation(T)[:B * N]
    s = mx_kscale(D)[:, None]
    z = mx_kscale(R)[:, None]
    x = n((B, D, R))
    return {
        "xT": (x * s).astype(np.float32),
        "wT": (n((D, T)) * (0.50 / np.sqrt(D)) / s).astype(np.float32),
        "vT": (n((D, T)) * (0.50 / np.sqrt(D)) / s).astype(np.float32),
        "wt": (np.random.uniform(0.5, 1.5, (B, R, 1)) * N / np.sqrt(R) * z).astype(np.float32),
        "xm": (x.transpose(0, 2, 1) / z).astype(np.float32),
        "offs": striped(idx),
    }


def reference(xT, wT, vT, wt, xm, offs):
    idx = unstriped(offs)
    pick = lambda x: x[:, idx].reshape(x.shape[0], B, N).transpose(1, 0, 2)
    xq = mxq(f64(xT), 1, "e4m3").transpose(0, 2, 1)
    a = xq @ mxq(pick(f64(wT)), 1, "e4m3")
    av = xq @ mxq(pick(f64(vT)), 1, "e4m3")
    e = np.exp(a - a.max(-1, keepdims=True))
    f = np.exp(av - av.max(-1, keepdims=True))
    g = f64(wt) * (e / e.sum(-1, keepdims=True) - f / f.sum(-1, keepdims=True))
    dw = mxq(f64(xm), 1, "e4m3").transpose(0, 2, 1) @ mxq(g, 1, "e5m2")
    gw = np.zeros((D, T))
    gw[:, idx] = dw.transpose(1, 0, 2).reshape(D, B * N)
    return gw

@@ -1,0 +1,209 @@
+from contextlib import ExitStack
+
+import concourse.mybir as mybir
+
+N, T, D, R = 512, 2048, 512, 1024
+FLOPS = 3 * 2 * R * N * D
+
+F32 = mybir.dt.float32
+BF16 = mybir.dt.bfloat16
+U32 = mybir.dt.uint32
+I32 = mybir.dt.int32
+U16 = mybir.dt.uint16
+U8 = mybir.dt.uint8
+E4M3 = mybir.dt.float8_e4m3fn_x4
+E5M2 = mybir.dt.float8_e5m2_x4
+ALU = mybir.AluOpType
+ACT = mybir.ActivationFunctionType
+AXIS_X = mybir.AxisListType.X
+
+P = 128
+PACK = 4
+K_PASS = P * PACK
+ROW_PASSES = R // K_PASS
+X_SPLIT = 88
+G_SPLIT = 352
+
+
+def tile_attend_gds_kl_kernel(tc, xT, wT, vT, wt, xm, offs, out):
+    nc = tc.nc
+    with ExitStack() as ctx:
+        held = ctx.enter_context(tc.tile_pool(name="held", bufs=1))
+        raw = ctx.enter_context(tc.tile_pool(name="raw", bufs=10))
+        ring = ctx.enter_context(tc.tile_pool(name="ring", bufs=4))
+        psum = ctx.enter_context(tc.psum_pool(name="psum", bufs=8))
+
+        offsets = held.tile([P, N // 16], U16, name="offsets")
+        nc.sync.dma_start(offsets[:], offs)
+
+        def load(source, shape):
+            tile = raw.tile(shape, F32, name="raw")
+            nc.sync.dma_start(out=tile[:], in_=source)
+            return tile
+
+        w_rows = wT.rearrange("(p j) t -> p j t", j=PACK)
+        v_rows = vT.rearrange("(p j) t -> p j t", j=PACK)
+        x_rows = xT[0].rearrange("(p j) r -> p j r", j=PACK)
+        m_rows = xm[0].rearrange("(g p j) d -> g p j d", p=P, j=PACK)
+
+        weight = held.tile([P, ROW_PASSES, PACK], F32, name="weight")
+        nc.scalar.dma_start(out=weight[:], in_=wt[0].rearrange("(g p t) o -> p g (t o)", p=P, t=PACK))
+
+        zero = held.tile([P, 1], F32, name="zero")
+        warm = held.tile([P, 1], F32, name="warm")
+        nc.gpsimd.memset(zero[:], 0.0)
+        nc.scalar.activation(warm[:], zero[:], ACT.Exp)
+
+        windows = [held.tile([P, T], F32, name="window%d" % c) for c in range(D // P)]
+        for c, window in enumerate(windows):
+            engine = nc.vector if c < 2 else nc.gpsimd
+            engine.memset(window[:].bitcast(I32), 0)
+
+        def operand(name):
+            grouped = held.tile([P, K_PASS, PACK], BF16, name=name + "_grouped", align_bytes=64)
+            codes = held.tile([P, K_PASS], U32, name=name + "_codes", align_bytes=64)
+            scales = held.tile([P, K_PASS], U8, name=name + "_scales", align_bytes=64)
+            return grouped, codes, scales
+
+        def quantize(op, fmt):
+            grouped, codes, scales = op
+            nc.vector.quantize_mx(out=codes[:].bitcast(fmt), scales=scales[:],
+                                  in_=grouped[:].rearrange("p c j -> p (c j)"))
+
+        def matmul(acc, stationary, block, moving, moving_fmt, start, stop):
+            cols = slice(block * P, (block + 1) * P)
+            nc.tensor.matmul_mx(out=acc[:], lhsT=stationary[1][:, cols].bitcast(E4M3),
+                                lhsT_scale=stationary[2][:, cols],
+                                rhs=moving[1][:].bitcast(moving_fmt), rhs_scale=moving[2][:],
+                                start=start, stop=stop)
+
+        def copier(engine):
+            return nc.vector.tensor_copy if engine == "vector" else nc.scalar.copy
+
+        def interleave(engine, grouped, planes, lo, hi):
+            copier(engine)(out=grouped[:, lo:hi, :].rearrange("p (c i) j -> p c j i", i=PACK),
+                           in_=planes[:, :, lo:hi].rearrange("p j (c i) -> p c j i", i=PACK))
+
+        def interleave_x(engine, grouped, planes, lo, hi):
+            copier(engine)(out=grouped[:].rearrange("p (t m) j -> p m j t", t=PACK)[:, lo:hi],
+                           in_=planes[:].rearrange("p j (m t) -> p m j t", t=PACK)[:, lo:hi])
+
+        w_op = operand("w")
+        for j in range(PACK):
+            plane = load(w_rows[:, j, :], [P, T])
+            nc.vector.tensor_copy(w_op[0][:, :, j], plane[:].indirect(offsets[:]))
+        quantize(w_op, E4M3)
+
+        x_ops = [operand("x%d" % g) for g in range(ROW_PASSES)]
+        x_raw = [load(x_rows[:, :, g * K_PASS:(g + 1) * K_PASS], [P, PACK, K_PASS]) for g in range(ROW_PASSES)]
+        v_planes = [load(v_rows[:, j, :], [P, T]) for j in range(PACK)]
+        m_raw = [load(m_rows[g], [P, PACK, D]) for g in range(ROW_PASSES)]
+
+        interleave_x("vector", x_ops[0][0], x_raw[0], 0, X_SPLIT)
+        interleave_x("scalar", x_ops[0][0], x_raw[0], X_SPLIT, P)
+        quantize(x_ops[0], E4M3)
+        for q in range(4):
+            interleave_x("scalar", x_ops[1][0], x_raw[1], q * 32, (q + 1) * 32)
+        quantize(x_ops[1], E4M3)
+
+        def stats(name):
+            return held.tile([P, ROW_PASSES * PACK], F32, name=name)
+
+        def exps(table, tile_no, neg_max, total):
+            g, t = divmod(tile_no, PACK)
+            col = slice(tile_no, tile_no + 1)
+            acc = psum.tile([P, N], F32, name="acc")
+            matmul(acc, x_ops[g], t, table, E4M3, True, True)
+            nc.vector.tensor_reduce(out=neg_max[:, col], in_=acc[:], axis=AXIS_X, op=ALU.max, negate=True)
+            result = ring.tile([P, N], F32, name="exp")
+            nc.scalar.activation(result[:], acc[:], ACT.Exp, bias=neg_max[:, col], accum_out=total[:, col])
+            return result
+
+        weight_cols = weight[:].rearrange("p g t -> p (g t)")
+
+        def factors(cols, total, inverse, factor, sign):
+            nc.vector.reciprocal(inverse[:, cols], total[:, cols])
+            nc.vector.scalar_tensor_tensor(out=factor[:, cols], in0=inverse[:, cols], scalar=sign,
+                                           in1=weight_cols[:, cols], op0=ALU.mult, op1=ALU.mult)
+
+        v_op = operand("v")
+        v_pair = held.tile([P, 2, N], F32, name="v_pair")
+
+        def gather_v(j):
+            target = v_pair[:, j, :] if j < 2 else v_op[0][:, :, j]
+            nc.vector.tensor_copy(target, v_planes[j][:].indirect(offsets[:]))
+
+        gather_v(0)
+        gather_v(1)
+        nc.scalar.copy(out=v_op[0][:, :, 0:2], in_=v_pair[:].rearrange("p j i -> p i j"))
+        gather_v(2)
+        gather_v(3)
+        quantize(v_op, E4M3)
+
+        s_max, s_sum, s_inv, s_fac = stats("s_max"), stats("s_sum"), stats("s_inv"), stats("s_fac")
+        student = held.tile([P, ROW_PASSES * PACK, N], F32, name="student")
+        for pair in range(4):
+            tiles = [2 * pair, 2 * pair + 1]
+            e = [exps(w_op, n, s_max, s_sum) for n in tiles]
+            factors(slice(tiles[0], tiles[1] + 1), s_sum, s_inv, s_fac, 1.0)
+            for n, tile in zip(tiles, e):
+                nc.scalar.activation(student[:, n, :], tile[:], ACT.Copy, scale=s_fac[:, n:n + 1])
+
+        t_max, t_sum, t_inv, t_fac = stats("t_max"), stats("t_sum"), stats("t_inv"), stats("t_fac")
+        g_ops = [operand("g%d" % g) for g in range(ROW_PASSES)]
+        m_grouped = held.tile([P, D // P, ROW_PASSES, P, PACK], BF16, name="m_grouped", align_bytes=64)
+        m_codes = held.tile([P, D // P, ROW_PASSES, P], U32, name="m_codes", align_bytes=64)
+        m_scales = held.tile([P, D // P, ROW_PASSES, P], U8, name="m_scales", align_bytes=64)
+
+        def prepare_m(c):
+            for g in range(ROW_PASSES):
+                nc.scalar.copy(out=m_grouped[:, c, g].rearrange("p (c i) j -> p c j i", i=PACK),
+                               in_=m_raw[g][:, :, c * P:(c + 1) * P].rearrange("p j (c i) -> p c j i", i=PACK))
+            nc.vector.quantize_mx(out=m_codes[:, c].rearrange("p g m -> p (g m)").bitcast(E4M3),
+                                  scales=m_scales[:, c].rearrange("p g m -> p (g m)"),
+                                  in_=m_grouped[:, c].rearrange("p g m j -> p (g m j)"))
+
+        g_planes = [held.tile([P, PACK, N], BF16, name="g_planes%d" % g) for g in range(ROW_PASSES)]
+        z = {}
+
+        def combine(tiles):
+            factors(slice(tiles[0], tiles[-1] + 1), t_sum, t_inv, t_fac, -1.0)
+            for n in tiles:
+                g, t = divmod(n, PACK)
+                nc.vector.scalar_tensor_tensor(out=g_planes[g][:, t, :], in0=z[n][:], scalar=t_fac[:, n:n + 1],
+                                               in1=student[:, n, :], op0=ALU.mult, op1=ALU.add)
+
+        for pair in range(4):
+            for n in (2 * pair, 2 * pair + 1):
+                z[n] = exps(v_op, n, t_max, t_sum)
+            if pair > 0:
+                combine([2 * pair - 2, 2 * pair - 1])
+            if pair == 2:
+                for q in range(4):
+                    interleave("scalar", g_ops[0][0], g_planes[0], q * P, (q + 1) * P)
+        combine([6])
+        combine([7])
+        interleave("vector", g_ops[1][0], g_planes[1], 0, G_SPLIT)
+        interleave("scalar", g_ops[1][0], g_planes[1], G_SPLIT, N)
+        quantize(g_ops[0], E5M2)
+        prepare_m(0)
+        quantize(g_ops[1], E5M2)
+
+        def product(c):
+            acc = psum.tile([P, N], F32, name="acc")
+            for g in range(ROW_PASSES):
+                nc.tensor.matmul_mx(out=acc[:], lhsT=m_codes[:, c, g].bitcast(E4M3), lhsT_scale=m_scales[:, c, g],
+                                    rhs=g_ops[g][1][:].bitcast(E5M2), rhs_scale=g_ops[g][2][:],
+                                    start=g == 0, stop=g == ROW_PASSES - 1)
+            dw = ring.tile([P, N], F32, name="dw")
+            nc.scalar.copy(out=dw[:], in_=acc[:])
+            return dw
+
+        dw = product(0)
+        for c in range(D // P):
+            if c + 1 < D // P:
+                prepare_m(c + 1)
+                following = product(c + 1)
+            nc.vector.tensor_copy(windows[c][:].indirect(offsets[:]), dw[:])
+            nc.sync.dma_start(out=out[c * P:(c + 1) * P, :], in_=windows[c][:])
+            dw = following

@@ -21,7 +21,6 @@ P = 128
 PACK = 4
 K_PASS = P * PACK
 ROW_PASSES = R // K_PASS
-X_SPLIT = 88
 G_SPLIT = 352
 
 
@@ -29,15 +28,15 @@ def tile_attend_gds_kl_kernel(tc, xT, wT, vT, wt, xm, offs, out):
     nc = tc.nc
     with ExitStack() as ctx:
         held = ctx.enter_context(tc.tile_pool(name="held", bufs=1))
-        raw = ctx.enter_context(tc.tile_pool(name="raw", bufs=10))
+        raw = ctx.enter_context(tc.tile_pool(name="raw", bufs=1))
         ring = ctx.enter_context(tc.tile_pool(name="ring", bufs=4))
         psum = ctx.enter_context(tc.psum_pool(name="psum", bufs=8))
 
         offsets = held.tile([P, N // 16], U16, name="offsets")
         nc.sync.dma_start(offsets[:], offs)
 
-        def load(source, shape):
-            tile = raw.tile(shape, F32, name="raw")
+        def load(source, shape, name):
+            tile = raw.tile(shape, F32, name=name)
             nc.sync.dma_start(out=tile[:], in_=source)
             return tile
 
@@ -84,38 +83,36 @@ def tile_attend_gds_kl_kernel(tc, xT, wT, vT, wt, xm, offs, out):
             copier(engine)(out=grouped[:, lo:hi, :].rearrange("p (c i) j -> p c j i", i=PACK),
                            in_=planes[:, :, lo:hi].rearrange("p j (c i) -> p c j i", i=PACK))
 
-        def interleave_x(engine, grouped, planes, lo, hi):
-            copier(engine)(out=grouped[:].rearrange("p (t m) j -> p m j t", t=PACK)[:, lo:hi],
-                           in_=planes[:].rearrange("p j (m t) -> p m j t", t=PACK)[:, lo:hi])
+        def prepare_x(g, engines):
+            grouped, codes, scales = x_ops[g]
+            for half, engine in enumerate(engines):
+                tiles = slice(2 * half, 2 * half + 2)
+                cols = slice(2 * half * P, (2 * half + 2) * P)
+                copier(engine)(out=grouped[:].rearrange("p (t m) j -> p m j t", t=PACK)[:, :, :, tiles],
+                               in_=x_raw[g][:].rearrange("p j (m t) -> p m j t", t=PACK)[:, :, :, tiles])
+                nc.vector.quantize_mx(out=codes[:, cols].bitcast(E4M3), scales=scales[:, cols],
+                                      in_=grouped[:, cols, :].rearrange("p c j -> p (c j)"))
 
         w_op = operand("w")
         for j in range(PACK):
-            plane = load(w_rows[:, j, :], [P, T])
+            plane = load(w_rows[:, j, :], [P, T], "w%d" % j)
             nc.vector.tensor_copy(w_op[0][:, :, j], plane[:].indirect(offsets[:]))
         quantize(w_op, E4M3)
 
         x_ops = [operand("x%d" % g) for g in range(ROW_PASSES)]
-        x_raw = [load(x_rows[:, :, g * K_PASS:(g + 1) * K_PASS], [P, PACK, K_PASS]) for g in range(ROW_PASSES)]
-        v_planes = [load(v_rows[:, j, :], [P, T]) for j in range(PACK)]
-        m_raw = [load(m_rows[g], [P, PACK, D]) for g in range(ROW_PASSES)]
-
-        interleave_x("vector", x_ops[0][0], x_raw[0], 0, X_SPLIT)
-        interleave_x("scalar", x_ops[0][0], x_raw[0], X_SPLIT, P)
-        quantize(x_ops[0], E4M3)
-        for q in range(4):
-            interleave_x("scalar", x_ops[1][0], x_raw[1], q * 32, (q + 1) * 32)
-        quantize(x_ops[1], E4M3)
+        x_raw = [load(x_rows[:, :, g * K_PASS:(g + 1) * K_PASS], [P, PACK, K_PASS], "x%d" % g) for g in range(ROW_PASSES)]
+        v_planes = [load(v_rows[:, j, :], [P, T], "v%d" % j) for j in range(PACK)]
 
         def stats(name):
             return held.tile([P, ROW_PASSES * PACK], F32, name=name)
 
-        def exps(table, tile_no, neg_max, total):
+        def exps(name, table, tile_no, neg_max, total):
             g, t = divmod(tile_no, PACK)
             col = slice(tile_no, tile_no + 1)
             acc = psum.tile([P, N], F32, name="acc")
             matmul(acc, x_ops[g], t, table, E4M3, True, True)
             nc.vector.tensor_reduce(out=neg_max[:, col], in_=acc[:], axis=AXIS_X, op=ALU.max, negate=True)
-            result = ring.tile([P, N], F32, name="exp")
+            result = held.tile([P, N], F32, name="exp_%s%d" % (name, tile_no))
             nc.scalar.activation(result[:], acc[:], ACT.Exp, bias=neg_max[:, col], accum_out=total[:, col])
             return result
 
@@ -127,30 +124,37 @@ def tile_attend_gds_kl_kernel(tc, xT, wT, vT, wt, xm, offs, out):
                                            in1=weight_cols[:, cols], op0=ALU.mult, op1=ALU.mult)
 
         v_op = operand("v")
-        v_pair = held.tile([P, 2, N], F32, name="v_pair")
+        v_listed = held.tile([P, PACK, N], F32, name="v_listed")
 
-        def gather_v(j):
-            target = v_pair[:, j, :] if j < 2 else v_op[0][:, :, j]
-            nc.vector.tensor_copy(target, v_planes[j][:].indirect(offsets[:]))
+        def prepare_v():
+            for j in range(PACK):
+                nc.vector.tensor_copy(v_listed[:, j, :], v_planes[j][:].indirect(offsets[:]))
+            interleave("vector", v_op[0], v_listed, 0, 336)
+            interleave("scalar", v_op[0], v_listed, 336, N)
+            quantize(v_op, E4M3)
 
-        gather_v(0)
-        gather_v(1)
-        nc.scalar.copy(out=v_op[0][:, :, 0:2], in_=v_pair[:].rearrange("p j i -> p i j"))
-        gather_v(2)
-        gather_v(3)
-        quantize(v_op, E4M3)
-
-        s_max, s_sum, s_inv, s_fac = stats("s_max"), stats("s_sum"), stats("s_inv"), stats("s_fac")
+        s_max, s_sum, s_inv = stats("s_max"), stats("s_sum"), stats("s_inv")
         student = held.tile([P, ROW_PASSES * PACK, N], F32, name="student")
-        for pair in range(4):
-            tiles = [2 * pair, 2 * pair + 1]
-            e = [exps(w_op, n, s_max, s_sum) for n in tiles]
-            factors(slice(tiles[0], tiles[1] + 1), s_sum, s_inv, s_fac, 1.0)
-            for n, tile in zip(tiles, e):
-                nc.scalar.activation(student[:, n, :], tile[:], ACT.Copy, scale=s_fac[:, n:n + 1])
+        e = {}
+
+        def student_exps(tiles):
+            for n in tiles:
+                e[n] = exps("s", w_op, n, s_max, s_sum)
+
+        def teacher_exps(tiles):
+            for n in tiles:
+                z[n] = exps("t", v_op, n, t_max, t_sum)
+
+        def prescale(tiles):
+            cols = slice(tiles[0], tiles[-1] + 1)
+            nc.vector.reciprocal(s_inv[:, cols], s_sum[:, cols])
+            for n in tiles:
+                nc.gpsimd.tensor_scalar(out=student[:, n, :], in0=e[n][:], scalar1=s_inv[:, n:n + 1],
+                                        scalar2=weight_cols[:, n:n + 1], op0=ALU.mult, op1=ALU.mult)
 
         t_max, t_sum, t_inv, t_fac = stats("t_max"), stats("t_sum"), stats("t_inv"), stats("t_fac")
         g_ops = [operand("g%d" % g) for g in range(ROW_PASSES)]
+        m_raw = []
         m_grouped = held.tile([P, D // P, ROW_PASSES, P, PACK], BF16, name="m_grouped", align_bytes=64)
         m_codes = held.tile([P, D // P, ROW_PASSES, P], U32, name="m_codes", align_bytes=64)
         m_scales = held.tile([P, D // P, ROW_PASSES, P], U8, name="m_scales", align_bytes=64)
@@ -173,20 +177,25 @@ def tile_attend_gds_kl_kernel(tc, xT, wT, vT, wt, xm, offs, out):
                 nc.vector.scalar_tensor_tensor(out=g_planes[g][:, t, :], in0=z[n][:], scalar=t_fac[:, n:n + 1],
                                                in1=student[:, n, :], op0=ALU.mult, op1=ALU.add)
 
-        for pair in range(4):
-            for n in (2 * pair, 2 * pair + 1):
-                z[n] = exps(v_op, n, t_max, t_sum)
-            if pair > 0:
-                combine([2 * pair - 2, 2 * pair - 1])
-            if pair == 2:
-                for q in range(4):
-                    interleave("scalar", g_ops[0][0], g_planes[0], q * P, (q + 1) * P)
-        combine([6])
-        combine([7])
+        prepare_x(0, ["vector", "scalar"])
+        prepare_x(1, ["scalar", "scalar"])
+        student_exps([0, 1, 2, 3])
+        prescale([0, 1, 2, 3])
+        student_exps([4, 5, 6, 7])
+        prescale([4, 5, 6, 7])
+        prepare_v()
+        m_raw.extend(load(m_rows[g], [P, PACK, D], "v%d" % (g + 2)) for g in range(ROW_PASSES))
+        teacher_exps([0, 1, 2, 3])
+        teacher_exps([4, 5, 6, 7])
+        combine([0, 1, 2, 3])
+        for q in range(4):
+            interleave("scalar", g_ops[0][0], g_planes[0], q * P, (q + 1) * P)
+        quantize(g_ops[0], E5M2)
+        combine([4, 5])
+        combine([6, 7])
+        prepare_m(0)
         interleave("vector", g_ops[1][0], g_planes[1], 0, G_SPLIT)
         interleave("scalar", g_ops[1][0], g_planes[1], G_SPLIT, N)
-        quantize(g_ops[0], E5M2)
-        prepare_m(0)
         quantize(g_ops[1], E5M2)
 
         def product(c):

@@ -33,7 +33,6 @@ def tile_attend_gds_kl_kernel(tc, xT, wT, vT, wt, xm, offs, out):
         psum = ctx.enter_context(tc.psum_pool(name="psum", bufs=8))
 
         offsets = held.tile([P, N // 16], U16, name="offsets")
-        nc.sync.dma_start(offsets[:], offs)
 
         def load(source, shape, name):
             tile = raw.tile(shape, F32, name=name)
@@ -96,6 +95,8 @@ def tile_attend_gds_kl_kernel(tc, xT, wT, vT, wt, xm, offs, out):
         w_op = operand("w")
         for j in range(PACK):
             plane = load(w_rows[:, j, :], [P, T], "w%d" % j)
+            if j == 0:
+                nc.sync.dma_start(offsets[:], offs)
             nc.vector.tensor_copy(w_op[0][:, :, j], plane[:].indirect(offsets[:]))
         quantize(w_op, E4M3)
 
@@ -134,7 +135,7 @@ def tile_attend_gds_kl_kernel(tc, xT, wT, vT, wt, xm, offs, out):
             quantize(v_op, E4M3)
 
         s_max, s_sum, s_inv = stats("s_max"), stats("s_sum"), stats("s_inv")
-        student = held.tile([P, ROW_PASSES * PACK, N], F32, name="student")
+        student = {}
         e = {}
 
         def student_exps(tiles):
@@ -147,9 +148,11 @@ def tile_attend_gds_kl_kernel(tc, xT, wT, vT, wt, xm, offs, out):
 
         def prescale(tiles):
             cols = slice(tiles[0], tiles[-1] + 1)
+            g = tiles[0] // PACK
+            student[g] = held.tile([P, PACK, N], F32, name="v_grouped" if g else "student", align_bytes=64)
             nc.vector.reciprocal(s_inv[:, cols], s_sum[:, cols])
             for n in tiles:
-                nc.gpsimd.tensor_scalar(out=student[:, n, :], in0=e[n][:], scalar1=s_inv[:, n:n + 1],
+                nc.gpsimd.tensor_scalar(out=student[g][:, n % PACK, :], in0=e[n][:], scalar1=s_inv[:, n:n + 1],
                                         scalar2=weight_cols[:, n:n + 1], op0=ALU.mult, op1=ALU.mult)
 
         t_max, t_sum, t_inv, t_fac = stats("t_max"), stats("t_sum"), stats("t_inv"), stats("t_fac")
@@ -175,16 +178,16 @@ def tile_attend_gds_kl_kernel(tc, xT, wT, vT, wt, xm, offs, out):
             for n in tiles:
                 g, t = divmod(n, PACK)
                 nc.vector.scalar_tensor_tensor(out=g_planes[g][:, t, :], in0=z[n][:], scalar=t_fac[:, n:n + 1],
-                                               in1=student[:, n, :], op0=ALU.mult, op1=ALU.add)
+                                               in1=student[g][:, t, :], op0=ALU.mult, op1=ALU.add)
 
         prepare_x(0, ["vector", "scalar"])
         prepare_x(1, ["scalar", "scalar"])
         student_exps([0, 1, 2, 3])
         prescale([0, 1, 2, 3])
         student_exps([4, 5, 6, 7])
-        prescale([4, 5, 6, 7])
         prepare_v()
         m_raw.extend(load(m_rows[g], [P, PACK, D], "v%d" % (g + 2)) for g in range(ROW_PASSES))
+        prescale([4, 5, 6, 7])
         teacher_exps([0, 1, 2, 3])
         teacher_exps([4, 5, 6, 7])
         combine([0, 1, 2, 3])
@@ -198,6 +201,10 @@ def tile_attend_gds_kl_kernel(tc, xT, wT, vT, wt, xm, offs, out):
         interleave("scalar", g_ops[1][0], g_planes[1], G_SPLIT, N)
         quantize(g_ops[1], E5M2)
 
+        def pieces(c):
+            count = 2 if c == 0 else 1
+            return [slice(h * N // count, (h + 1) * N // count) for h in range(count)]
+
         def product(c):
             acc = psum.tile([P, N], F32, name="acc")
             for g in range(ROW_PASSES):
@@ -205,7 +212,8 @@ def tile_attend_gds_kl_kernel(tc, xT, wT, vT, wt, xm, offs, out):
                                     rhs=g_ops[g][1][:].bitcast(E5M2), rhs_scale=g_ops[g][2][:],
                                     start=g == 0, stop=g == ROW_PASSES - 1)
             dw = ring.tile([P, N], F32, name="dw")
-            nc.scalar.copy(out=dw[:], in_=acc[:])
+            for cols in pieces(c):
+                nc.scalar.copy(out=dw[:, cols], in_=acc[:, cols])
             return dw
 
         dw = product(0)
@@ -213,6 +221,8 @@ def tile_attend_gds_kl_kernel(tc, xT, wT, vT, wt, xm, offs, out):
             if c + 1 < D // P:
                 prepare_m(c + 1)
                 following = product(c + 1)
-            nc.vector.tensor_copy(windows[c][:].indirect(offsets[:]), dw[:])
+            for cols in pieces(c):
+                listed = offsets[:, cols.start // 16:cols.stop // 16]
+                nc.vector.tensor_copy(windows[c][:].indirect(listed), dw[:, cols])
             nc.sync.dma_start(out=out[c * P:(c + 1) * P, :], in_=windows[c][:])
             dw = following

@@ -21,7 +21,10 @@ P = 128
 PACK = 4
 K_PASS = P * PACK
 ROW_PASSES = R // K_PASS
-G_SPLIT = 352
+ROW_TILES = R // P
+ON_SCALAR = 3
+G_SPLIT = 208
+HALVES = [slice(0, N // 2), slice(N // 2, N)]
 
 
 def tile_attend_gds_kl_kernel(tc, xT, wT, vT, wt, xm, offs, out):
@@ -43,9 +46,6 @@ def tile_attend_gds_kl_kernel(tc, xT, wT, vT, wt, xm, offs, out):
         v_rows = vT.rearrange("(p j) t -> p j t", j=PACK)
         x_rows = xT[0].rearrange("(p j) r -> p j r", j=PACK)
         m_rows = xm[0].rearrange("(g p j) d -> g p j d", p=P, j=PACK)
-
-        weight = held.tile([P, ROW_PASSES, PACK], F32, name="weight")
-        nc.scalar.dma_start(out=weight[:], in_=wt[0].rearrange("(g p t) o -> p g (t o)", p=P, t=PACK))
 
         zero = held.tile([P, 1], F32, name="zero")
         warm = held.tile([P, 1], F32, name="warm")
@@ -103,6 +103,9 @@ def tile_attend_gds_kl_kernel(tc, xT, wT, vT, wt, xm, offs, out):
         x_ops = [operand("x%d" % g) for g in range(ROW_PASSES)]
         x_raw = [load(x_rows[:, :, g * K_PASS:(g + 1) * K_PASS], [P, PACK, K_PASS], "x%d" % g) for g in range(ROW_PASSES)]
         v_planes = [load(v_rows[:, j, :], [P, T], "v%d" % j) for j in range(PACK)]
+        weight = held.tile([P, ROW_PASSES, PACK], F32, name="weight")
+        nc.sync.dma_start(out=weight[:], in_=wt[0].rearrange("(g p t) o -> p g (t o)", p=P, t=PACK))
+
 
         def stats(name):
             return held.tile([P, ROW_PASSES * PACK], F32, name=name)
@@ -129,12 +132,28 @@ def tile_attend_gds_kl_kernel(tc, xT, wT, vT, wt, xm, offs, out):
 
         def prepare_v():
             for j in range(PACK):
-                nc.vector.tensor_copy(v_listed[:, j, :], v_planes[j][:].indirect(offsets[:]))
-            interleave("vector", v_op[0], v_listed, 0, 336)
-            interleave("scalar", v_op[0], v_listed, 336, N)
+                for cols in (HALVES if j == PACK - 1 else [slice(0, N)]):
+                    listed = offsets[:, cols.start // 16:cols.stop // 16]
+                    nc.vector.tensor_copy(v_listed[:, j, cols], v_planes[j][:].indirect(listed))
+            nc.vector.reciprocal(s_inv[:], s_sum[:])
+            nc.vector.tensor_tensor(out=s_fac[:, :ON_SCALAR], in0=s_inv[:, :ON_SCALAR], in1=weight_cols[:, :ON_SCALAR],
+                                    op=ALU.mult)
+            interleave("scalar", v_op[0], v_listed, 0, N // 2)
+            interleave("vector", v_op[0], v_listed, N // 2, N)
             quantize(v_op, E4M3)
+            first = held.tile([P, ON_SCALAR, N], F32, name="student")
+            rest = held.tile([P, ROW_TILES - ON_SCALAR, N], F32, name="v_grouped", align_bytes=64)
+            for n in range(ROW_TILES):
+                if n < ON_SCALAR:
+                    student[n] = first[:, n, :]
+                    nc.scalar.activation(student[n], e[n][:], ACT.Copy, scale=s_fac[:, n:n + 1])
+                else:
+                    student[n] = rest[:, n - ON_SCALAR, :]
+                    nc.gpsimd.tensor_scalar(out=student[n], in0=e[n][:], scalar1=s_inv[:, n:n + 1],
+                                            scalar2=weight_cols[:, n:n + 1], op0=ALU.mult, op1=ALU.mult)
 
         s_max, s_sum, s_inv = stats("s_max"), stats("s_sum"), stats("s_inv")
+        s_fac = held.tile([P, ON_SCALAR], F32, name="s_fac")
         student = {}
         e = {}
 
@@ -145,15 +164,6 @@ def tile_attend_gds_kl_kernel(tc, xT, wT, vT, wt, xm, offs, out):
         def teacher_exps(tiles):
             for n in tiles:
                 z[n] = exps("t", v_op, n, t_max, t_sum)
-
-        def prescale(tiles):
-            cols = slice(tiles[0], tiles[-1] + 1)
-            g = tiles[0] // PACK
-            student[g] = held.tile([P, PACK, N], F32, name="v_grouped" if g else "student", align_bytes=64)
-            nc.vector.reciprocal(s_inv[:, cols], s_sum[:, cols])
-            for n in tiles:
-                nc.gpsimd.tensor_scalar(out=student[g][:, n % PACK, :], in0=e[n][:], scalar1=s_inv[:, n:n + 1],
-                                        scalar2=weight_cols[:, n:n + 1], op0=ALU.mult, op1=ALU.mult)
 
         t_max, t_sum, t_inv, t_fac = stats("t_max"), stats("t_sum"), stats("t_inv"), stats("t_fac")
         g_ops = [operand("g%d" % g) for g in range(ROW_PASSES)]
@@ -177,17 +187,17 @@ def tile_attend_gds_kl_kernel(tc, xT, wT, vT, wt, xm, offs, out):
             factors(slice(tiles[0], tiles[-1] + 1), t_sum, t_inv, t_fac, -1.0)
             for n in tiles:
                 g, t = divmod(n, PACK)
-                nc.vector.scalar_tensor_tensor(out=g_planes[g][:, t, :], in0=z[n][:], scalar=t_fac[:, n:n + 1],
-                                               in1=student[g][:, t, :], op0=ALU.mult, op1=ALU.add)
+                for cols in (HALVES if n == ROW_TILES - 1 else [slice(0, N)]):
+                    nc.vector.scalar_tensor_tensor(out=g_planes[g][:, t, cols], in0=z[n][:, cols],
+                                                   scalar=t_fac[:, n:n + 1], in1=student[n][:, cols],
+                                                   op0=ALU.mult, op1=ALU.add)
 
         prepare_x(0, ["vector", "scalar"])
         prepare_x(1, ["scalar", "scalar"])
         student_exps([0, 1, 2, 3])
-        prescale([0, 1, 2, 3])
         student_exps([4, 5, 6, 7])
         prepare_v()
         m_raw.extend(load(m_rows[g], [P, PACK, D], "v%d" % (g + 2)) for g in range(ROW_PASSES))
-        prescale([4, 5, 6, 7])
         teacher_exps([0, 1, 2, 3])
         teacher_exps([4, 5, 6, 7])
         combine([0, 1, 2, 3])
@@ -197,8 +207,8 @@ def tile_attend_gds_kl_kernel(tc, xT, wT, vT, wt, xm, offs, out):
         combine([4, 5])
         combine([6, 7])
         prepare_m(0)
-        interleave("vector", g_ops[1][0], g_planes[1], 0, G_SPLIT)
-        interleave("scalar", g_ops[1][0], g_planes[1], G_SPLIT, N)
+        interleave("scalar", g_ops[1][0], g_planes[1], 0, G_SPLIT)
+        interleave("vector", g_ops[1][0], g_planes[1], G_SPLIT, N)
         quantize(g_ops[1], E5M2)
 
         def pieces(c):

@@ -22,8 +22,11 @@ PACK = 4
 K_PASS = P * PACK
 ROW_PASSES = R // K_PASS
 ROW_TILES = R // P
-ON_SCALAR = 3
-G_SPLIT = 208
+V_SCALAR = (128, 96)
+EARLY = 6
+PAD = 256
+PRODUCT_BANKS = 2
+WHOLE = [slice(0, N)]
 HALVES = [slice(0, N // 2), slice(N // 2, N)]
 
 
@@ -32,8 +35,7 @@ def tile_attend_gds_kl_kernel(tc, xT, wT, vT, wt, xm, offs, out):
     with ExitStack() as ctx:
         held = ctx.enter_context(tc.tile_pool(name="held", bufs=1))
         raw = ctx.enter_context(tc.tile_pool(name="raw", bufs=1))
-        ring = ctx.enter_context(tc.tile_pool(name="ring", bufs=4))
-        psum = ctx.enter_context(tc.psum_pool(name="psum", bufs=8))
+        psum = ctx.enter_context(tc.psum_pool(name="psum", bufs=8 - PRODUCT_BANKS))
 
         offsets = held.tile([P, N // 16], U16, name="offsets")
 
@@ -57,23 +59,16 @@ def tile_attend_gds_kl_kernel(tc, xT, wT, vT, wt, xm, offs, out):
             engine = nc.vector if c < 2 else nc.gpsimd
             engine.memset(window[:].bitcast(I32), 0)
 
-        def operand(name):
-            grouped = held.tile([P, K_PASS, PACK], BF16, name=name + "_grouped", align_bytes=64)
+        def operand(name, staging):
+            grouped = held.tile([P, K_PASS, PACK], BF16, name=staging, align_bytes=64)
             codes = held.tile([P, K_PASS], U32, name=name + "_codes", align_bytes=64)
             scales = held.tile([P, K_PASS], U8, name=name + "_scales", align_bytes=64)
             return grouped, codes, scales
 
-        def quantize(op, fmt):
+        def quantize(op, fmt, cols=slice(0, K_PASS)):
             grouped, codes, scales = op
-            nc.vector.quantize_mx(out=codes[:].bitcast(fmt), scales=scales[:],
-                                  in_=grouped[:].rearrange("p c j -> p (c j)"))
-
-        def matmul(acc, stationary, block, moving, moving_fmt, start, stop):
-            cols = slice(block * P, (block + 1) * P)
-            nc.tensor.matmul_mx(out=acc[:], lhsT=stationary[1][:, cols].bitcast(E4M3),
-                                lhsT_scale=stationary[2][:, cols],
-                                rhs=moving[1][:].bitcast(moving_fmt), rhs_scale=moving[2][:],
-                                start=start, stop=stop)
+            nc.vector.quantize_mx(out=codes[:, cols].bitcast(fmt), scales=scales[:, cols],
+                                  in_=grouped[:, cols, :].rearrange("p c j -> p (c j)"))
 
         def copier(engine):
             return nc.vector.tensor_copy if engine == "vector" else nc.scalar.copy
@@ -82,17 +77,15 @@ def tile_attend_gds_kl_kernel(tc, xT, wT, vT, wt, xm, offs, out):
             copier(engine)(out=grouped[:, lo:hi, :].rearrange("p (c i) j -> p c j i", i=PACK),
                            in_=planes[:, :, lo:hi].rearrange("p j (c i) -> p c j i", i=PACK))
 
-        def prepare_x(g, engines):
-            grouped, codes, scales = x_ops[g]
-            for half, engine in enumerate(engines):
-                tiles = slice(2 * half, 2 * half + 2)
-                cols = slice(2 * half * P, (2 * half + 2) * P)
-                copier(engine)(out=grouped[:].rearrange("p (t m) j -> p m j t", t=PACK)[:, :, :, tiles],
-                               in_=x_raw[g][:].rearrange("p j (m t) -> p m j t", t=PACK)[:, :, :, tiles])
-                nc.vector.quantize_mx(out=codes[:, cols].bitcast(E4M3), scales=scales[:, cols],
-                                      in_=grouped[:, cols, :].rearrange("p c j -> p (c j)"))
+        def cast_x(g, half, engine):
+            tiles = slice(2 * half, 2 * half + 2)
+            copier(engine)(out=x_ops[g][0][:].rearrange("p (t m) j -> p m j t", t=PACK)[:, :, :, tiles],
+                           in_=x_raw[g][:].rearrange("p j (m t) -> p m j t", t=PACK)[:, :, :, tiles])
 
-        w_op = operand("w")
+        def quantize_x(g, half):
+            quantize(x_ops[g], E4M3, HALVES[half])
+
+        w_op = operand("w", "staging")
         for j in range(PACK):
             plane = load(w_rows[:, j, :], [P, T], "w%d" % j)
             if j == 0:
@@ -100,139 +93,199 @@ def tile_attend_gds_kl_kernel(tc, xT, wT, vT, wt, xm, offs, out):
             nc.vector.tensor_copy(w_op[0][:, :, j], plane[:].indirect(offsets[:]))
         quantize(w_op, E4M3)
 
-        x_ops = [operand("x%d" % g) for g in range(ROW_PASSES)]
+        x_ops = []
         x_raw = [load(x_rows[:, :, g * K_PASS:(g + 1) * K_PASS], [P, PACK, K_PASS], "x%d" % g) for g in range(ROW_PASSES)]
-        v_planes = [load(v_rows[:, j, :], [P, T], "v%d" % j) for j in range(PACK)]
         weight = held.tile([P, ROW_PASSES, PACK], F32, name="weight")
         nc.sync.dma_start(out=weight[:], in_=wt[0].rearrange("(g p t) o -> p g (t o)", p=P, t=PACK))
-
+        weight_cols = weight[:].rearrange("p g t -> p (g t)")
+        v_planes = [load(v_rows[:, j, :], [P, T], "v%d" % j) for j in range(PACK)]
 
         def stats(name):
-            return held.tile([P, ROW_PASSES * PACK], F32, name=name)
+            return held.tile([P, ROW_TILES], F32, name=name)
 
-        def exps(name, table, tile_no, neg_max, total):
+        def scores(table, tile_no, pieces):
             g, t = divmod(tile_no, PACK)
-            col = slice(tile_no, tile_no + 1)
             acc = psum.tile([P, N], F32, name="acc")
-            matmul(acc, x_ops[g], t, table, E4M3, True, True)
-            nc.vector.tensor_reduce(out=neg_max[:, col], in_=acc[:], axis=AXIS_X, op=ALU.max, negate=True)
+            cols = slice(t * P, (t + 1) * P)
+            for piece in pieces:
+                nc.tensor.matmul_mx(out=acc[:, piece], lhsT=x_ops[g][1][:, cols].bitcast(E4M3),
+                                    lhsT_scale=x_ops[g][2][:, cols], rhs=table[1][:, piece].bitcast(E4M3),
+                                    rhs_scale=table[2][:, piece], start=True, stop=True)
+            return acc
+
+        def exps(name, acc, tile_no, neg_max, total):
+            nc.vector.tensor_reduce(out=neg_max, in_=acc[:], axis=AXIS_X, op=ALU.max, negate=True)
             result = held.tile([P, N], F32, name="exp_%s%d" % (name, tile_no))
-            nc.scalar.activation(result[:], acc[:], ACT.Exp, bias=neg_max[:, col], accum_out=total[:, col])
+            nc.scalar.activation(result[:], acc[:], ACT.Exp, bias=neg_max, accum_out=total)
             return result
 
-        weight_cols = weight[:].rearrange("p g t -> p (g t)")
-
-        def factors(cols, total, inverse, factor, sign):
-            nc.vector.reciprocal(inverse[:, cols], total[:, cols])
-            nc.vector.scalar_tensor_tensor(out=factor[:, cols], in0=inverse[:, cols], scalar=sign,
-                                           in1=weight_cols[:, cols], op0=ALU.mult, op1=ALU.mult)
-
-        v_op = operand("v")
         v_listed = held.tile([P, PACK, N], F32, name="v_listed")
-
-        def prepare_v():
-            for j in range(PACK):
-                for cols in (HALVES if j == PACK - 1 else [slice(0, N)]):
-                    listed = offsets[:, cols.start // 16:cols.stop // 16]
-                    nc.vector.tensor_copy(v_listed[:, j, cols], v_planes[j][:].indirect(listed))
-            nc.vector.reciprocal(s_inv[:], s_sum[:])
-            nc.vector.tensor_tensor(out=s_fac[:, :ON_SCALAR], in0=s_inv[:, :ON_SCALAR], in1=weight_cols[:, :ON_SCALAR],
-                                    op=ALU.mult)
-            interleave("scalar", v_op[0], v_listed, 0, N // 2)
-            interleave("vector", v_op[0], v_listed, N // 2, N)
-            quantize(v_op, E4M3)
-            first = held.tile([P, ON_SCALAR, N], F32, name="student")
-            rest = held.tile([P, ROW_TILES - ON_SCALAR, N], F32, name="v_grouped", align_bytes=64)
-            for n in range(ROW_TILES):
-                if n < ON_SCALAR:
-                    student[n] = first[:, n, :]
-                    nc.scalar.activation(student[n], e[n][:], ACT.Copy, scale=s_fac[:, n:n + 1])
-                else:
-                    student[n] = rest[:, n - ON_SCALAR, :]
-                    nc.gpsimd.tensor_scalar(out=student[n], in0=e[n][:], scalar1=s_inv[:, n:n + 1],
-                                            scalar2=weight_cols[:, n:n + 1], op0=ALU.mult, op1=ALU.mult)
-
         s_max, s_sum, s_inv = stats("s_max"), stats("s_sum"), stats("s_inv")
-        s_fac = held.tile([P, ON_SCALAR], F32, name="s_fac")
-        student = {}
-        e = {}
+        t_max, t_sum, t_inv, t_fac = stats("t_max"), stats("t_sum"), stats("t_inv"), stats("t_fac")
+        max_in_plane = {0: 0, 4: 1}
+        e, z, student = {}, {}, {}
 
         def student_exps(tiles):
             for n in tiles:
-                e[n] = exps("s", w_op, n, s_max, s_sum)
+                neg_max = v_listed[:, max_in_plane[n], 0:1] if n in max_in_plane else s_max[:, n:n + 1]
+                e[n] = exps("s", scores(w_op, n, WHOLE), n, neg_max, s_sum[:, n:n + 1])
 
-        def teacher_exps(tiles):
+        def scale_on_gpsimd(tiles):
+            cols = slice(tiles[0], tiles[-1] + 1)
+            nc.vector.reciprocal(s_inv[:, cols], s_sum[:, cols])
             for n in tiles:
-                z[n] = exps("t", v_op, n, t_max, t_sum)
+                student[n] = e[n][:]
+                nc.gpsimd.tensor_scalar(out=student[n], in0=e[n][:], scalar1=s_inv[:, n:n + 1],
+                                        scalar2=weight_cols[:, n:n + 1], op0=ALU.mult, op1=ALU.mult)
 
-        t_max, t_sum, t_inv, t_fac = stats("t_max"), stats("t_sum"), stats("t_inv"), stats("t_fac")
-        g_ops = [operand("g%d" % g) for g in range(ROW_PASSES)]
-        m_raw = []
-        m_grouped = held.tile([P, D // P, ROW_PASSES, P, PACK], BF16, name="m_grouped", align_bytes=64)
+        def factors(total, inverse, factor, cols, sign):
+            nc.vector.reciprocal(inverse, total)
+            nc.vector.scalar_tensor_tensor(out=factor[:, cols], in0=inverse, scalar=sign,
+                                           in1=weight_cols[:, cols], op0=ALU.mult, op1=ALU.mult)
+
+        def teacher_factors(cols):
+            factors(t_sum[:, cols], t_inv[:, cols], t_fac, cols, -1.0)
+
+        def gather_v(j):
+            for cols in (HALVES if j == PACK - 1 else [slice(0, N)]):
+                listed = offsets[:, cols.start // 16:cols.stop // 16]
+                nc.vector.tensor_copy(v_listed[:, j, cols], v_planes[j][:].indirect(listed))
+
+        HALF = N // 2
+        g_grouped = [held.tile([P, N, PACK], BF16, name="g%d_grouped" % g, align_bytes=64) for g in range(ROW_PASSES)]
+        g_codes = [held.tile([P, PAD + N], U32, name="g%d_codes" % g, align_bytes=64) for g in range(ROW_PASSES)]
+        g_scales = [held.tile([P, PAD + N], U8, name="g%d_scales" % g, align_bytes=64) for g in range(ROW_PASSES)]
+        for g in range(ROW_PASSES):
+            nc.gpsimd.memset(g_codes[g][:, :PAD], 0)
+            nc.gpsimd.memset(g_scales[g][:, :PAD].bitcast(U32), 0)
+        g_planes = {(g, h): held.tile([P, PACK, HALF], BF16, name="g_planes%d%d" % (g, h))
+                    for g in range(ROW_PASSES) for h in range(2)}
         m_codes = held.tile([P, D // P, ROW_PASSES, P], U32, name="m_codes", align_bytes=64)
         m_scales = held.tile([P, D // P, ROW_PASSES, P], U8, name="m_scales", align_bytes=64)
 
-        def prepare_m(c):
-            for g in range(ROW_PASSES):
-                nc.scalar.copy(out=m_grouped[:, c, g].rearrange("p (c i) j -> p c j i", i=PACK),
-                               in_=m_raw[g][:, :, c * P:(c + 1) * P].rearrange("p j (c i) -> p c j i", i=PACK))
+        def cast_m(engine, g, lo, hi):
+            if engine == "gpsimd":
+                nc.gpsimd.tensor_copy(out=m_grouped[:, lo:hi, g],
+                                      in_=m_raw[g][:, :, lo * P:hi * P].rearrange("p j (c m) -> p c m j", m=P))
+            else:
+                nc.scalar.copy(out=m_grouped[:, lo:hi, g].rearrange("p c (m i) j -> p c m j i", i=PACK),
+                               in_=m_raw[g][:, :, lo * P:hi * P].rearrange("p j (c m i) -> p c m j i", i=PACK, m=P // PACK))
+
+        def quantize_m(c):
             nc.vector.quantize_mx(out=m_codes[:, c].rearrange("p g m -> p (g m)").bitcast(E4M3),
                                   scales=m_scales[:, c].rearrange("p g m -> p (g m)"),
                                   in_=m_grouped[:, c].rearrange("p g m j -> p (g m j)"))
 
-        g_planes = [held.tile([P, PACK, N], BF16, name="g_planes%d" % g) for g in range(ROW_PASSES)]
-        z = {}
+        def combine(g, h):
+            cols = HALVES[h]
+            for t in range(PACK):
+                n = g * PACK + t
+                nc.vector.scalar_tensor_tensor(out=g_planes[g, h][:, t, :], in0=z[n][:, cols], scalar=t_fac[:, n:n + 1],
+                                               in1=student[n][:, cols], op0=ALU.mult, op1=ALU.add)
 
-        def combine(tiles):
-            factors(slice(tiles[0], tiles[-1] + 1), t_sum, t_inv, t_fac, -1.0)
-            for n in tiles:
-                g, t = divmod(n, PACK)
-                for cols in (HALVES if n == ROW_TILES - 1 else [slice(0, N)]):
-                    nc.vector.scalar_tensor_tensor(out=g_planes[g][:, t, cols], in0=z[n][:, cols],
-                                                   scalar=t_fac[:, n:n + 1], in1=student[n][:, cols],
-                                                   op0=ALU.mult, op1=ALU.add)
+        def weave_g(g, h):
+            nc.scalar.copy(out=g_grouped[g][:, HALVES[h], :].rearrange("p (c i) j -> p c j i", i=PACK),
+                           in_=g_planes[g, h][:].rearrange("p j (c i) -> p c j i", i=PACK))
 
-        prepare_x(0, ["vector", "scalar"])
-        prepare_x(1, ["scalar", "scalar"])
-        student_exps([0, 1, 2, 3])
-        student_exps([4, 5, 6, 7])
-        prepare_v()
-        m_raw.extend(load(m_rows[g], [P, PACK, D], "v%d" % (g + 2)) for g in range(ROW_PASSES))
-        teacher_exps([0, 1, 2, 3])
-        teacher_exps([4, 5, 6, 7])
-        combine([0, 1, 2, 3])
-        for q in range(4):
-            interleave("scalar", g_ops[0][0], g_planes[0], q * P, (q + 1) * P)
-        quantize(g_ops[0], E5M2)
-        combine([4, 5])
-        combine([6, 7])
-        prepare_m(0)
-        interleave("scalar", g_ops[1][0], g_planes[1], 0, G_SPLIT)
-        interleave("vector", g_ops[1][0], g_planes[1], G_SPLIT, N)
-        quantize(g_ops[1], E5M2)
+        def quantize_g(g, h):
+            cols = slice(PAD + h * HALF, PAD + (h + 1) * HALF)
+            nc.vector.quantize_mx(out=g_codes[g][:, cols].bitcast(E5M2), scales=g_scales[g][:, cols],
+                                  in_=g_grouped[g][:, HALVES[h], :].rearrange("p c j -> p (c j)"))
 
-        def pieces(c):
-            count = 2 if c == 0 else 1
-            return [slice(h * N // count, (h + 1) * N // count) for h in range(count)]
-
-        def product(c):
-            acc = psum.tile([P, N], F32, name="acc")
+        def product(c, cols):
+            acc = psum.tile([P, N], F32, name="product", bufs=PRODUCT_BANKS)
+            width = cols.stop - cols.start
             for g in range(ROW_PASSES):
-                nc.tensor.matmul_mx(out=acc[:], lhsT=m_codes[:, c, g].bitcast(E4M3), lhsT_scale=m_scales[:, c, g],
-                                    rhs=g_ops[g][1][:].bitcast(E5M2), rhs_scale=g_ops[g][2][:],
+                nc.tensor.matmul_mx(out=acc[:, :width], lhsT=m_codes[:, c, g].bitcast(E4M3), lhsT_scale=m_scales[:, c, g],
+                                    rhs=g_codes[g][:, cols].bitcast(E5M2), rhs_scale=g_scales[g][:, cols],
                                     start=g == 0, stop=g == ROW_PASSES - 1)
-            dw = ring.tile([P, N], F32, name="dw")
-            for cols in pieces(c):
-                nc.scalar.copy(out=dw[:, cols], in_=acc[:, cols])
+            return acc
+
+        def copy_out(source, width, name):
+            dw = held.tile([P, width], F32, name=name)
+            nc.scalar.copy(out=dw[:], in_=source)
             return dw
 
-        dw = product(0)
-        for c in range(D // P):
-            if c + 1 < D // P:
-                prepare_m(c + 1)
-                following = product(c + 1)
-            for cols in pieces(c):
-                listed = offsets[:, cols.start // 16:cols.stop // 16]
-                nc.vector.tensor_copy(windows[c][:].indirect(listed), dw[:, cols])
+        def scatter(c, dw, cols):
+            listed = offsets[:, cols.start // 16:cols.stop // 16]
+            nc.vector.tensor_copy(windows[c][:].indirect(listed), dw[:])
+
+        def store(c):
             nc.sync.dma_start(out=out[c * P:(c + 1) * P, :], in_=windows[c][:])
-            dw = following
+
+        x_ops.append(operand("x0", "staging"))
+        cast_x(0, 0, "vector")
+        cast_x(0, 1, "scalar")
+        quantize_x(0, 0)
+        quantize_x(0, 1)
+        x_ops.append(operand("x1", "staging"))
+        cast_x(1, 0, "scalar")
+        student_exps([0, 1, 2, 3])
+        quantize_x(1, 0)
+        scale_on_gpsimd([0, 1])
+        gather_v(0)
+        student_exps([4, 5])
+        cast_x(1, 1, "scalar")
+        scale_on_gpsimd([2, 3])
+        gather_v(1)
+        quantize_x(1, 1)
+        scale_on_gpsimd([4, 5])
+        student_exps(range(6, EARLY))
+        late_scores = {n: scores(w_op, n, WHOLE) for n in range(EARLY, ROW_TILES)}
+        gather_v(2)
+        gather_v(3)
+        shared = held.tile([P, D * ROW_PASSES * PACK], BF16, name="staging", align_bytes=64)
+        v_op = (shared[:, :N * PACK].rearrange("p (c j) -> p c j", j=PACK),
+                held.tile([P, K_PASS], U32, name="v_codes", align_bytes=64),
+                held.tile([P, K_PASS], U8, name="v_scales", align_bytes=64))
+        m_grouped = shared[:].rearrange("p (c g m j) -> p c g m j", g=ROW_PASSES, m=P, j=PACK)
+        for cols, share in zip(HALVES, V_SCALAR):
+            interleave("scalar", v_op[0], v_listed, cols.start, cols.start + share)
+            interleave("vector", v_op[0], v_listed, cols.start + share, cols.stop)
+        for cols in HALVES:
+            quantize(v_op, E4M3, cols)
+        late_max = shared[:, N * PACK // 2 - 16:N * PACK // 2].bitcast(F32)
+        for n in range(EARLY, ROW_TILES):
+            e[n] = exps("s", late_scores[n], n, late_max[:, n:n + 1], s_sum[:, n:n + 1])
+        m_raw = [load(m_rows[g], [P, PACK, D], "w%d" % (g + 2)) for g in range(ROW_PASSES)]
+        cast_m("gpsimd", 0, 0, 3)
+        cast_m("gpsimd", 1, 0, 2)
+        for n in range(ROW_TILES):
+            z[n] = exps("t", scores(v_op, n, WHOLE), n, t_max[:, n:n + 1], t_sum[:, n:n + 1])
+            if n == 1:
+                scale_on_gpsimd([6, 7])
+            if n == 5:
+                teacher_factors(slice(0, 4))
+        quantize_m(0)
+        teacher_factors(slice(4, 7))
+        combine(0, 0)
+        weave_g(0, 0)
+        teacher_factors(slice(7, 8))
+        combine(1, 0)
+        weave_g(1, 0)
+        quantize_g(0, 0)
+        quantize_g(1, 0)
+        quantize_m(1)
+        early = [product(c, slice(0, N)) for c in range(2)]
+        combine(0, 1)
+        weave_g(0, 1)
+        first = copy_out(early[0][:, HALF:], HALF, "dw_first0")
+        combine(1, 1)
+        weave_g(1, 1)
+        quantize_g(0, 1)
+        quantize_g(1, 1)
+        scatter(0, first, HALVES[0])
+        first = copy_out(early[1][:, HALF:], HALF, "g_planes11")
+        scatter(1, first, HALVES[0])
+        for c in range(2):
+            acc = product(c, slice(PAD, PAD + N))
+            scatter(c, copy_out(acc[:, HALF:], HALF, "dw_second%d" % c), HALVES[1])
+            store(c)
+        cast_m("scalar", 1, 2, 3)
+        cast_m("scalar", 0, 3, 4)
+        cast_m("scalar", 1, 3, 4)
+        for c in range(2, 4):
+            quantize_m(c)
+            acc = product(c, slice(PAD, PAD + N))
+            scatter(c, copy_out(acc[:], N, "dw%d" % c), slice(0, N))
+            store(c)

@@ -26,7 +26,7 @@ V_SCALAR = (128, 96)
 EARLY = 6
 PAD = 256
 PRODUCT_BANKS = 2
-WHOLE = [slice(0, N)]
+SCORE_BANKS = 8 - 2
 HALVES = [slice(0, N // 2), slice(N // 2, N)]
 
 
@@ -35,7 +35,7 @@ def tile_attend_gds_kl_kernel(tc, xT, wT, vT, wt, xm, offs, out):
     with ExitStack() as ctx:
         held = ctx.enter_context(tc.tile_pool(name="held", bufs=1))
         raw = ctx.enter_context(tc.tile_pool(name="raw", bufs=1))
-        psum = ctx.enter_context(tc.psum_pool(name="psum", bufs=8 - PRODUCT_BANKS))
+        psum = ctx.enter_context(tc.psum_pool(name="psum", bufs=1))
 
         offsets = held.tile([P, N // 16], U16, name="offsets")
 
@@ -101,34 +101,31 @@ def tile_attend_gds_kl_kernel(tc, xT, wT, vT, wt, xm, offs, out):
         v_planes = [load(v_rows[:, j, :], [P, T], "v%d" % j) for j in range(PACK)]
 
         def stats(name):
-            return held.tile([P, ROW_TILES], F32, name=name)
+            return held.tile([P, ROW_TILES], F32, name=name, align_bytes=64)
 
-        def scores(table, tile_no, pieces):
+        def scores(table, tile_no, bank):
             g, t = divmod(tile_no, PACK)
-            acc = psum.tile([P, N], F32, name="acc")
+            acc = psum.tile([P, N], F32, name="bank%d" % bank)
             cols = slice(t * P, (t + 1) * P)
-            for piece in pieces:
-                nc.tensor.matmul_mx(out=acc[:, piece], lhsT=x_ops[g][1][:, cols].bitcast(E4M3),
-                                    lhsT_scale=x_ops[g][2][:, cols], rhs=table[1][:, piece].bitcast(E4M3),
-                                    rhs_scale=table[2][:, piece], start=True, stop=True)
+            nc.tensor.matmul_mx(out=acc[:], lhsT=x_ops[g][1][:, cols].bitcast(E4M3), lhsT_scale=x_ops[g][2][:, cols],
+                                rhs=table[1][:].bitcast(E4M3), rhs_scale=table[2][:], start=True, stop=True)
             return acc
 
         def exps(name, acc, tile_no, neg_max, total):
             nc.vector.tensor_reduce(out=neg_max, in_=acc[:], axis=AXIS_X, op=ALU.max, negate=True)
-            result = held.tile([P, N], F32, name="exp_%s%d" % (name, tile_no))
+            result = held.tile([P, N], F32, name="exp_%s%d" % (name, tile_no), align_bytes=64)
             nc.scalar.activation(result[:], acc[:], ACT.Exp, bias=neg_max, accum_out=total)
             return result
 
         v_listed = held.tile([P, PACK, N], F32, name="v_listed")
         s_max, s_sum, s_inv = stats("s_max"), stats("s_sum"), stats("s_inv")
         t_max, t_sum, t_inv, t_fac = stats("t_max"), stats("t_sum"), stats("t_inv"), stats("t_fac")
-        max_in_plane = {0: 0, 4: 1}
-        e, z, student = {}, {}, {}
+        e, z, student, m_grouped = {}, {}, {}, {}
 
         def student_exps(tiles):
             for n in tiles:
-                neg_max = v_listed[:, max_in_plane[n], 0:1] if n in max_in_plane else s_max[:, n:n + 1]
-                e[n] = exps("s", scores(w_op, n, WHOLE), n, neg_max, s_sum[:, n:n + 1])
+                neg_max = s_max[:, n:n + 1]
+                e[n] = exps("s", scores(w_op, n, n if n < 4 else n - 2), n, neg_max, s_sum[:, n:n + 1])
 
         def scale_on_gpsimd(tiles):
             cols = slice(tiles[0], tiles[-1] + 1)
@@ -158,23 +155,26 @@ def tile_attend_gds_kl_kernel(tc, xT, wT, vT, wt, xm, offs, out):
         for g in range(ROW_PASSES):
             nc.gpsimd.memset(g_codes[g][:, :PAD], 0)
             nc.gpsimd.memset(g_scales[g][:, :PAD].bitcast(U32), 0)
-        g_planes = {(g, h): held.tile([P, PACK, HALF], BF16, name="g_planes%d%d" % (g, h))
+        g_planes = {(g, h): held.tile([P, PACK, HALF], BF16, name="g_planes%d%d" % (g, h), align_bytes=64)
                     for g in range(ROW_PASSES) for h in range(2)}
         m_codes = held.tile([P, D // P, ROW_PASSES, P], U32, name="m_codes", align_bytes=64)
         m_scales = held.tile([P, D // P, ROW_PASSES, P], U8, name="m_scales", align_bytes=64)
 
-        def cast_m(engine, g, lo, hi):
+        def cast_m(engine, c, g):
+            source = m_raw[g][:, :, c * P:(c + 1) * P]
             if engine == "gpsimd":
-                nc.gpsimd.tensor_copy(out=m_grouped[:, lo:hi, g],
-                                      in_=m_raw[g][:, :, lo * P:hi * P].rearrange("p j (c m) -> p c m j", m=P))
+                nc.gpsimd.tensor_copy(out=m_grouped[c][:, g], in_=source.rearrange("p j m -> p m j"))
             else:
-                nc.scalar.copy(out=m_grouped[:, lo:hi, g].rearrange("p c (m i) j -> p c m j i", i=PACK),
-                               in_=m_raw[g][:, :, lo * P:hi * P].rearrange("p j (c m i) -> p c m j i", i=PACK, m=P // PACK))
+                nc.scalar.copy(out=m_grouped[c][:, g].rearrange("p (m i) j -> p m j i", i=PACK),
+                               in_=source.rearrange("p j (m i) -> p m j i", i=PACK))
+
+        def stage_m(c, name):
+            m_grouped[c] = held.tile([P, ROW_PASSES, P, PACK], BF16, name=name, align_bytes=64)[:]
 
         def quantize_m(c):
             nc.vector.quantize_mx(out=m_codes[:, c].rearrange("p g m -> p (g m)").bitcast(E4M3),
                                   scales=m_scales[:, c].rearrange("p g m -> p (g m)"),
-                                  in_=m_grouped[:, c].rearrange("p g m j -> p (g m j)"))
+                                  in_=m_grouped[c].rearrange("p g m j -> p (g m j)"))
 
         def combine(g, h):
             cols = HALVES[h]
@@ -183,9 +183,11 @@ def tile_attend_gds_kl_kernel(tc, xT, wT, vT, wt, xm, offs, out):
                 nc.vector.scalar_tensor_tensor(out=g_planes[g, h][:, t, :], in0=z[n][:, cols], scalar=t_fac[:, n:n + 1],
                                                in1=student[n][:, cols], op0=ALU.mult, op1=ALU.add)
 
-        def weave_g(g, h):
-            nc.scalar.copy(out=g_grouped[g][:, HALVES[h], :].rearrange("p (c i) j -> p c j i", i=PACK),
-                           in_=g_planes[g, h][:].rearrange("p j (c i) -> p c j i", i=PACK))
+        def weave_g(g, h, share=HALF):
+            target = g_grouped[g][:, HALVES[h], :]
+            interleave("scalar", target, g_planes[g, h], 0, share)
+            if share < HALF:
+                interleave("vector", target, g_planes[g, h], share, HALF)
 
         def quantize_g(g, h):
             cols = slice(PAD + h * HALF, PAD + (h + 1) * HALF)
@@ -202,23 +204,23 @@ def tile_attend_gds_kl_kernel(tc, xT, wT, vT, wt, xm, offs, out):
             return acc
 
         def copy_out(source, width, name):
-            dw = held.tile([P, width], F32, name=name)
+            dw = held.tile([P, width], F32, name=name, align_bytes=64)
             nc.scalar.copy(out=dw[:], in_=source)
-            return dw
+            return dw[:]
 
         def scatter(c, dw, cols):
             listed = offsets[:, cols.start // 16:cols.stop // 16]
-            nc.vector.tensor_copy(windows[c][:].indirect(listed), dw[:])
+            nc.vector.tensor_copy(windows[c][:].indirect(listed), dw)
 
         def store(c):
             nc.sync.dma_start(out=out[c * P:(c + 1) * P, :], in_=windows[c][:])
 
-        x_ops.append(operand("x0", "staging"))
+        x_ops.append(operand("x0", "x0_grouped"))
         cast_x(0, 0, "vector")
         cast_x(0, 1, "scalar")
         quantize_x(0, 0)
         quantize_x(0, 1)
-        x_ops.append(operand("x1", "staging"))
+        x_ops.append(operand("x1", "x0_grouped"))
         cast_x(1, 0, "scalar")
         student_exps([0, 1, 2, 3])
         quantize_x(1, 0)
@@ -231,40 +233,43 @@ def tile_attend_gds_kl_kernel(tc, xT, wT, vT, wt, xm, offs, out):
         quantize_x(1, 1)
         scale_on_gpsimd([4, 5])
         student_exps(range(6, EARLY))
-        late_scores = {n: scores(w_op, n, WHOLE) for n in range(EARLY, ROW_TILES)}
+        late_scores = {n: scores(w_op, n, n - 2) for n in range(EARLY, ROW_TILES)}
         gather_v(2)
         gather_v(3)
-        shared = held.tile([P, D * ROW_PASSES * PACK], BF16, name="staging", align_bytes=64)
-        v_op = (shared[:, :N * PACK].rearrange("p (c j) -> p c j", j=PACK),
+        shared = held.tile([P, N * PACK], BF16, name="staging", align_bytes=64)
+        v_op = (shared[:].rearrange("p (c j) -> p c j", j=PACK),
                 held.tile([P, K_PASS], U32, name="v_codes", align_bytes=64),
                 held.tile([P, K_PASS], U8, name="v_scales", align_bytes=64))
-        m_grouped = shared[:].rearrange("p (c g m j) -> p c g m j", g=ROW_PASSES, m=P, j=PACK)
         for cols, share in zip(HALVES, V_SCALAR):
             interleave("scalar", v_op[0], v_listed, cols.start, cols.start + share)
             interleave("vector", v_op[0], v_listed, cols.start + share, cols.stop)
         for cols in HALVES:
             quantize(v_op, E4M3, cols)
+        m_raw = [load(m_rows[g], [P, PACK, D], "w%d" % (g + 2)) for g in range(ROW_PASSES)]
+        stage_m(0, "m0_grouped")
+        cast_m("scalar", 0, 0)
         late_max = shared[:, N * PACK // 2 - 16:N * PACK // 2].bitcast(F32)
         for n in range(EARLY, ROW_TILES):
             e[n] = exps("s", late_scores[n], n, late_max[:, n:n + 1], s_sum[:, n:n + 1])
-        m_raw = [load(m_rows[g], [P, PACK, D], "w%d" % (g + 2)) for g in range(ROW_PASSES)]
-        cast_m("gpsimd", 0, 0, 3)
-        cast_m("gpsimd", 1, 0, 2)
         for n in range(ROW_TILES):
-            z[n] = exps("t", scores(v_op, n, WHOLE), n, t_max[:, n:n + 1], t_sum[:, n:n + 1])
+            z[n] = exps("t", scores(v_op, n, n % SCORE_BANKS), n, t_max[:, n:n + 1], t_sum[:, n:n + 1])
             if n == 1:
                 scale_on_gpsimd([6, 7])
             if n == 5:
                 teacher_factors(slice(0, 4))
-        quantize_m(0)
+        cast_m("scalar", 0, 1)
         teacher_factors(slice(4, 7))
         combine(0, 0)
         weave_g(0, 0)
         teacher_factors(slice(7, 8))
         combine(1, 0)
-        weave_g(1, 0)
+        weave_g(1, 0, 256)
+        quantize_m(0)
         quantize_g(0, 0)
         quantize_g(1, 0)
+        stage_m(1, "t_max")
+        for g in range(ROW_PASSES):
+            cast_m("scalar", 1, g)
         quantize_m(1)
         early = [product(c, slice(0, N)) for c in range(2)]
         combine(0, 1)
@@ -275,16 +280,18 @@ def tile_attend_gds_kl_kernel(tc, xT, wT, vT, wt, xm, offs, out):
         quantize_g(0, 1)
         quantize_g(1, 1)
         scatter(0, first, HALVES[0])
-        first = copy_out(early[1][:, HALF:], HALF, "g_planes11")
-        scatter(1, first, HALVES[0])
+        after_weave = held.tile([P, HALF + 2 * N], F32, name="g_planes11", align_bytes=64)
+        nc.scalar.copy(out=after_weave[:, :HALF], in_=early[1][:, HALF:])
+        scatter(1, after_weave[:, :HALF], HALVES[0])
         for c in range(2):
             acc = product(c, slice(PAD, PAD + N))
             scatter(c, copy_out(acc[:, HALF:], HALF, "dw_second%d" % c), HALVES[1])
             store(c)
-        cast_m("scalar", 1, 2, 3)
-        cast_m("scalar", 0, 3, 4)
-        cast_m("scalar", 1, 3, 4)
         for c in range(2, 4):
+            words = after_weave[:, HALF + (c - 2) * N:HALF + (c - 1) * N]
+            m_grouped[c] = words.bitcast(BF16).rearrange("p (g m j) -> p g m j", g=ROW_PASSES, j=PACK)
+            for g in range(ROW_PASSES):
+                cast_m("scalar", c, g)
             quantize_m(c)
             acc = product(c, slice(PAD, PAD + N))
             scatter(c, copy_out(acc[:], N, "dw%d" % c), slice(0, N))

@@ -1,6 +1,7 @@
 from contextlib import ExitStack
 
 import concourse.mybir as mybir
+from concourse.masks import make_identity
 
 N, T, D, R = 512, 2048, 512, 1024
 FLOPS = 3 * 2 * R * N * D
@@ -54,6 +55,11 @@ def tile_attend_gds_kl_kernel(tc, xT, wT, vT, wt, xm, offs, out):
         nc.gpsimd.memset(zero[:], 0.0)
         nc.scalar.activation(warm[:], zero[:], ACT.Exp)
 
+        weight_rows = held.tile([P, K_PASS], F32, name="weight_rows")
+        nc.vector.memset(weight_rows[:], 0.0)
+        identity = held.tile([P, P], F32, name="identity")
+        make_identity(nc, identity[:])
+
         windows = [held.tile([P, T], F32, name="window%d" % c) for c in range(D // P)]
         for c, window in enumerate(windows):
             engine = nc.vector if c < 2 else nc.gpsimd
@@ -90,14 +96,20 @@ def tile_attend_gds_kl_kernel(tc, xT, wT, vT, wt, xm, offs, out):
             plane = load(w_rows[:, j, :], [P, T], "w%d" % j)
             if j == 0:
                 nc.sync.dma_start(offsets[:], offs)
+                nc.sync.dma_start(out=weight_rows[:ROW_PASSES, :],
+                                  in_=wt[0].rearrange("(g r) o -> g (r o)", g=ROW_PASSES))
             nc.vector.tensor_copy(w_op[0][:, :, j], plane[:].indirect(offsets[:]))
         quantize(w_op, E4M3)
 
+        turned = psum.tile([P, PACK, P], F32, name="bank5")
+        for t in range(PACK):
+            nc.tensor.transpose(turned[:, t, :], weight_rows[:, t::PACK], identity[:])
+        weight = held.tile([P, ROW_PASSES, PACK], F32, name="weight")
+        nc.scalar.copy(out=weight[:], in_=turned[:, :, :ROW_PASSES].rearrange("p t g -> p g t"))
+        weight_cols = weight[:].rearrange("p g t -> p (g t)")
+
         x_ops = []
         x_raw = [load(x_rows[:, :, g * K_PASS:(g + 1) * K_PASS], [P, PACK, K_PASS], "x%d" % g) for g in range(ROW_PASSES)]
-        weight = held.tile([P, ROW_PASSES, PACK], F32, name="weight")
-        nc.sync.dma_start(out=weight[:], in_=wt[0].rearrange("(g p t) o -> p g (t o)", p=P, t=PACK))
-        weight_cols = weight[:].rearrange("p g t -> p (g t)")
         v_planes = [load(v_rows[:, j, :], [P, T], "v%d" % j) for j in range(PACK)]
 
         def stats(name):

@@ -23,7 +23,6 @@ PACK = 4
 K_PASS = P * PACK
 ROW_PASSES = R // K_PASS
 ROW_TILES = R // P
-V_SCALAR = (128, 96)
 EARLY = 6
 PAD = 256
 PRODUCT_BANKS = 2
@@ -129,7 +128,6 @@ def tile_attend_gds_kl_kernel(tc, xT, wT, vT, wt, xm, offs, out):
             nc.scalar.activation(result[:], acc[:], ACT.Exp, bias=neg_max, accum_out=total)
             return result
 
-        v_listed = held.tile([P, PACK, N], F32, name="v_listed")
         s_max, s_sum, s_inv = stats("s_max"), stats("s_sum"), stats("s_inv")
         t_max, t_sum, t_inv, t_fac = stats("t_max"), stats("t_sum"), stats("t_inv"), stats("t_fac")
         e, z, student, m_grouped = {}, {}, {}, {}
@@ -158,7 +156,7 @@ def tile_attend_gds_kl_kernel(tc, xT, wT, vT, wt, xm, offs, out):
         def gather_v(j):
             for cols in (HALVES if j == PACK - 1 else [slice(0, N)]):
                 listed = offsets[:, cols.start // 16:cols.stop // 16]
-                nc.vector.tensor_copy(v_listed[:, j, cols], v_planes[j][:].indirect(listed))
+                nc.vector.tensor_copy(v_op[0][:, cols, j], v_planes[j][:].indirect(listed))
 
         HALF = N // 2
         g_grouped = [held.tile([P, N, PACK], BF16, name="g%d_grouped" % g, align_bytes=64) for g in range(ROW_PASSES)]
@@ -169,24 +167,20 @@ def tile_attend_gds_kl_kernel(tc, xT, wT, vT, wt, xm, offs, out):
             nc.gpsimd.memset(g_scales[g][:, :PAD].bitcast(U32), 0)
         g_planes = {(g, h): held.tile([P, PACK, HALF], BF16, name="g_planes%d%d" % (g, h), align_bytes=64)
                     for g in range(ROW_PASSES) for h in range(2)}
-        m_codes = held.tile([P, D // P, ROW_PASSES, P], U32, name="m_codes", align_bytes=64)
-        m_scales = held.tile([P, D // P, ROW_PASSES, P], U8, name="m_scales", align_bytes=64)
+        m_codes = held.tile([P, ROW_PASSES, D], U32, name="m_codes", align_bytes=64)
+        m_scales = held.tile([P, ROW_PASSES, D], U8, name="m_scales", align_bytes=64)
 
-        def cast_m(engine, c, g):
-            source = m_raw[g][:, :, c * P:(c + 1) * P]
+        def cast_m(engine, g, h, lo=0, hi=HALF):
+            source = m_raw[g][:, :, h * HALF + lo:h * HALF + hi]
+            target = m_grouped[g, h].rearrange("p (m j) -> p m j", j=PACK)
             if engine == "gpsimd":
-                nc.gpsimd.tensor_copy(out=m_grouped[c][:, g], in_=source.rearrange("p j m -> p m j"))
+                nc.gpsimd.tensor_copy(out=target[:, lo:hi, :], in_=source.rearrange("p j m -> p m j"))
             else:
-                nc.scalar.copy(out=m_grouped[c][:, g].rearrange("p (m i) j -> p m j i", i=PACK),
-                               in_=source.rearrange("p j (m i) -> p m j i", i=PACK))
+                interleave(engine, target, m_raw[g][:, :, HALVES[h]], lo, hi)
 
-        def stage_m(c, name):
-            m_grouped[c] = held.tile([P, ROW_PASSES, P, PACK], BF16, name=name, align_bytes=64)[:]
-
-        def quantize_m(c):
-            nc.vector.quantize_mx(out=m_codes[:, c].rearrange("p g m -> p (g m)").bitcast(E4M3),
-                                  scales=m_scales[:, c].rearrange("p g m -> p (g m)"),
-                                  in_=m_grouped[c].rearrange("p g m j -> p (g m j)"))
+        def quantize_m(g, h):
+            nc.vector.quantize_mx(out=m_codes[:, g, HALVES[h]].bitcast(E4M3), scales=m_scales[:, g, HALVES[h]],
+                                  in_=m_grouped[g, h])
 
         def combine(g, h):
             cols = HALVES[h]
@@ -206,11 +200,12 @@ def tile_attend_gds_kl_kernel(tc, xT, wT, vT, wt, xm, offs, out):
             nc.vector.quantize_mx(out=g_codes[g][:, cols].bitcast(E5M2), scales=g_scales[g][:, cols],
                                   in_=g_grouped[g][:, HALVES[h], :].rearrange("p c j -> p (c j)"))
 
-        def product(c, cols):
-            acc = psum.tile([P, N], F32, name="product", bufs=PRODUCT_BANKS)
+        def product(c, cols, bank):
+            acc = psum.tile([P, N], F32, name="product%d" % bank)
             width = cols.stop - cols.start
             for g in range(ROW_PASSES):
-                nc.tensor.matmul_mx(out=acc[:, :width], lhsT=m_codes[:, c, g].bitcast(E4M3), lhsT_scale=m_scales[:, c, g],
+                nc.tensor.matmul_mx(out=acc[:, :width], lhsT=m_codes[:, g, c * P:(c + 1) * P].bitcast(E4M3),
+                                    lhsT_scale=m_scales[:, g, c * P:(c + 1) * P],
                                     rhs=g_codes[g][:, cols].bitcast(E5M2), rhs_scale=g_scales[g][:, cols],
                                     start=g == 0, stop=g == ROW_PASSES - 1)
             return acc
@@ -237,6 +232,10 @@ def tile_attend_gds_kl_kernel(tc, xT, wT, vT, wt, xm, offs, out):
         student_exps([0, 1, 2, 3])
         quantize_x(1, 0)
         scale_on_gpsimd([0, 1])
+        shared = held.tile([P, N * PACK], BF16, name="staging", align_bytes=64)
+        v_op = (shared[:].rearrange("p (c j) -> p c j", j=PACK),
+                held.tile([P, K_PASS], U32, name="v_codes", align_bytes=64),
+                held.tile([P, K_PASS], U8, name="v_scales", align_bytes=64))
         gather_v(0)
         student_exps([4, 5])
         cast_x(1, 1, "scalar")
@@ -248,63 +247,61 @@ def tile_attend_gds_kl_kernel(tc, xT, wT, vT, wt, xm, offs, out):
         late_scores = {n: scores(w_op, n, n - 2) for n in range(EARLY, ROW_TILES)}
         gather_v(2)
         gather_v(3)
-        shared = held.tile([P, N * PACK], BF16, name="staging", align_bytes=64)
-        v_op = (shared[:].rearrange("p (c j) -> p c j", j=PACK),
-                held.tile([P, K_PASS], U32, name="v_codes", align_bytes=64),
-                held.tile([P, K_PASS], U8, name="v_scales", align_bytes=64))
-        for cols, share in zip(HALVES, V_SCALAR):
-            interleave("scalar", v_op[0], v_listed, cols.start, cols.start + share)
-            interleave("vector", v_op[0], v_listed, cols.start + share, cols.stop)
         for cols in HALVES:
             quantize(v_op, E4M3, cols)
         m_raw = [load(m_rows[g], [P, PACK, D], "w%d" % (g + 2)) for g in range(ROW_PASSES)]
-        stage_m(0, "m0_grouped")
-        cast_m("scalar", 0, 0)
         late_max = shared[:, N * PACK // 2 - 16:N * PACK // 2].bitcast(F32)
         for n in range(EARLY, ROW_TILES):
             e[n] = exps("s", late_scores[n], n, late_max[:, n:n + 1], s_sum[:, n:n + 1])
+        m_grouped[0, 0] = shared[:, N * PACK // 2:]
+        m_grouped[1, 0] = held.tile([P, HALF * PACK], BF16, name="m_grouped", align_bytes=64)[:]
+        cast_m("gpsimd", 0, 0)
+        cast_m("gpsimd", 1, 0, 0, 128)
         for n in range(ROW_TILES):
             z[n] = exps("t", scores(v_op, n, n % SCORE_BANKS), n, t_max[:, n:n + 1], t_sum[:, n:n + 1])
-            if n == 1:
+            if n == 2:
                 scale_on_gpsimd([6, 7])
             if n == 5:
                 teacher_factors(slice(0, 4))
-        cast_m("scalar", 0, 1)
+        cast_m("scalar", 1, 0, 128, HALF)
+        quantize_m(0, 0)
         teacher_factors(slice(4, 7))
         combine(0, 0)
         weave_g(0, 0)
         teacher_factors(slice(7, 8))
         combine(1, 0)
         weave_g(1, 0, 256)
-        quantize_m(0)
-        quantize_g(0, 0)
         quantize_g(1, 0)
-        stage_m(1, "t_max")
-        for g in range(ROW_PASSES):
-            cast_m("scalar", 1, g)
-        quantize_m(1)
-        early = [product(c, slice(0, N)) for c in range(2)]
         combine(0, 1)
+        quantize_g(0, 0)
+        quantize_m(1, 0)
+        early = product(0, slice(0, N), 0)
         weave_g(0, 1)
-        first = copy_out(early[0][:, HALF:], HALF, "dw_first0")
+        first = copy_out(early[:, HALF:], HALF, "dw_first0")
         combine(1, 1)
         weave_g(1, 1)
         quantize_g(0, 1)
         quantize_g(1, 1)
         scatter(0, first, HALVES[0])
-        after_weave = held.tile([P, HALF + 2 * N], F32, name="g_planes11", align_bytes=64)
-        nc.scalar.copy(out=after_weave[:, :HALF], in_=early[1][:, HALF:])
+        early = product(1, slice(0, N), 0)
+        after_weave = held.tile([P, HALF + N], F32, name="g_planes11", align_bytes=64)
+        nc.scalar.copy(out=after_weave[:, :HALF], in_=early[:, HALF:])
         scatter(1, after_weave[:, :HALF], HALVES[0])
-        for c in range(2):
-            acc = product(c, slice(PAD, PAD + N))
-            scatter(c, copy_out(acc[:, HALF:], HALF, "dw_second%d" % c), HALVES[1])
+
+        def finish(c, first_slot):
+            acc = product(c, slice(PAD, PAD + N), (c + 1) % 2)
+            scatter(c, copy_out(acc[:, first_slot:], N - first_slot, "dw%d" % c), slice(first_slot, N))
             store(c)
-        for c in range(2, 4):
-            words = after_weave[:, HALF + (c - 2) * N:HALF + (c - 1) * N]
-            m_grouped[c] = words.bitcast(BF16).rearrange("p (g m j) -> p g m j", g=ROW_PASSES, j=PACK)
-            for g in range(ROW_PASSES):
-                cast_m("scalar", c, g)
-            quantize_m(c)
-            acc = product(c, slice(PAD, PAD + N))
-            scatter(c, copy_out(acc[:], N, "dw%d" % c), slice(0, N))
-            store(c)
+
+        finish(0, HALF)
+        for g in range(ROW_PASSES):
+            if g == 0:
+                m_grouped[g, 1] = held.tile([P, HALF * PACK], BF16, name="g_planes01", align_bytes=64)[:]
+            else:
+                m_grouped[g, 1] = after_weave[:, HALF:].bitcast(BF16)
+            for lo in (0, P):
+                cast_m("scalar", g, 1, lo, lo + P)
+            quantize_m(g, 1)
+        finish(1, HALF)
+        finish(2, 0)
+        finish(3, 0)

@@ -23,6 +23,7 @@ PACK = 4
 K_PASS = P * PACK
 ROW_PASSES = R // K_PASS
 ROW_TILES = R // P
+V_SCALAR = (128, 96)
 EARLY = 6
 PAD = 256
 PRODUCT_BANKS = 2
@@ -91,13 +92,14 @@ def tile_attend_gds_kl_kernel(tc, xT, wT, vT, wt, xm, offs, out):
             quantize(x_ops[g], E4M3, HALVES[half])
 
         w_op = operand("w", "staging")
+        first_planes = load(w_rows[:, :2, :], [P, 2, T], "w01")
         for j in range(PACK):
-            plane = load(w_rows[:, j, :], [P, T], "w%d" % j)
+            plane = first_planes[:, j, :] if j < 2 else load(w_rows[:, j, :], [P, T], "w%d" % j)[:]
             if j == 0:
                 nc.sync.dma_start(offsets[:], offs)
-                nc.sync.dma_start(out=weight_rows[:ROW_PASSES, :],
-                                  in_=wt[0].rearrange("(g r) o -> g (r o)", g=ROW_PASSES))
-            nc.vector.tensor_copy(w_op[0][:, :, j], plane[:].indirect(offsets[:]))
+                nc.scalar.dma_start(out=weight_rows[:ROW_PASSES, :],
+                                    in_=wt[0].rearrange("(g r) o -> g (r o)", g=ROW_PASSES))
+            nc.vector.tensor_copy(w_op[0][:, :, j], plane.indirect(offsets[:]))
         quantize(w_op, E4M3)
 
         turned = psum.tile([P, PACK, P], F32, name="bank5")
@@ -128,6 +130,7 @@ def tile_attend_gds_kl_kernel(tc, xT, wT, vT, wt, xm, offs, out):
             nc.scalar.activation(result[:], acc[:], ACT.Exp, bias=neg_max, accum_out=total)
             return result
 
+        v_listed = held.tile([P, PACK, N], F32, name="v_listed")
         s_max, s_sum, s_inv = stats("s_max"), stats("s_sum"), stats("s_inv")
         t_max, t_sum, t_inv, t_fac = stats("t_max"), stats("t_sum"), stats("t_inv"), stats("t_fac")
         e, z, student, m_grouped = {}, {}, {}, {}
@@ -156,7 +159,7 @@ def tile_attend_gds_kl_kernel(tc, xT, wT, vT, wt, xm, offs, out):
         def gather_v(j):
             for cols in (HALVES if j == PACK - 1 else [slice(0, N)]):
                 listed = offsets[:, cols.start // 16:cols.stop // 16]
-                nc.vector.tensor_copy(v_op[0][:, cols, j], v_planes[j][:].indirect(listed))
+                nc.vector.tensor_copy(v_listed[:, j, cols], v_planes[j][:].indirect(listed))
 
         HALF = N // 2
         g_grouped = [held.tile([P, N, PACK], BF16, name="g%d_grouped" % g, align_bytes=64) for g in range(ROW_PASSES)]
@@ -247,6 +250,9 @@ def tile_attend_gds_kl_kernel(tc, xT, wT, vT, wt, xm, offs, out):
         late_scores = {n: scores(w_op, n, n - 2) for n in range(EARLY, ROW_TILES)}
         gather_v(2)
         gather_v(3)
+        for cols, share in zip(HALVES, V_SCALAR):
+            interleave("scalar", v_op[0], v_listed, cols.start, cols.start + share)
+            interleave("vector", v_op[0], v_listed, cols.start + share, cols.stop)
         for cols in HALVES:
             quantize(v_op, E4M3, cols)
         m_raw = [load(m_rows[g], [P, PACK, D], "w%d" % (g + 2)) for g in range(ROW_PASSES)]
@@ -256,14 +262,14 @@ def tile_attend_gds_kl_kernel(tc, xT, wT, vT, wt, xm, offs, out):
         m_grouped[0, 0] = shared[:, N * PACK // 2:]
         m_grouped[1, 0] = held.tile([P, HALF * PACK], BF16, name="m_grouped", align_bytes=64)[:]
         cast_m("gpsimd", 0, 0)
-        cast_m("gpsimd", 1, 0, 0, 128)
+        cast_m("gpsimd", 1, 0, 0, 64)
         for n in range(ROW_TILES):
             z[n] = exps("t", scores(v_op, n, n % SCORE_BANKS), n, t_max[:, n:n + 1], t_sum[:, n:n + 1])
             if n == 2:
                 scale_on_gpsimd([6, 7])
             if n == 5:
                 teacher_factors(slice(0, 4))
-        cast_m("scalar", 1, 0, 128, HALF)
+        cast_m("scalar", 1, 0, 64, HALF)
         quantize_m(0, 0)
         teacher_factors(slice(4, 7))
         combine(0, 0)

@@ -50,13 +50,17 @@ def tile_attend_gds_kl_kernel(tc, xT, wT, vT, wt, xm, offs, out):
         x_rows = xT[0].rearrange("(p j) r -> p j r", j=PACK)
         m_rows = xm[0].rearrange("(g p j) d -> g p j d", p=P, j=PACK)
 
+        nc.sync.dma_start(offsets[:], offs)
+        first_plane = raw.tile([P, T], F32, name="w0")
+        nc.scalar.dma_start(out=first_plane[:], in_=w_rows[:, 0, :])
+
         zero = held.tile([P, 1], F32, name="zero")
         warm = held.tile([P, 1], F32, name="warm")
         nc.gpsimd.memset(zero[:], 0.0)
         nc.scalar.activation(warm[:], zero[:], ACT.Exp)
 
         weight_rows = held.tile([P, K_PASS], F32, name="weight_rows")
-        nc.vector.memset(weight_rows[:], 0.0)
+        nc.gpsimd.memset(weight_rows[:], 0.0)
         identity = held.tile([P, P], F32, name="identity")
         make_identity(nc, identity[:])
 
@@ -92,11 +96,9 @@ def tile_attend_gds_kl_kernel(tc, xT, wT, vT, wt, xm, offs, out):
             quantize(x_ops[g], E4M3, HALVES[half])
 
         w_op = operand("w", "staging")
-        first_planes = load(w_rows[:, :2, :], [P, 2, T], "w01")
         for j in range(PACK):
-            plane = first_planes[:, j, :] if j < 2 else load(w_rows[:, j, :], [P, T], "w%d" % j)[:]
+            plane = first_plane[:] if j == 0 else load(w_rows[:, j, :], [P, T], "w%d" % j)[:]
             if j == 0:
-                nc.sync.dma_start(offsets[:], offs)
                 nc.scalar.dma_start(out=weight_rows[:ROW_PASSES, :],
                                     in_=wt[0].rearrange("(g r) o -> g (r o)", g=ROW_PASSES))
             nc.vector.tensor_copy(w_op[0][:, :, j], plane.indirect(offsets[:]))

@@ -23,12 +23,13 @@ PACK = 4
 K_PASS = P * PACK
 ROW_PASSES = R // K_PASS
 ROW_TILES = R // P
-V_SCALAR = (128, 96)
-EARLY = 6
-PAD = 256
-PRODUCT_BANKS = 2
-SCORE_BANKS = 8 - 2
-HALVES = [slice(0, N // 2), slice(N // 2, N)]
+LIST_ROWS = 16
+HALF = N // 2
+HALVES = [slice(0, HALF), slice(HALF, N)]
+V_SCALAR_SHARE = (128, 96)
+FIRST_LATE_TILE = 6
+M_GPSIMD_SHARE = 32
+SCORE_BANKS = 6
 
 
 def tile_attend_gds_kl_kernel(tc, xT, wT, vT, wt, xm, offs, out):
@@ -38,7 +39,10 @@ def tile_attend_gds_kl_kernel(tc, xT, wT, vT, wt, xm, offs, out):
         raw = ctx.enter_context(tc.tile_pool(name="raw", bufs=1))
         psum = ctx.enter_context(tc.psum_pool(name="psum", bufs=1))
 
-        offsets = held.tile([P, N // 16], U16, name="offsets")
+        offsets = held.tile([P, N // LIST_ROWS], U16, name="offsets")
+
+        def listed(slots):
+            return offsets[:, slots.start // LIST_ROWS:slots.stop // LIST_ROWS]
 
         def load(source, shape, name):
             tile = raw.tile(shape, F32, name=name)
@@ -54,11 +58,6 @@ def tile_attend_gds_kl_kernel(tc, xT, wT, vT, wt, xm, offs, out):
         first_plane = raw.tile([P, T], F32, name="w0")
         nc.scalar.dma_start(out=first_plane[:], in_=w_rows[:, 0, :])
 
-        zero = held.tile([P, 1], F32, name="zero")
-        warm = held.tile([P, 1], F32, name="warm")
-        nc.gpsimd.memset(zero[:], 0.0)
-        nc.scalar.activation(warm[:], zero[:], ACT.Exp)
-
         weight_rows = held.tile([P, K_PASS], F32, name="weight_rows")
         nc.gpsimd.memset(weight_rows[:], 0.0)
         identity = held.tile([P, P], F32, name="identity")
@@ -66,7 +65,7 @@ def tile_attend_gds_kl_kernel(tc, xT, wT, vT, wt, xm, offs, out):
 
         windows = [held.tile([P, T], F32, name="window%d" % c) for c in range(D // P)]
         for c, window in enumerate(windows):
-            engine = nc.vector if c < 2 else nc.gpsimd
+            engine = nc.vector if c < len(windows) // 2 else nc.gpsimd
             engine.memset(window[:].bitcast(I32), 0)
 
         def operand(name, staging):
@@ -75,9 +74,9 @@ def tile_attend_gds_kl_kernel(tc, xT, wT, vT, wt, xm, offs, out):
             scales = held.tile([P, K_PASS], U8, name=name + "_scales", align_bytes=64)
             return grouped, codes, scales
 
-        def quantize(op, fmt, cols=slice(0, K_PASS)):
+        def quantize_e4m3(op, cols):
             grouped, codes, scales = op
-            nc.vector.quantize_mx(out=codes[:, cols].bitcast(fmt), scales=scales[:, cols],
+            nc.vector.quantize_mx(out=codes[:, cols].bitcast(E4M3), scales=scales[:, cols],
                                   in_=grouped[:, cols, :].rearrange("p c j -> p (c j)"))
 
         def copier(engine):
@@ -92,19 +91,15 @@ def tile_attend_gds_kl_kernel(tc, xT, wT, vT, wt, xm, offs, out):
             copier(engine)(out=x_ops[g][0][:].rearrange("p (t m) j -> p m j t", t=PACK)[:, :, :, tiles],
                            in_=x_raw[g][:].rearrange("p j (m t) -> p m j t", t=PACK)[:, :, :, tiles])
 
-        def quantize_x(g, half):
-            quantize(x_ops[g], E4M3, HALVES[half])
-
         w_op = operand("w", "staging")
-        for j in range(PACK):
-            plane = first_plane[:] if j == 0 else load(w_rows[:, j, :], [P, T], "w%d" % j)[:]
-            if j == 0:
-                nc.scalar.dma_start(out=weight_rows[:ROW_PASSES, :],
-                                    in_=wt[0].rearrange("(g r) o -> g (r o)", g=ROW_PASSES))
-            nc.vector.tensor_copy(w_op[0][:, :, j], plane.indirect(offsets[:]))
-        quantize(w_op, E4M3)
+        nc.scalar.dma_start(out=weight_rows[:ROW_PASSES, :], in_=wt[0].rearrange("(g r) o -> g (r o)", g=ROW_PASSES))
+        nc.vector.tensor_copy(w_op[0][:, :, 0], first_plane[:].indirect(offsets[:]))
+        for j in range(1, PACK):
+            plane = load(w_rows[:, j, :], [P, T], "w%d" % j)
+            nc.vector.tensor_copy(w_op[0][:, :, j], plane[:].indirect(offsets[:]))
+        quantize_e4m3(w_op, slice(0, N))
 
-        turned = psum.tile([P, PACK, P], F32, name="bank5")
+        turned = psum.tile([P, PACK, P], F32, name="bank%d" % (SCORE_BANKS - 1))
         for t in range(PACK):
             nc.tensor.transpose(turned[:, t, :], weight_rows[:, t::PACK], identity[:])
         weight = held.tile([P, ROW_PASSES, PACK], F32, name="weight")
@@ -118,99 +113,97 @@ def tile_attend_gds_kl_kernel(tc, xT, wT, vT, wt, xm, offs, out):
         def stats(name):
             return held.tile([P, ROW_TILES], F32, name=name, align_bytes=64)
 
-        def scores(table, tile_no, bank):
-            g, t = divmod(tile_no, PACK)
+        def scores(table, n, bank):
+            g, t = divmod(n, PACK)
             acc = psum.tile([P, N], F32, name="bank%d" % bank)
             cols = slice(t * P, (t + 1) * P)
             nc.tensor.matmul_mx(out=acc[:], lhsT=x_ops[g][1][:, cols].bitcast(E4M3), lhsT_scale=x_ops[g][2][:, cols],
                                 rhs=table[1][:].bitcast(E4M3), rhs_scale=table[2][:], start=True, stop=True)
             return acc
 
-        def exps(name, acc, tile_no, neg_max, total):
+        def student_bank(n):
+            return n if n < PACK else n - 2
+
+        def exps(name, acc, n, neg_max, total):
             nc.vector.tensor_reduce(out=neg_max, in_=acc[:], axis=AXIS_X, op=ALU.max, negate=True)
-            result = held.tile([P, N], F32, name="exp_%s%d" % (name, tile_no), align_bytes=64)
+            result = held.tile([P, N], F32, name="exp_%s%d" % (name, n), align_bytes=64)
             nc.scalar.activation(result[:], acc[:], ACT.Exp, bias=neg_max, accum_out=total)
             return result
 
         v_listed = held.tile([P, PACK, N], F32, name="v_listed")
         s_max, s_sum, s_inv = stats("s_max"), stats("s_sum"), stats("s_inv")
         t_max, t_sum, t_inv, t_fac = stats("t_max"), stats("t_sum"), stats("t_inv"), stats("t_fac")
-        e, z, student, m_grouped = {}, {}, {}, {}
+        student, teacher, m_grouped = {}, {}, {}
 
         def student_exps(tiles):
             for n in tiles:
-                neg_max = s_max[:, n:n + 1]
-                e[n] = exps("s", scores(w_op, n, n if n < 4 else n - 2), n, neg_max, s_sum[:, n:n + 1])
+                student[n] = exps("s", scores(w_op, n, student_bank(n)), n, s_max[:, n:n + 1], s_sum[:, n:n + 1])
 
-        def scale_on_gpsimd(tiles):
+        def scale_student(tiles):
             cols = slice(tiles[0], tiles[-1] + 1)
             nc.vector.reciprocal(s_inv[:, cols], s_sum[:, cols])
             for n in tiles:
-                student[n] = e[n][:]
-                nc.gpsimd.tensor_scalar(out=student[n], in0=e[n][:], scalar1=s_inv[:, n:n + 1],
+                nc.gpsimd.tensor_scalar(out=student[n][:], in0=student[n][:], scalar1=s_inv[:, n:n + 1],
                                         scalar2=weight_cols[:, n:n + 1], op0=ALU.mult, op1=ALU.mult)
 
-        def factors(total, inverse, factor, cols, sign):
-            nc.vector.reciprocal(inverse, total)
-            nc.vector.scalar_tensor_tensor(out=factor[:, cols], in0=inverse, scalar=sign,
+        def teacher_factors(cols):
+            nc.vector.reciprocal(t_inv[:, cols], t_sum[:, cols])
+            nc.vector.scalar_tensor_tensor(out=t_fac[:, cols], in0=t_inv[:, cols], scalar=-1.0,
                                            in1=weight_cols[:, cols], op0=ALU.mult, op1=ALU.mult)
 
-        def teacher_factors(cols):
-            factors(t_sum[:, cols], t_inv[:, cols], t_fac, cols, -1.0)
+        def gather_v(j, slots):
+            nc.vector.tensor_copy(v_listed[:, j, slots], v_planes[j][:].indirect(listed(slots)))
 
-        def gather_v(j):
-            for cols in (HALVES if j == PACK - 1 else [slice(0, N)]):
-                listed = offsets[:, cols.start // 16:cols.stop // 16]
-                nc.vector.tensor_copy(v_listed[:, j, cols], v_planes[j][:].indirect(listed))
-
-        HALF = N // 2
-        g_grouped = [held.tile([P, N, PACK], BF16, name="g%d_grouped" % g, align_bytes=64) for g in range(ROW_PASSES)]
-        g_codes = [held.tile([P, PAD + N], U32, name="g%d_codes" % g, align_bytes=64) for g in range(ROW_PASSES)]
-        g_scales = [held.tile([P, PAD + N], U8, name="g%d_scales" % g, align_bytes=64) for g in range(ROW_PASSES)]
+        g_grouped = {(g, h): held.tile([P, HALF * PACK], BF16, name="g_grouped%d%d" % (g, h), align_bytes=64)[:]
+                     for g, h in ((0, 0), (0, 1), (1, 1))}
+        g_shared = held.tile([P, HALF * (PACK + 1)], BF16, name="g_shared", align_bytes=64)
+        g_grouped[1, 0] = g_shared[:, HALF:]
+        g_codes = [held.tile([P, HALF + N], U32, name="g%d_codes" % g, align_bytes=64) for g in range(ROW_PASSES)]
+        g_scales = [held.tile([P, HALF + N], U8, name="g%d_scales" % g, align_bytes=64) for g in range(ROW_PASSES)]
         for g in range(ROW_PASSES):
-            nc.gpsimd.memset(g_codes[g][:, :PAD], 0)
-            nc.gpsimd.memset(g_scales[g][:, :PAD].bitcast(U32), 0)
+            nc.gpsimd.memset(g_codes[g][:, :HALF], 0)
+            nc.gpsimd.memset(g_scales[g][:, :HALF].bitcast(U32), 0)
+        padded_first_half = slice(0, N)
+        all_slots = slice(HALF, HALF + N)
         g_planes = {(g, h): held.tile([P, PACK, HALF], BF16, name="g_planes%d%d" % (g, h), align_bytes=64)
-                    for g in range(ROW_PASSES) for h in range(2)}
-        m_codes = held.tile([P, ROW_PASSES, D], U32, name="m_codes", align_bytes=64)
+                    for g, h in ((0, 0), (0, 1), (1, 0))}
+        g_planes[1, 1] = g_shared[:, :HALF * PACK].rearrange("p (j c) -> p j c", j=PACK)
+        m_codes = {}
         m_scales = held.tile([P, ROW_PASSES, D], U8, name="m_scales", align_bytes=64)
 
-        def cast_m(engine, g, h, lo=0, hi=HALF):
-            source = m_raw[g][:, :, h * HALF + lo:h * HALF + hi]
+        def cast_m(engine, g, h, lo, hi):
+            planes = m_raw[g][:, :, HALVES[h]]
             target = m_grouped[g, h].rearrange("p (m j) -> p m j", j=PACK)
             if engine == "gpsimd":
-                nc.gpsimd.tensor_copy(out=target[:, lo:hi, :], in_=source.rearrange("p j m -> p m j"))
+                nc.gpsimd.tensor_copy(out=target[:, lo:hi, :], in_=planes[:, :, lo:hi].rearrange("p j m -> p m j"))
             else:
-                interleave(engine, target, m_raw[g][:, :, HALVES[h]], lo, hi)
+                interleave(engine, target, planes, lo, hi)
 
-        def quantize_m(g, h):
-            nc.vector.quantize_mx(out=m_codes[:, g, HALVES[h]].bitcast(E4M3), scales=m_scales[:, g, HALVES[h]],
+        def quantize_m(g, h, name):
+            m_codes[g, h] = held.tile([P, HALF], U32, name=name, align_bytes=64)
+            nc.vector.quantize_mx(out=m_codes[g, h][:].bitcast(E4M3), scales=m_scales[:, g, HALVES[h]],
                                   in_=m_grouped[g, h])
 
         def combine(g, h):
-            cols = HALVES[h]
             for t in range(PACK):
                 n = g * PACK + t
-                nc.vector.scalar_tensor_tensor(out=g_planes[g, h][:, t, :], in0=z[n][:, cols], scalar=t_fac[:, n:n + 1],
-                                               in1=student[n][:, cols], op0=ALU.mult, op1=ALU.add)
+                nc.vector.scalar_tensor_tensor(out=g_planes[g, h][:, t, :], in0=teacher[n][:, HALVES[h]],
+                                               scalar=t_fac[:, n:n + 1], in1=student[n][:, HALVES[h]],
+                                               op0=ALU.mult, op1=ALU.add)
 
-        def weave_g(g, h, share=HALF):
-            target = g_grouped[g][:, HALVES[h], :]
-            interleave("scalar", target, g_planes[g, h], 0, share)
-            if share < HALF:
-                interleave("vector", target, g_planes[g, h], share, HALF)
+        def interleave_g(g, h):
+            interleave("scalar", g_grouped[g, h].rearrange("p (c j) -> p c j", j=PACK), g_planes[g, h], 0, HALF)
 
         def quantize_g(g, h):
-            cols = slice(PAD + h * HALF, PAD + (h + 1) * HALF)
+            cols = slice((h + 1) * HALF, (h + 2) * HALF)
             nc.vector.quantize_mx(out=g_codes[g][:, cols].bitcast(E5M2), scales=g_scales[g][:, cols],
-                                  in_=g_grouped[g][:, HALVES[h], :].rearrange("p c j -> p (c j)"))
+                                  in_=g_grouped[g, h])
 
         def product(c, cols, bank):
             acc = psum.tile([P, N], F32, name="product%d" % bank)
-            width = cols.stop - cols.start
+            block = slice(c * P, (c + 1) * P)
             for g in range(ROW_PASSES):
-                nc.tensor.matmul_mx(out=acc[:, :width], lhsT=m_codes[:, g, c * P:(c + 1) * P].bitcast(E4M3),
-                                    lhsT_scale=m_scales[:, g, c * P:(c + 1) * P],
+                nc.tensor.matmul_mx(out=acc[:], lhsT=m_codes[g, c // 2][:, c % 2 * P:(c % 2 + 1) * P].bitcast(E4M3), lhsT_scale=m_scales[:, g, block],
                                     rhs=g_codes[g][:, cols].bitcast(E5M2), rhs_scale=g_scales[g][:, cols],
                                     start=g == 0, stop=g == ROW_PASSES - 1)
             return acc
@@ -220,96 +213,100 @@ def tile_attend_gds_kl_kernel(tc, xT, wT, vT, wt, xm, offs, out):
             nc.scalar.copy(out=dw[:], in_=source)
             return dw[:]
 
-        def scatter(c, dw, cols):
-            listed = offsets[:, cols.start // 16:cols.stop // 16]
-            nc.vector.tensor_copy(windows[c][:].indirect(listed), dw)
+        def scatter(c, dw, slots):
+            nc.vector.tensor_copy(windows[c][:].indirect(listed(slots)), dw)
 
-        def store(c):
+        def finish(c, first_slot):
+            acc = product(c, all_slots, (c + 1) % 2)
+            scatter(c, copy_out(acc[:, first_slot:], N - first_slot, "dw%d" % c), slice(first_slot, N))
             nc.sync.dma_start(out=out[c * P:(c + 1) * P, :], in_=windows[c][:])
 
-        x_ops.append(operand("x0", "x0_grouped"))
+        x_ops.append(operand("x0", "x_grouped"))
         cast_x(0, 0, "vector")
         cast_x(0, 1, "scalar")
-        quantize_x(0, 0)
-        quantize_x(0, 1)
-        x_ops.append(operand("x1", "x0_grouped"))
+        for cols in HALVES:
+            quantize_e4m3(x_ops[0], cols)
+        x_ops.append(operand("x1", "x_grouped"))
         cast_x(1, 0, "scalar")
         student_exps([0, 1, 2, 3])
-        quantize_x(1, 0)
-        scale_on_gpsimd([0, 1])
-        shared = held.tile([P, N * PACK], BF16, name="staging", align_bytes=64)
-        v_op = (shared[:].rearrange("p (c j) -> p c j", j=PACK),
+        quantize_e4m3(x_ops[1], HALVES[0])
+        scale_student([0, 1])
+        v_staging = held.tile([P, N * PACK], BF16, name="staging", align_bytes=64)
+        v_op = (v_staging[:].rearrange("p (c j) -> p c j", j=PACK),
                 held.tile([P, K_PASS], U32, name="v_codes", align_bytes=64),
                 held.tile([P, K_PASS], U8, name="v_scales", align_bytes=64))
-        gather_v(0)
+        gather_v(0, slice(0, N))
         student_exps([4, 5])
         cast_x(1, 1, "scalar")
-        scale_on_gpsimd([2, 3])
-        gather_v(1)
-        quantize_x(1, 1)
-        scale_on_gpsimd([4, 5])
-        student_exps(range(6, EARLY))
-        late_scores = {n: scores(w_op, n, n - 2) for n in range(EARLY, ROW_TILES)}
-        gather_v(2)
-        gather_v(3)
-        for cols, share in zip(HALVES, V_SCALAR):
-            interleave("scalar", v_op[0], v_listed, cols.start, cols.start + share)
-            interleave("vector", v_op[0], v_listed, cols.start + share, cols.stop)
-        for cols in HALVES:
-            quantize(v_op, E4M3, cols)
+        scale_student([2, 3])
+        gather_v(1, slice(0, N))
+        quantize_e4m3(x_ops[1], HALVES[1])
+        scale_student([4, 5])
+        late_tiles = list(range(FIRST_LATE_TILE, ROW_TILES))
+        late_scores = {n: scores(w_op, n, student_bank(n)) for n in late_tiles}
+        gather_v(2, slice(0, N))
+
+        for slots in HALVES:
+            gather_v(PACK - 1, slots)
+        for slots, share in zip(HALVES, V_SCALAR_SHARE):
+            interleave("scalar", v_op[0], v_listed, slots.start, slots.start + share)
+            interleave("vector", v_op[0], v_listed, slots.start + share, slots.stop)
+        for slots in HALVES:
+            quantize_e4m3(v_op, slots)
         m_raw = [load(m_rows[g], [P, PACK, D], "w%d" % (g + 2)) for g in range(ROW_PASSES)]
-        late_max = shared[:, N * PACK // 2 - 16:N * PACK // 2].bitcast(F32)
-        for n in range(EARLY, ROW_TILES):
-            e[n] = exps("s", late_scores[n], n, late_max[:, n:n + 1], s_sum[:, n:n + 1])
-        m_grouped[0, 0] = shared[:, N * PACK // 2:]
+
+        late_max = v_staging[:, HALF * PACK - 2 * ROW_TILES:HALF * PACK].bitcast(F32)
+        m_grouped[0, 1] = held.tile([P, HALF * PACK], BF16, name="m01_grouped", align_bytes=64)[:]
+        for n in late_tiles:
+            student[n] = exps("s", late_scores[n], n, late_max[:, n:n + 1], s_sum[:, n:n + 1])
+        m_grouped[0, 0] = v_staging[:, HALF * PACK:]
         m_grouped[1, 0] = held.tile([P, HALF * PACK], BF16, name="m_grouped", align_bytes=64)[:]
-        cast_m("gpsimd", 0, 0)
-        cast_m("gpsimd", 1, 0, 0, 64)
-        for n in range(ROW_TILES):
-            z[n] = exps("t", scores(v_op, n, n % SCORE_BANKS), n, t_max[:, n:n + 1], t_sum[:, n:n + 1])
-            if n == 2:
-                scale_on_gpsimd([6, 7])
-            if n == 5:
-                teacher_factors(slice(0, 4))
-        cast_m("scalar", 1, 0, 64, HALF)
-        quantize_m(0, 0)
-        teacher_factors(slice(4, 7))
+        cast_m("gpsimd", 0, 0, 0, HALF)
+        cast_m("gpsimd", 0, 1, 0, HALF)
+        cast_m("gpsimd", 1, 0, 0, M_GPSIMD_SHARE)
+
+        def teacher_exps(tiles):
+            for n in tiles:
+                teacher[n] = exps("t", scores(v_op, n, n % SCORE_BANKS), n, t_max[:, n:n + 1], t_sum[:, n:n + 1])
+
+        teacher_exps([0, 1, 2])
+        scale_student(late_tiles)
+        teacher_exps([3, 4, 5])
+        teacher_factors(slice(0, PACK))
+        teacher_exps([6, 7])
+        cast_m("scalar", 1, 0, M_GPSIMD_SHARE, HALF)
+        quantize_m(0, 0, "m_codes00")
+
+        teacher_factors(slice(PACK, ROW_TILES - 1))
         combine(0, 0)
-        weave_g(0, 0)
-        teacher_factors(slice(7, 8))
+        interleave_g(0, 0)
+        teacher_factors(slice(ROW_TILES - 1, ROW_TILES))
         combine(1, 0)
-        weave_g(1, 0, 256)
+        interleave_g(1, 0)
         quantize_g(1, 0)
         combine(0, 1)
         quantize_g(0, 0)
-        quantize_m(1, 0)
-        early = product(0, slice(0, N), 0)
-        weave_g(0, 1)
-        first = copy_out(early[:, HALF:], HALF, "dw_first0")
+        quantize_m(1, 0, "m_codes10")
+
+        early = product(0, padded_first_half, 0)
+        interleave_g(0, 1)
+        dw_early = copy_out(early[:, HALF:], HALF, "dw_early")
         combine(1, 1)
-        weave_g(1, 1)
+        interleave_g(1, 1)
         quantize_g(0, 1)
+        quantize_m(0, 1, "exp_s6")
         quantize_g(1, 1)
-        scatter(0, first, HALVES[0])
-        early = product(1, slice(0, N), 0)
-        after_weave = held.tile([P, HALF + N], F32, name="g_planes11", align_bytes=64)
-        nc.scalar.copy(out=after_weave[:, :HALF], in_=early[:, HALF:])
-        scatter(1, after_weave[:, :HALF], HALVES[0])
+        scatter(0, dw_early, HALVES[0])
 
-        def finish(c, first_slot):
-            acc = product(c, slice(PAD, PAD + N), (c + 1) % 2)
-            scatter(c, copy_out(acc[:, first_slot:], N - first_slot, "dw%d" % c), slice(first_slot, N))
-            store(c)
-
+        early = product(1, padded_first_half, 0)
+        after_g = held.tile([P, HALF + N], F32, name="g_shared", align_bytes=64)
+        nc.scalar.copy(out=after_g[:, :HALF], in_=early[:, HALF:])
+        scatter(1, after_g[:, :HALF], HALVES[0])
         finish(0, HALF)
-        for g in range(ROW_PASSES):
-            if g == 0:
-                m_grouped[g, 1] = held.tile([P, HALF * PACK], BF16, name="g_planes01", align_bytes=64)[:]
-            else:
-                m_grouped[g, 1] = after_weave[:, HALF:].bitcast(BF16)
-            for lo in (0, P):
-                cast_m("scalar", g, 1, lo, lo + P)
-            quantize_m(g, 1)
+        m_grouped[1, 1] = after_g[:, HALF:].bitcast(BF16)
+        for lo in (0, P):
+            cast_m("scalar", 1, 1, lo, lo + P)
+        quantize_m(1, 1, "m_codes11")
         finish(1, HALF)
         finish(2, 0)
         finish(3, 0)

@@ -29,6 +29,7 @@ HALVES = [slice(0, HALF), slice(HALF, N)]
 V_SCALAR_SHARE = (128, 96)
 FIRST_LATE_TILE = 6
 M_GPSIMD_SHARE = 32
+M_GPSIMD_COLUMNS = 192
 SCORE_BANKS = 6
 
 
@@ -93,19 +94,21 @@ def tile_attend_gds_kl_kernel(tc, xT, wT, vT, wt, xm, offs, out):
 
         w_op = operand("w", "staging")
         nc.scalar.dma_start(out=weight_rows[:ROW_PASSES, :], in_=wt[0].rearrange("(g r) o -> g (r o)", g=ROW_PASSES))
-        nc.vector.tensor_copy(w_op[0][:, :, 0], first_plane[:].indirect(offsets[:]))
-        for j in range(1, PACK):
-            plane = load(w_rows[:, j, :], [P, T], "w%d" % j)
-            nc.vector.tensor_copy(w_op[0][:, :, j], plane[:].indirect(offsets[:]))
-        quantize_e4m3(w_op, slice(0, N))
+        w_planes = [first_plane] + [load(w_rows[:, j, :], [P, T], "w%d" % j) for j in range(1, PACK)]
+        w_listed = held.tile([P, PACK, N], F32, name="w_listed")
+        for j in range(PACK - 1):
+            nc.vector.tensor_copy(w_listed[:, j, :], w_planes[j][:].indirect(offsets[:]))
+        for slots in HALVES:
+            nc.vector.tensor_copy(w_listed[:, PACK - 1, slots], w_planes[PACK - 1][:].indirect(listed(slots)))
+        for slots, share in zip(HALVES, V_SCALAR_SHARE):
+            interleave("scalar", w_op[0], w_listed, slots.start, slots.start + share)
+            interleave("vector", w_op[0], w_listed, slots.start + share, slots.stop)
+        for slots in HALVES:
+            quantize_e4m3(w_op, slots)
 
         turned = psum.tile([P, PACK, P], F32, name="bank%d" % (SCORE_BANKS - 1))
         for t in range(PACK):
             nc.tensor.transpose(turned[:, t, :], weight_rows[:, t::PACK], identity[:])
-        weight = held.tile([P, ROW_PASSES, PACK], F32, name="weight")
-        nc.scalar.copy(out=weight[:], in_=turned[:, :, :ROW_PASSES].rearrange("p t g -> p g t"))
-        weight_cols = weight[:].rearrange("p g t -> p (g t)")
-
         x_ops = []
         x_raw = [load(x_rows[:, :, g * K_PASS:(g + 1) * K_PASS], [P, PACK, K_PASS], "x%d" % g) for g in range(ROW_PASSES)]
         v_planes = [load(v_rows[:, j, :], [P, T], "v%d" % j) for j in range(PACK)]
@@ -166,7 +169,10 @@ def tile_attend_gds_kl_kernel(tc, xT, wT, vT, wt, xm, offs, out):
         padded_first_half = slice(0, N)
         all_slots = slice(HALF, HALF + N)
         g_planes = {(g, h): held.tile([P, PACK, HALF], BF16, name="g_planes%d%d" % (g, h), align_bytes=64)
-                    for g, h in ((0, 0), (0, 1), (1, 0))}
+                    for g, h in ((0, 0), (0, 1))}
+        m_shared = held.tile([P, (M_GPSIMD_COLUMNS + HALF) * PACK], BF16, name="m_shared", align_bytes=64)
+        g_planes[1, 0] = m_shared[:, M_GPSIMD_COLUMNS * PACK:].rearrange("p (j c) -> p j c", j=PACK)
+        m_grouped[0, 1] = m_shared[:, :HALF * PACK]
         g_planes[1, 1] = g_shared[:, :HALF * PACK].rearrange("p (j c) -> p j c", j=PACK)
         m_codes = {}
         m_scales = held.tile([P, ROW_PASSES, D], U8, name="m_scales", align_bytes=64)
@@ -226,6 +232,10 @@ def tile_attend_gds_kl_kernel(tc, xT, wT, vT, wt, xm, offs, out):
         cast_x(0, 1, "scalar")
         for cols in HALVES:
             quantize_e4m3(x_ops[0], cols)
+        weight = raw.tile([P, ROW_PASSES, PACK], F32, name="x0")
+        nc.scalar.copy(out=weight[:], in_=turned[:, :, :ROW_PASSES].rearrange("p t g -> p g t"))
+        weight_cols = weight[:].rearrange("p g t -> p (g t)")
+
         x_ops.append(operand("x1", "x_grouped"))
         cast_x(1, 0, "scalar")
         student_exps([0, 1, 2, 3])
@@ -256,13 +266,12 @@ def tile_attend_gds_kl_kernel(tc, xT, wT, vT, wt, xm, offs, out):
         m_raw = [load(m_rows[g], [P, PACK, D], "w%d" % (g + 2)) for g in range(ROW_PASSES)]
 
         late_max = v_staging[:, HALF * PACK - 2 * ROW_TILES:HALF * PACK].bitcast(F32)
-        m_grouped[0, 1] = held.tile([P, HALF * PACK], BF16, name="m01_grouped", align_bytes=64)[:]
         for n in late_tiles:
             student[n] = exps("s", late_scores[n], n, late_max[:, n:n + 1], s_sum[:, n:n + 1])
         m_grouped[0, 0] = v_staging[:, HALF * PACK:]
         m_grouped[1, 0] = held.tile([P, HALF * PACK], BF16, name="m_grouped", align_bytes=64)[:]
         cast_m("gpsimd", 0, 0, 0, HALF)
-        cast_m("gpsimd", 0, 1, 0, HALF)
+        cast_m("gpsimd", 0, 1, 0, M_GPSIMD_COLUMNS)
         cast_m("gpsimd", 1, 0, 0, M_GPSIMD_SHARE)
 
         def teacher_exps(tiles):
@@ -290,6 +299,7 @@ def tile_attend_gds_kl_kernel(tc, xT, wT, vT, wt, xm, offs, out):
 
         early = product(0, padded_first_half, 0)
         interleave_g(0, 1)
+        cast_m("scalar", 0, 1, M_GPSIMD_COLUMNS, HALF)
         dw_early = copy_out(early[:, HALF:], HALF, "dw_early")
         combine(1, 1)
         interleave_g(1, 1)

@@ -28,8 +28,6 @@ HALF = N // 2
 HALVES = [slice(0, HALF), slice(HALF, N)]
 V_SCALAR_SHARE = (128, 96)
 FIRST_LATE_TILE = 6
-M_GPSIMD_SHARE = 32
-M_GPSIMD_COLUMNS = 192
 SCORE_BANKS = 6
 
 
@@ -116,16 +114,18 @@ def tile_attend_gds_kl_kernel(tc, xT, wT, vT, wt, xm, offs, out):
         def stats(name):
             return held.tile([P, ROW_TILES], F32, name=name, align_bytes=64)
 
-        def scores(table, n, bank):
+        def scores(table, n, bank, parts=(slice(0, N),)):
             g, t = divmod(n, PACK)
             acc = psum.tile([P, N], F32, name="bank%d" % bank)
             cols = slice(t * P, (t + 1) * P)
-            nc.tensor.matmul_mx(out=acc[:], lhsT=x_ops[g][1][:, cols].bitcast(E4M3), lhsT_scale=x_ops[g][2][:, cols],
-                                rhs=table[1][:].bitcast(E4M3), rhs_scale=table[2][:], start=True, stop=True)
+            for slots in parts:
+                nc.tensor.matmul_mx(out=acc[:, slots], lhsT=x_ops[g][1][:, cols].bitcast(E4M3),
+                                    lhsT_scale=x_ops[g][2][:, cols], rhs=table[1][:, slots].bitcast(E4M3),
+                                    rhs_scale=table[2][:, slots], start=True, stop=True)
             return acc
 
         def student_bank(n):
-            return n if n < PACK else n - 2
+            return n % SCORE_BANKS
 
         def exps(name, acc, n, neg_max, total):
             nc.vector.tensor_reduce(out=neg_max, in_=acc[:], axis=AXIS_X, op=ALU.max, negate=True)
@@ -136,7 +136,7 @@ def tile_attend_gds_kl_kernel(tc, xT, wT, vT, wt, xm, offs, out):
         v_listed = held.tile([P, PACK, N], F32, name="v_listed")
         s_max, s_sum, s_inv = stats("s_max"), stats("s_sum"), stats("s_inv")
         t_max, t_sum, t_inv, t_fac = stats("t_max"), stats("t_sum"), stats("t_inv"), stats("t_fac")
-        student, teacher, m_grouped = {}, {}, {}
+        student, teacher = {}, {}
 
         def student_exps(tiles):
             for n in tiles:
@@ -149,18 +149,16 @@ def tile_attend_gds_kl_kernel(tc, xT, wT, vT, wt, xm, offs, out):
                 nc.gpsimd.tensor_scalar(out=student[n][:], in0=student[n][:], scalar1=s_inv[:, n:n + 1],
                                         scalar2=weight_cols[:, n:n + 1], op0=ALU.mult, op1=ALU.mult)
 
-        def teacher_factors(cols):
+        def teacher_inverses(cols):
             nc.vector.reciprocal(t_inv[:, cols], t_sum[:, cols])
+
+        def teacher_factors(cols):
             nc.vector.scalar_tensor_tensor(out=t_fac[:, cols], in0=t_inv[:, cols], scalar=-1.0,
                                            in1=weight_cols[:, cols], op0=ALU.mult, op1=ALU.mult)
 
         def gather_v(j, slots):
             nc.vector.tensor_copy(v_listed[:, j, slots], v_planes[j][:].indirect(listed(slots)))
 
-        g_grouped = {(g, h): held.tile([P, HALF * PACK], BF16, name="g_grouped%d%d" % (g, h), align_bytes=64)[:]
-                     for g, h in ((0, 0), (0, 1), (1, 1))}
-        g_shared = held.tile([P, HALF * (PACK + 1)], BF16, name="g_shared", align_bytes=64)
-        g_grouped[1, 0] = g_shared[:, HALF:]
         g_codes = [held.tile([P, HALF + N], U32, name="g%d_codes" % g, align_bytes=64) for g in range(ROW_PASSES)]
         g_scales = [held.tile([P, HALF + N], U8, name="g%d_scales" % g, align_bytes=64) for g in range(ROW_PASSES)]
         for g in range(ROW_PASSES):
@@ -168,50 +166,52 @@ def tile_attend_gds_kl_kernel(tc, xT, wT, vT, wt, xm, offs, out):
             nc.gpsimd.memset(g_scales[g][:, :HALF].bitcast(U32), 0)
         padded_first_half = slice(0, N)
         all_slots = slice(HALF, HALF + N)
-        g_planes = {(g, h): held.tile([P, PACK, HALF], BF16, name="g_planes%d%d" % (g, h), align_bytes=64)
-                    for g, h in ((0, 0), (0, 1))}
-        m_shared = held.tile([P, (M_GPSIMD_COLUMNS + HALF) * PACK], BF16, name="m_shared", align_bytes=64)
-        g_planes[1, 0] = m_shared[:, M_GPSIMD_COLUMNS * PACK:].rearrange("p (j c) -> p j c", j=PACK)
-        m_grouped[0, 1] = m_shared[:, :HALF * PACK]
-        g_planes[1, 1] = g_shared[:, :HALF * PACK].rearrange("p (j c) -> p j c", j=PACK)
-        m_codes = {}
+        g_grouped, g_planes = {}, {}
+        m_codes = [held.tile([P, D], U32, name="m_codes%d" % g, align_bytes=64) for g in range(ROW_PASSES)]
         m_scales = held.tile([P, ROW_PASSES, D], U8, name="m_scales", align_bytes=64)
 
-        def cast_m(engine, g, h, lo, hi):
-            planes = m_raw[g][:, :, HALVES[h]]
-            target = m_grouped[g, h].rearrange("p (m j) -> p m j", j=PACK)
+        def half_tile(name):
+            tile = held.tile([P, HALF * PACK], BF16, name=name, align_bytes=64)
+            return tile[:]
+
+        def as_planes(flat):
+            return flat.rearrange("p (j c) -> p j c", j=PACK)
+
+        def as_grouped(flat):
+            return flat.rearrange("p (c j) -> p c j", j=PACK)
+
+        def cast_m(engine, g, cols, target):
+            planes = m_raw[g][:, :, cols]
             if engine == "gpsimd":
-                nc.gpsimd.tensor_copy(out=target[:, lo:hi, :], in_=planes[:, :, lo:hi].rearrange("p j m -> p m j"))
+                nc.gpsimd.tensor_copy(out=as_grouped(target), in_=planes.rearrange("p j m -> p m j"))
             else:
-                interleave(engine, target, planes, lo, hi)
+                interleave(engine, as_grouped(target), planes, 0, cols.stop - cols.start)
 
-        def quantize_m(g, h, name):
-            m_codes[g, h] = held.tile([P, HALF], U32, name=name, align_bytes=64)
-            nc.vector.quantize_mx(out=m_codes[g, h][:].bitcast(E4M3), scales=m_scales[:, g, HALVES[h]],
-                                  in_=m_grouped[g, h])
+        def quantize_m(g, cols, source):
+            nc.vector.quantize_mx(out=m_codes[g][:, cols].bitcast(E4M3), scales=m_scales[:, g, cols], in_=source)
 
-        def combine(g, h):
-            for t in range(PACK):
+        def combine(g, h, planes=range(PACK)):
+            for t in planes:
                 n = g * PACK + t
                 nc.vector.scalar_tensor_tensor(out=g_planes[g, h][:, t, :], in0=teacher[n][:, HALVES[h]],
                                                scalar=t_fac[:, n:n + 1], in1=student[n][:, HALVES[h]],
                                                op0=ALU.mult, op1=ALU.add)
 
-        def interleave_g(g, h):
-            interleave("scalar", g_grouped[g, h].rearrange("p (c j) -> p c j", j=PACK), g_planes[g, h], 0, HALF)
+        def interleave_g(g, h, engine="scalar", lo=0, hi=HALF):
+            interleave(engine, as_grouped(g_grouped[g, h]), g_planes[g, h], lo, hi)
 
         def quantize_g(g, h):
             cols = slice((h + 1) * HALF, (h + 2) * HALF)
             nc.vector.quantize_mx(out=g_codes[g][:, cols].bitcast(E5M2), scales=g_scales[g][:, cols],
                                   in_=g_grouped[g, h])
 
-        def product(c, cols, bank):
-            acc = psum.tile([P, N], F32, name="product%d" % bank)
+        def product(c, cols, bank, passes=(0, 1)):
+            acc = psum.tile([P, N], F32, name=bank)
             block = slice(c * P, (c + 1) * P)
-            for g in range(ROW_PASSES):
-                nc.tensor.matmul_mx(out=acc[:], lhsT=m_codes[g, c // 2][:, c % 2 * P:(c % 2 + 1) * P].bitcast(E4M3), lhsT_scale=m_scales[:, g, block],
+            for g in passes:
+                nc.tensor.matmul_mx(out=acc[:], lhsT=m_codes[g][:, block].bitcast(E4M3), lhsT_scale=m_scales[:, g, block],
                                     rhs=g_codes[g][:, cols].bitcast(E5M2), rhs_scale=g_scales[g][:, cols],
-                                    start=g == 0, stop=g == ROW_PASSES - 1)
+                                    start=g == passes[0], stop=g == passes[-1])
             return acc
 
         def copy_out(source, width, name):
@@ -223,7 +223,7 @@ def tile_attend_gds_kl_kernel(tc, xT, wT, vT, wt, xm, offs, out):
             nc.vector.tensor_copy(windows[c][:].indirect(listed(slots)), dw)
 
         def finish(c, first_slot):
-            acc = product(c, all_slots, (c + 1) % 2)
+            acc = product(c, all_slots, "product%d" % ((c + 1) % 2))
             scatter(c, copy_out(acc[:, first_slot:], N - first_slot, "dw%d" % c), slice(first_slot, N))
             nc.sync.dma_start(out=out[c * P:(c + 1) * P, :], in_=windows[c][:])
 
@@ -238,23 +238,26 @@ def tile_attend_gds_kl_kernel(tc, xT, wT, vT, wt, xm, offs, out):
 
         x_ops.append(operand("x1", "x_grouped"))
         cast_x(1, 0, "scalar")
+        cast_x(1, 1, "scalar")
         student_exps([0, 1, 2, 3])
-        quantize_e4m3(x_ops[1], HALVES[0])
-        scale_student([0, 1])
+        quantize_e4m3(x_ops[1], slice(0, K_PASS))
         v_staging = held.tile([P, N * PACK], BF16, name="staging", align_bytes=64)
         v_op = (v_staging[:].rearrange("p (c j) -> p c j", j=PACK),
                 held.tile([P, K_PASS], U32, name="v_codes", align_bytes=64),
                 held.tile([P, K_PASS], U8, name="v_scales", align_bytes=64))
         gather_v(0, slice(0, N))
+        scale_student([0, 1])
         student_exps([4, 5])
-        cast_x(1, 1, "scalar")
         scale_student([2, 3])
-        gather_v(1, slice(0, N))
-        quantize_e4m3(x_ops[1], HALVES[1])
+        student_exps([6, 7])
         scale_student([4, 5])
-        late_tiles = list(range(FIRST_LATE_TILE, ROW_TILES))
-        late_scores = {n: scores(w_op, n, student_bank(n)) for n in late_tiles}
+        gather_v(1, slice(0, N))
+        late = slice(FIRST_LATE_TILE, ROW_TILES)
+        nc.vector.reciprocal(s_inv[:, late], s_sum[:, late])
         gather_v(2, slice(0, N))
+        s_fac = stats("s_fac")
+        for n in range(FIRST_LATE_TILE, ROW_TILES):
+            nc.scalar.activation(s_fac[:, n:n + 1], s_inv[:, n:n + 1], ACT.Copy, scale=weight_cols[:, n:n + 1])
 
         for slots in HALVES:
             gather_v(PACK - 1, slots)
@@ -263,60 +266,68 @@ def tile_attend_gds_kl_kernel(tc, xT, wT, vT, wt, xm, offs, out):
             interleave("vector", v_op[0], v_listed, slots.start + share, slots.stop)
         for slots in HALVES:
             quantize_e4m3(v_op, slots)
+        scaled_late = held.tile([P, (ROW_TILES - FIRST_LATE_TILE) * N], F32, name="v_listed")
+        for n in range(FIRST_LATE_TILE, ROW_TILES):
+            target = scaled_late[:, (n - FIRST_LATE_TILE) * N:(n - FIRST_LATE_TILE + 1) * N]
+            nc.scalar.activation(target, student[n][:], ACT.Copy, scale=s_fac[:, n:n + 1])
+            student[n] = target
         m_raw = [load(m_rows[g], [P, PACK, D], "w%d" % (g + 2)) for g in range(ROW_PASSES)]
 
-        late_max = v_staging[:, HALF * PACK - 2 * ROW_TILES:HALF * PACK].bitcast(F32)
-        for n in late_tiles:
-            student[n] = exps("s", late_scores[n], n, late_max[:, n:n + 1], s_sum[:, n:n + 1])
-        m_grouped[0, 0] = v_staging[:, HALF * PACK:]
-        m_grouped[1, 0] = held.tile([P, HALF * PACK], BF16, name="m_grouped", align_bytes=64)[:]
-        cast_m("gpsimd", 0, 0, 0, HALF)
-        cast_m("gpsimd", 0, 1, 0, M_GPSIMD_COLUMNS)
-        cast_m("gpsimd", 1, 0, 0, M_GPSIMD_SHARE)
+        m_first = held.tile([P, 2 * HALF * PACK], BF16, name="staging", align_bytes=64)
+        m_second = [half_tile("m_second0"), None]
+        first = [m_first[:, g * HALF * PACK:(g + 1) * HALF * PACK] for g in range(ROW_PASSES)]
+        for g in range(ROW_PASSES):
+            cast_m("gpsimd", g, HALVES[0], first[g])
+        cast_m("scalar", 0, HALVES[1], m_second[0])
 
         def teacher_exps(tiles):
             for n in tiles:
-                teacher[n] = exps("t", scores(v_op, n, n % SCORE_BANKS), n, t_max[:, n:n + 1], t_sum[:, n:n + 1])
+                acc = scores(v_op, n, (n + 2) % SCORE_BANKS, HALVES if n == 0 else (slice(0, N),))
+                teacher[n] = exps("t", acc, n, t_max[:, n:n + 1], t_sum[:, n:n + 1])
 
-        teacher_exps([0, 1, 2])
-        scale_student(late_tiles)
-        teacher_exps([3, 4, 5])
+        teacher_exps([0, 1, 2, 3, 4, 5, 6])
+        teacher_inverses(slice(0, PACK))
+        teacher_exps([7])
         teacher_factors(slice(0, PACK))
-        teacher_exps([6, 7])
-        cast_m("scalar", 1, 0, M_GPSIMD_SHARE, HALF)
-        quantize_m(0, 0, "m_codes00")
-
-        teacher_factors(slice(PACK, ROW_TILES - 1))
-        combine(0, 0)
+        quantize_m(0, HALVES[0], first[0])
+        for g in range(ROW_PASSES):
+            g_planes[g, 0] = as_planes(half_tile("g_planes%d0" % g))
+            g_grouped[g, 0] = half_tile("g_grouped%d0" % g)
+        pair = [slice(PACK, PACK + 2), slice(PACK + 2, ROW_TILES)]
+        teacher_inverses(pair[0])
+        combine(0, 0, [0])
+        teacher_factors(pair[0])
+        combine(0, 0, [1, 2, 3])
         interleave_g(0, 0)
-        teacher_factors(slice(ROW_TILES - 1, ROW_TILES))
-        combine(1, 0)
+        teacher_inverses(pair[1])
+        combine(1, 0, [0])
+        teacher_factors(pair[1])
+        combine(1, 0, [1, 2, 3])
         interleave_g(1, 0)
+        g_planes[0, 1] = as_planes(half_tile("g_planes01"))
         quantize_g(1, 0)
         combine(0, 1)
         quantize_g(0, 0)
-        quantize_m(1, 0, "m_codes10")
-
-        early = product(0, padded_first_half, 0)
+        quantize_m(1, HALVES[0], first[1])
+        early = product(0, padded_first_half, "product0")
+        dw_early = copy_out(early[:, HALF:], HALF, "dw_early0")
+        g_grouped[0, 1] = half_tile("g_grouped00")
         interleave_g(0, 1)
-        cast_m("scalar", 0, 1, M_GPSIMD_COLUMNS, HALF)
-        dw_early = copy_out(early[:, HALF:], HALF, "dw_early")
+        g_planes[1, 1] = as_planes(half_tile("staging"))
         combine(1, 1)
+        quantize_m(0, HALVES[1], m_second[0])
+        g_grouped[1, 1] = half_tile("g_grouped10")
         interleave_g(1, 1)
         quantize_g(0, 1)
-        quantize_m(0, 1, "exp_s6")
-        quantize_g(1, 1)
         scatter(0, dw_early, HALVES[0])
-
-        early = product(1, padded_first_half, 0)
-        after_g = held.tile([P, HALF + N], F32, name="g_shared", align_bytes=64)
-        nc.scalar.copy(out=after_g[:, :HALF], in_=early[:, HALF:])
-        scatter(1, after_g[:, :HALF], HALVES[0])
+        quantize_g(1, 1)
+        early = product(1, padded_first_half, "product0")
+        dw_early = copy_out(early[:, HALF:], HALF, "staging")
+        scatter(1, dw_early, HALVES[0])
+        m_second[1] = half_tile("g_grouped10")
         finish(0, HALF)
-        m_grouped[1, 1] = after_g[:, HALF:].bitcast(BF16)
-        for lo in (0, P):
-            cast_m("scalar", 1, 1, lo, lo + P)
-        quantize_m(1, 1, "m_codes11")
+        cast_m("scalar", 1, HALVES[1], m_second[1])
+        quantize_m(1, HALVES[1], m_second[1])
         finish(1, HALF)
         finish(2, 0)
         finish(3, 0)

@@ -27,7 +27,9 @@ LIST_ROWS = 16
 HALF = N // 2
 HALVES = [slice(0, HALF), slice(HALF, N)]
 V_SCALAR_SHARE = (128, 96)
-FIRST_LATE_TILE = 6
+LATE_TILE = 7
+X_SCALAR_SHARE = 48
+M_EARLY_COLUMNS = 128
 SCORE_BANKS = 6
 
 
@@ -85,10 +87,10 @@ def tile_attend_gds_kl_kernel(tc, xT, wT, vT, wt, xm, offs, out):
             copier(engine)(out=grouped[:, lo:hi, :].rearrange("p (c i) j -> p c j i", i=PACK),
                            in_=planes[:, :, lo:hi].rearrange("p j (c i) -> p c j i", i=PACK))
 
-        def cast_x(g, half, engine):
+        def cast_x(g, half, engine, lo=0, hi=P):
             tiles = slice(2 * half, 2 * half + 2)
-            copier(engine)(out=x_ops[g][0][:].rearrange("p (t m) j -> p m j t", t=PACK)[:, :, :, tiles],
-                           in_=x_raw[g][:].rearrange("p j (m t) -> p m j t", t=PACK)[:, :, :, tiles])
+            copier(engine)(out=x_ops[g][0][:].rearrange("p (t m) j -> p m j t", t=PACK)[:, lo:hi, :, tiles],
+                           in_=x_raw[g][:].rearrange("p j (m t) -> p m j t", t=PACK)[:, lo:hi, :, tiles])
 
         w_op = operand("w", "staging")
         nc.scalar.dma_start(out=weight_rows[:ROW_PASSES, :], in_=wt[0].rearrange("(g r) o -> g (r o)", g=ROW_PASSES))
@@ -129,36 +131,38 @@ def tile_attend_gds_kl_kernel(tc, xT, wT, vT, wt, xm, offs, out):
 
         def exps(name, acc, n, neg_max, total):
             nc.vector.tensor_reduce(out=neg_max, in_=acc[:], axis=AXIS_X, op=ALU.max, negate=True)
-            result = held.tile([P, N], F32, name="exp_%s%d" % (name, n), align_bytes=64)
+            result = held.tile([P, N], F32, name="exp_%s%d" % (name, n), align_bytes=64) if name + str(n) != "s0" else raw.tile([P, N], F32, name="x1")
             nc.scalar.activation(result[:], acc[:], ACT.Exp, bias=neg_max, accum_out=total)
             return result
 
         v_listed = held.tile([P, PACK, N], F32, name="v_listed")
         s_max, s_sum, s_inv = stats("s_max"), stats("s_sum"), stats("s_inv")
         t_max, t_sum, t_inv, t_fac = stats("t_max"), stats("t_sum"), stats("t_inv"), stats("t_fac")
-        student, teacher = {}, {}
+        student, teacher, m_grouped = {}, {}, {}
 
         def student_exps(tiles):
             for n in tiles:
                 student[n] = exps("s", scores(w_op, n, student_bank(n)), n, s_max[:, n:n + 1], s_sum[:, n:n + 1])
 
-        def scale_student(tiles):
-            cols = slice(tiles[0], tiles[-1] + 1)
+        def scale_student(tiles, also=0):
+            cols = slice(tiles[0], tiles[-1] + 1 + also)
             nc.vector.reciprocal(s_inv[:, cols], s_sum[:, cols])
             for n in tiles:
                 nc.gpsimd.tensor_scalar(out=student[n][:], in0=student[n][:], scalar1=s_inv[:, n:n + 1],
                                         scalar2=weight_cols[:, n:n + 1], op0=ALU.mult, op1=ALU.mult)
 
-        def teacher_inverses(cols):
-            nc.vector.reciprocal(t_inv[:, cols], t_sum[:, cols])
-
         def teacher_factors(cols):
+            nc.vector.reciprocal(t_inv[:, cols], t_sum[:, cols])
             nc.vector.scalar_tensor_tensor(out=t_fac[:, cols], in0=t_inv[:, cols], scalar=-1.0,
                                            in1=weight_cols[:, cols], op0=ALU.mult, op1=ALU.mult)
 
         def gather_v(j, slots):
             nc.vector.tensor_copy(v_listed[:, j, slots], v_planes[j][:].indirect(listed(slots)))
 
+        g_grouped = {(g, h): held.tile([P, HALF * PACK], BF16, name="g_grouped%d%d" % (g, h), align_bytes=64)[:]
+                     for g, h in ((0, 0), (0, 1), (1, 1))}
+        g_shared = held.tile([P, HALF * (PACK + 1)], BF16, name="g_shared", align_bytes=64)
+        g_grouped[1, 0] = g_shared[:, HALF:]
         g_codes = [held.tile([P, HALF + N], U32, name="g%d_codes" % g, align_bytes=64) for g in range(ROW_PASSES)]
         g_scales = [held.tile([P, HALF + N], U8, name="g%d_scales" % g, align_bytes=64) for g in range(ROW_PASSES)]
         for g in range(ROW_PASSES):
@@ -166,52 +170,50 @@ def tile_attend_gds_kl_kernel(tc, xT, wT, vT, wt, xm, offs, out):
             nc.gpsimd.memset(g_scales[g][:, :HALF].bitcast(U32), 0)
         padded_first_half = slice(0, N)
         all_slots = slice(HALF, HALF + N)
-        g_grouped, g_planes = {}, {}
-        m_codes = [held.tile([P, D], U32, name="m_codes%d" % g, align_bytes=64) for g in range(ROW_PASSES)]
+        g_planes = {(g, h): held.tile([P, PACK, HALF], BF16, name="g_planes%d%d" % (g, h), align_bytes=64)
+                    for g, h in ((0, 0), (0, 1))}
+        m_shared = held.tile([P, (M_EARLY_COLUMNS + HALF) * PACK], BF16, name="m_shared", align_bytes=64)
+        g_planes[1, 0] = m_shared[:, M_EARLY_COLUMNS * PACK:].rearrange("p (j c) -> p j c", j=PACK)
+        m_grouped[0, 1] = m_shared[:, :HALF * PACK]
+        g_planes[1, 1] = g_shared[:, :HALF * PACK].rearrange("p (j c) -> p j c", j=PACK)
+        m_codes = {}
         m_scales = held.tile([P, ROW_PASSES, D], U8, name="m_scales", align_bytes=64)
 
-        def half_tile(name):
-            tile = held.tile([P, HALF * PACK], BF16, name=name, align_bytes=64)
-            return tile[:]
-
-        def as_planes(flat):
-            return flat.rearrange("p (j c) -> p j c", j=PACK)
-
-        def as_grouped(flat):
-            return flat.rearrange("p (c j) -> p c j", j=PACK)
-
-        def cast_m(engine, g, cols, target):
-            planes = m_raw[g][:, :, cols]
+        def cast_m(engine, g, h, lo, hi):
+            planes = m_raw[g][:, :, HALVES[h]]
+            target = m_grouped[g, h].rearrange("p (m j) -> p m j", j=PACK)
             if engine == "gpsimd":
-                nc.gpsimd.tensor_copy(out=as_grouped(target), in_=planes.rearrange("p j m -> p m j"))
+                nc.gpsimd.tensor_copy(out=target[:, lo:hi, :], in_=planes[:, :, lo:hi].rearrange("p j m -> p m j"))
             else:
-                interleave(engine, as_grouped(target), planes, 0, cols.stop - cols.start)
+                interleave(engine, target, planes, lo, hi)
 
-        def quantize_m(g, cols, source):
-            nc.vector.quantize_mx(out=m_codes[g][:, cols].bitcast(E4M3), scales=m_scales[:, g, cols], in_=source)
+        def quantize_m(g, h, name):
+            m_codes[g, h] = held.tile([P, HALF], U32, name=name, align_bytes=64)
+            nc.vector.quantize_mx(out=m_codes[g, h][:].bitcast(E4M3), scales=m_scales[:, g, HALVES[h]],
+                                  in_=m_grouped[g, h])
 
-        def combine(g, h, planes=range(PACK)):
-            for t in planes:
+        def combine(g, h):
+            for t in range(PACK):
                 n = g * PACK + t
                 nc.vector.scalar_tensor_tensor(out=g_planes[g, h][:, t, :], in0=teacher[n][:, HALVES[h]],
                                                scalar=t_fac[:, n:n + 1], in1=student[n][:, HALVES[h]],
                                                op0=ALU.mult, op1=ALU.add)
 
-        def interleave_g(g, h, engine="scalar", lo=0, hi=HALF):
-            interleave(engine, as_grouped(g_grouped[g, h]), g_planes[g, h], lo, hi)
+        def interleave_g(g, h):
+            interleave("scalar", g_grouped[g, h].rearrange("p (c j) -> p c j", j=PACK), g_planes[g, h], 0, HALF)
 
         def quantize_g(g, h):
             cols = slice((h + 1) * HALF, (h + 2) * HALF)
             nc.vector.quantize_mx(out=g_codes[g][:, cols].bitcast(E5M2), scales=g_scales[g][:, cols],
                                   in_=g_grouped[g, h])
 
-        def product(c, cols, bank, passes=(0, 1)):
-            acc = psum.tile([P, N], F32, name=bank)
+        def product(c, cols, bank):
+            acc = psum.tile([P, N], F32, name="product%d" % bank)
             block = slice(c * P, (c + 1) * P)
-            for g in passes:
-                nc.tensor.matmul_mx(out=acc[:], lhsT=m_codes[g][:, block].bitcast(E4M3), lhsT_scale=m_scales[:, g, block],
+            for g in range(ROW_PASSES):
+                nc.tensor.matmul_mx(out=acc[:], lhsT=m_codes[g, c // 2][:, c % 2 * P:(c % 2 + 1) * P].bitcast(E4M3), lhsT_scale=m_scales[:, g, block],
                                     rhs=g_codes[g][:, cols].bitcast(E5M2), rhs_scale=g_scales[g][:, cols],
-                                    start=g == passes[0], stop=g == passes[-1])
+                                    start=g == 0, stop=g == ROW_PASSES - 1)
             return acc
 
         def copy_out(source, width, name):
@@ -223,14 +225,16 @@ def tile_attend_gds_kl_kernel(tc, xT, wT, vT, wt, xm, offs, out):
             nc.vector.tensor_copy(windows[c][:].indirect(listed(slots)), dw)
 
         def finish(c, first_slot):
-            acc = product(c, all_slots, "product%d" % ((c + 1) % 2))
+            acc = product(c, all_slots, (c + 1) % 2)
             scatter(c, copy_out(acc[:, first_slot:], N - first_slot, "dw%d" % c), slice(first_slot, N))
             nc.sync.dma_start(out=out[c * P:(c + 1) * P, :], in_=windows[c][:])
 
         x_ops.append(operand("x0", "x_grouped"))
-        cast_x(0, 0, "vector")
-        cast_x(0, 1, "scalar")
-        for cols in HALVES:
+        cast_x(0, 0, "scalar", 0, X_SCALAR_SHARE)
+        cast_x(0, 0, "vector", X_SCALAR_SHARE, P)
+        cast_x(0, 1, "scalar", 0, P - X_SCALAR_SHARE)
+        cast_x(0, 1, "vector", P - X_SCALAR_SHARE, P)
+        for cols in (slice(0, P), slice(P, HALF), HALVES[1]):
             quantize_e4m3(x_ops[0], cols)
         weight = raw.tile([P, ROW_PASSES, PACK], F32, name="x0")
         nc.scalar.copy(out=weight[:], in_=turned[:, :, :ROW_PASSES].rearrange("p t g -> p g t"))
@@ -240,7 +244,8 @@ def tile_attend_gds_kl_kernel(tc, xT, wT, vT, wt, xm, offs, out):
         cast_x(1, 0, "scalar")
         cast_x(1, 1, "scalar")
         student_exps([0, 1, 2, 3])
-        quantize_e4m3(x_ops[1], slice(0, K_PASS))
+        for cols in HALVES:
+            quantize_e4m3(x_ops[1], cols)
         v_staging = held.tile([P, N * PACK], BF16, name="staging", align_bytes=64)
         v_op = (v_staging[:].rearrange("p (c j) -> p c j", j=PACK),
                 held.tile([P, K_PASS], U32, name="v_codes", align_bytes=64),
@@ -249,15 +254,17 @@ def tile_attend_gds_kl_kernel(tc, xT, wT, vT, wt, xm, offs, out):
         scale_student([0, 1])
         student_exps([4, 5])
         scale_student([2, 3])
-        student_exps([6, 7])
-        scale_student([4, 5])
+        student_exps([6])
+        late_scores = scores(w_op, LATE_TILE, student_bank(LATE_TILE))
         gather_v(1, slice(0, N))
-        late = slice(FIRST_LATE_TILE, ROW_TILES)
-        nc.vector.reciprocal(s_inv[:, late], s_sum[:, late])
+        scalar_tiles = [5, 6]
+        scale_student([4], also=len(scalar_tiles))
         gather_v(2, slice(0, N))
         s_fac = stats("s_fac")
-        for n in range(FIRST_LATE_TILE, ROW_TILES):
+        for n in scalar_tiles:
             nc.scalar.activation(s_fac[:, n:n + 1], s_inv[:, n:n + 1], ACT.Copy, scale=weight_cols[:, n:n + 1])
+        for n in scalar_tiles:
+            nc.scalar.activation(student[n][:], student[n][:], ACT.Copy, scale=s_fac[:, n:n + 1])
 
         for slots in HALVES:
             gather_v(PACK - 1, slots)
@@ -266,68 +273,58 @@ def tile_attend_gds_kl_kernel(tc, xT, wT, vT, wt, xm, offs, out):
             interleave("vector", v_op[0], v_listed, slots.start + share, slots.stop)
         for slots in HALVES:
             quantize_e4m3(v_op, slots)
-        scaled_late = held.tile([P, (ROW_TILES - FIRST_LATE_TILE) * N], F32, name="v_listed")
-        for n in range(FIRST_LATE_TILE, ROW_TILES):
-            target = scaled_late[:, (n - FIRST_LATE_TILE) * N:(n - FIRST_LATE_TILE + 1) * N]
-            nc.scalar.activation(target, student[n][:], ACT.Copy, scale=s_fac[:, n:n + 1])
-            student[n] = target
+        late_max = v_staging[:, HALF * PACK - 2:HALF * PACK].bitcast(F32)
+        student[LATE_TILE] = exps("s", late_scores, LATE_TILE, late_max, s_sum[:, LATE_TILE:])
         m_raw = [load(m_rows[g], [P, PACK, D], "w%d" % (g + 2)) for g in range(ROW_PASSES)]
 
-        m_first = held.tile([P, 2 * HALF * PACK], BF16, name="staging", align_bytes=64)
-        m_second = [half_tile("m_second0"), None]
-        first = [m_first[:, g * HALF * PACK:(g + 1) * HALF * PACK] for g in range(ROW_PASSES)]
-        for g in range(ROW_PASSES):
-            cast_m("gpsimd", g, HALVES[0], first[g])
-        cast_m("scalar", 0, HALVES[1], m_second[0])
+        m_grouped[0, 0] = v_staging[:, HALF * PACK:]
+        m_grouped[1, 0] = held.tile([P, HALF * PACK], BF16, name="m_grouped", align_bytes=64)[:]
+        cast_m("gpsimd", 0, 0, 0, HALF)
+        cast_m("gpsimd", 1, 0, 0, HALF)
+        cast_m("scalar", 0, 1, 0, M_EARLY_COLUMNS)
 
         def teacher_exps(tiles):
             for n in tiles:
-                acc = scores(v_op, n, (n + 2) % SCORE_BANKS, HALVES if n == 0 else (slice(0, N),))
-                teacher[n] = exps("t", acc, n, t_max[:, n:n + 1], t_sum[:, n:n + 1])
+                teacher[n] = exps("t", scores(v_op, n, (n + 2) % SCORE_BANKS, HALVES if n == 0 else (slice(0, N),)), n, t_max[:, n:n + 1], t_sum[:, n:n + 1])
 
-        teacher_exps([0, 1, 2, 3, 4, 5, 6])
-        teacher_inverses(slice(0, PACK))
-        teacher_exps([7])
+        teacher_exps([0, 1, 2, 3])
+        scale_student([LATE_TILE])
+        teacher_exps([4, 5])
         teacher_factors(slice(0, PACK))
-        quantize_m(0, HALVES[0], first[0])
-        for g in range(ROW_PASSES):
-            g_planes[g, 0] = as_planes(half_tile("g_planes%d0" % g))
-            g_grouped[g, 0] = half_tile("g_grouped%d0" % g)
-        pair = [slice(PACK, PACK + 2), slice(PACK + 2, ROW_TILES)]
-        teacher_inverses(pair[0])
-        combine(0, 0, [0])
-        teacher_factors(pair[0])
-        combine(0, 0, [1, 2, 3])
+        teacher_exps([6, 7])
+        quantize_m(0, 0, "m_codes00")
+
+        teacher_factors(slice(PACK, ROW_TILES - 1))
+        combine(0, 0)
         interleave_g(0, 0)
-        teacher_inverses(pair[1])
-        combine(1, 0, [0])
-        teacher_factors(pair[1])
-        combine(1, 0, [1, 2, 3])
+        teacher_factors(slice(ROW_TILES - 1, ROW_TILES))
+        combine(1, 0)
         interleave_g(1, 0)
-        g_planes[0, 1] = as_planes(half_tile("g_planes01"))
         quantize_g(1, 0)
         combine(0, 1)
         quantize_g(0, 0)
-        quantize_m(1, HALVES[0], first[1])
-        early = product(0, padded_first_half, "product0")
-        dw_early = copy_out(early[:, HALF:], HALF, "dw_early0")
-        g_grouped[0, 1] = half_tile("g_grouped00")
+        quantize_m(1, 0, "m_codes10")
+
+        early = product(0, padded_first_half, 0)
         interleave_g(0, 1)
-        g_planes[1, 1] = as_planes(half_tile("staging"))
+        cast_m("scalar", 0, 1, M_EARLY_COLUMNS, HALF)
+        dw_early = copy_out(early[:, HALF:], HALF, "dw_early")
         combine(1, 1)
-        quantize_m(0, HALVES[1], m_second[0])
-        g_grouped[1, 1] = half_tile("g_grouped10")
         interleave_g(1, 1)
         quantize_g(0, 1)
-        scatter(0, dw_early, HALVES[0])
+        quantize_m(0, 1, "exp_s7")
         quantize_g(1, 1)
-        early = product(1, padded_first_half, "product0")
-        dw_early = copy_out(early[:, HALF:], HALF, "staging")
-        scatter(1, dw_early, HALVES[0])
-        m_second[1] = half_tile("g_grouped10")
+        scatter(0, dw_early, HALVES[0])
+
+        early = product(1, padded_first_half, 0)
+        after_g = held.tile([P, HALF + N], F32, name="g_shared", align_bytes=64)
+        nc.scalar.copy(out=after_g[:, :HALF], in_=early[:, HALF:])
+        scatter(1, after_g[:, :HALF], HALVES[0])
         finish(0, HALF)
-        cast_m("scalar", 1, HALVES[1], m_second[1])
-        quantize_m(1, HALVES[1], m_second[1])
+        m_grouped[1, 1] = after_g[:, HALF:].bitcast(BF16)
+        for lo in (0, P):
+            cast_m("scalar", 1, 1, lo, lo + P)
+        quantize_m(1, 1, "m_codes11")
         finish(1, HALF)
         finish(2, 0)
         finish(3, 0)

@@ -172,8 +172,8 @@ def tile_attend_gds_kl_kernel(tc, xT, wT, vT, wt, xm, offs, out):
         all_slots = slice(HALF, HALF + N)
         g_planes = {(g, h): held.tile([P, PACK, HALF], BF16, name="g_planes%d%d" % (g, h), align_bytes=64)
                     for g, h in ((0, 0), (0, 1))}
-        m_shared = held.tile([P, (M_EARLY_COLUMNS + HALF) * PACK], BF16, name="m_shared", align_bytes=64)
-        g_planes[1, 0] = m_shared[:, M_EARLY_COLUMNS * PACK:].rearrange("p (j c) -> p j c", j=PACK)
+        m_shared = held.tile([P, 2 * HALF * PACK], BF16, name="m_shared", align_bytes=64)
+        g_planes[1, 0] = m_shared[:, HALF * PACK:].rearrange("p (j c) -> p j c", j=PACK)
         m_grouped[0, 1] = m_shared[:, :HALF * PACK]
         g_planes[1, 1] = g_shared[:, :HALF * PACK].rearrange("p (j c) -> p j c", j=PACK)
         m_codes = {}
@@ -196,7 +196,8 @@ def tile_attend_gds_kl_kernel(tc, xT, wT, vT, wt, xm, offs, out):
             for t in range(PACK):
                 n = g * PACK + t
                 nc.vector.scalar_tensor_tensor(out=g_planes[g, h][:, t, :], in0=teacher[n][:, HALVES[h]],
-                                               scalar=t_fac[:, n:n + 1], in1=student[n][:, HALVES[h]],
+                                               scalar=t_fac[:, n:n + 1],
+                                               in1=late_halves[:, h, :] if n == LATE_TILE else student[n][:, HALVES[h]],
                                                op0=ALU.mult, op1=ALU.add)
 
         def interleave_g(g, h):
@@ -283,15 +284,23 @@ def tile_attend_gds_kl_kernel(tc, xT, wT, vT, wt, xm, offs, out):
         cast_m("gpsimd", 1, 0, 0, HALF)
         cast_m("scalar", 0, 1, 0, M_EARLY_COLUMNS)
 
+        last_max = m_shared[:, HALF * PACK - 2:HALF * PACK].bitcast(F32)
+
         def teacher_exps(tiles):
             for n in tiles:
-                teacher[n] = exps("t", scores(v_op, n, (n + 2) % SCORE_BANKS, HALVES if n == 0 else (slice(0, N),)), n, t_max[:, n:n + 1], t_sum[:, n:n + 1])
+                teacher[n] = exps("t", scores(v_op, n, (n + 2) % SCORE_BANKS, HALVES if n == 0 else (slice(0, N),)), n,
+                                  last_max if n == ROW_TILES - 1 else t_max[:, n:n + 1], t_sum[:, n:n + 1])
 
         teacher_exps([0, 1, 2, 3])
-        scale_student([LATE_TILE])
+        late = slice(LATE_TILE, ROW_TILES)
+        nc.vector.reciprocal(s_inv[:, late], s_sum[:, late])
+        late_halves = m_raw[1][:, :2, HALVES[0]]
+        nc.gpsimd.tensor_scalar(out=late_halves, in0=student[LATE_TILE][:].rearrange("p (h c) -> p h c", h=2),
+                                scalar1=s_inv[:, late], scalar2=weight_cols[:, late], op0=ALU.mult, op1=ALU.mult)
         teacher_exps([4, 5])
         teacher_factors(slice(0, PACK))
         teacher_exps([6, 7])
+        cast_m("scalar", 0, 1, M_EARLY_COLUMNS, HALF)
         quantize_m(0, 0, "m_codes00")
 
         teacher_factors(slice(PACK, ROW_TILES - 1))
@@ -307,12 +316,11 @@ def tile_attend_gds_kl_kernel(tc, xT, wT, vT, wt, xm, offs, out):
 
         early = product(0, padded_first_half, 0)
         interleave_g(0, 1)
-        cast_m("scalar", 0, 1, M_EARLY_COLUMNS, HALF)
         dw_early = copy_out(early[:, HALF:], HALF, "dw_early")
         combine(1, 1)
         interleave_g(1, 1)
         quantize_g(0, 1)
-        quantize_m(0, 1, "exp_s7")
+        quantize_m(0, 1, "exp_s6")
         quantize_g(1, 1)
         scatter(0, dw_early, HALVES[0])
 

@@ -30,6 +30,7 @@ V_SCALAR_SHARE = (128, 96)
 LATE_TILE = 7
 X_SCALAR_SHARE = 48
 M_EARLY_COLUMNS = 128
+G_SCALAR_SHARE = 224
 SCORE_BANKS = 6
 
 
@@ -200,8 +201,8 @@ def tile_attend_gds_kl_kernel(tc, xT, wT, vT, wt, xm, offs, out):
                                                in1=late_halves[:, h, :] if n == LATE_TILE else student[n][:, HALVES[h]],
                                                op0=ALU.mult, op1=ALU.add)
 
-        def interleave_g(g, h):
-            interleave("scalar", g_grouped[g, h].rearrange("p (c j) -> p c j", j=PACK), g_planes[g, h], 0, HALF)
+        def interleave_g(g, h, engine="scalar", lo=0, hi=HALF):
+            interleave(engine, g_grouped[g, h].rearrange("p (c j) -> p c j", j=PACK), g_planes[g, h], lo, hi)
 
         def quantize_g(g, h):
             cols = slice((h + 1) * HALF, (h + 2) * HALF)
@@ -228,7 +229,11 @@ def tile_attend_gds_kl_kernel(tc, xT, wT, vT, wt, xm, offs, out):
         def finish(c, first_slot):
             acc = product(c, all_slots, (c + 1) % 2)
             scatter(c, copy_out(acc[:, first_slot:], N - first_slot, "dw%d" % c), slice(first_slot, N))
-            nc.sync.dma_start(out=out[c * P:(c + 1) * P, :], in_=windows[c][:])
+            if c < len(windows) - 1:
+                nc.sync.dma_start(out=out[c * P:(c + 1) * P, :], in_=windows[c][:])
+                return
+            for queue, cols in ((nc.sync, slice(0, T // 2)), (nc.scalar, slice(T // 2, T))):
+                queue.dma_start(out=out[c * P:(c + 1) * P, cols], in_=windows[c][:, cols])
 
         x_ops.append(operand("x0", "x_grouped"))
         cast_x(0, 0, "scalar", 0, X_SCALAR_SHARE)
@@ -308,7 +313,8 @@ def tile_attend_gds_kl_kernel(tc, xT, wT, vT, wt, xm, offs, out):
         interleave_g(0, 0)
         teacher_factors(slice(ROW_TILES - 1, ROW_TILES))
         combine(1, 0)
-        interleave_g(1, 0)
+        interleave_g(1, 0, "scalar", 0, G_SCALAR_SHARE)
+        interleave_g(1, 0, "vector", G_SCALAR_SHARE, HALF)
         quantize_g(1, 0)
         combine(0, 1)
         quantize_g(0, 0)

@@ -39,6 +39,7 @@ def tile_attend_gds_kl_kernel(tc, xT, wT, vT, wt, xm, offs, out):
     with ExitStack() as ctx:
         held = ctx.enter_context(tc.tile_pool(name="held", bufs=1))
         raw = ctx.enter_context(tc.tile_pool(name="raw", bufs=1))
+        placed = ctx.enter_context(tc.tile_pool(name="placed", bufs=1))
         psum = ctx.enter_context(tc.psum_pool(name="psum", bufs=1))
 
         offsets = held.tile([P, N // LIST_ROWS], U16, name="offsets")
@@ -138,7 +139,8 @@ def tile_attend_gds_kl_kernel(tc, xT, wT, vT, wt, xm, offs, out):
 
         v_listed = held.tile([P, PACK, N], F32, name="v_listed")
         s_max, s_sum, s_inv = stats("s_max"), stats("s_sum"), stats("s_inv")
-        t_max, t_sum, t_inv, t_fac = stats("t_max"), stats("t_sum"), stats("t_inv"), stats("t_fac")
+        t_max, t_inv, t_fac = stats("t_max"), stats("t_inv"), stats("t_fac")
+        t_sum = placed.tile([P, ROW_TILES], F32, name="t_sum", align_bytes=64, offset=0)
         student, teacher, m_grouped = {}, {}, {}
 
         def student_exps(tiles):
@@ -171,8 +173,8 @@ def tile_attend_gds_kl_kernel(tc, xT, wT, vT, wt, xm, offs, out):
             nc.gpsimd.memset(g_scales[g][:, :HALF].bitcast(U32), 0)
         padded_first_half = slice(0, N)
         all_slots = slice(HALF, HALF + N)
-        g_planes = {(g, h): held.tile([P, PACK, HALF], BF16, name="g_planes%d%d" % (g, h), align_bytes=64)
-                    for g, h in ((0, 0), (0, 1))}
+        first_planes = held.tile([P, PACK * HALF], BF16, name="g_planes00", align_bytes=64)
+        g_planes = {(0, 0): first_planes[:].rearrange("p (j c) -> p j c", j=PACK)}
         m_shared = held.tile([P, 2 * HALF * PACK], BF16, name="m_shared", align_bytes=64)
         g_planes[1, 0] = m_shared[:, HALF * PACK:].rearrange("p (j c) -> p j c", j=PACK)
         m_grouped[0, 1] = m_shared[:, :HALF * PACK]
@@ -193,8 +195,8 @@ def tile_attend_gds_kl_kernel(tc, xT, wT, vT, wt, xm, offs, out):
             nc.vector.quantize_mx(out=m_codes[g, h][:].bitcast(E4M3), scales=m_scales[:, g, HALVES[h]],
                                   in_=m_grouped[g, h])
 
-        def combine(g, h):
-            for t in range(PACK):
+        def combine(g, h, places=range(PACK)):
+            for t in places:
                 n = g * PACK + t
                 nc.vector.scalar_tensor_tensor(out=g_planes[g, h][:, t, :], in0=teacher[n][:, HALVES[h]],
                                                scalar=t_fac[:, n:n + 1],
@@ -289,12 +291,13 @@ def tile_attend_gds_kl_kernel(tc, xT, wT, vT, wt, xm, offs, out):
         cast_m("gpsimd", 1, 0, 0, HALF)
         cast_m("scalar", 0, 1, 0, M_EARLY_COLUMNS)
 
-        last_max = m_shared[:, HALF * PACK - 2:HALF * PACK].bitcast(F32)
+        held_max = {ROW_TILES - 2: m_shared[:, HALF * PACK - 2:HALF * PACK].bitcast(F32),
+                    ROW_TILES - 1: first_planes[:, HALF * PACK - 2:].bitcast(F32)}
 
         def teacher_exps(tiles):
             for n in tiles:
                 teacher[n] = exps("t", scores(v_op, n, (n + 2) % SCORE_BANKS, HALVES if n == 0 else (slice(0, N),)), n,
-                                  last_max if n == ROW_TILES - 1 else t_max[:, n:n + 1], t_sum[:, n:n + 1])
+                                  held_max.get(n, t_max[:, n:n + 1]), t_sum[:, n:n + 1])
 
         teacher_exps([0, 1, 2, 3])
         late = slice(LATE_TILE, ROW_TILES)
@@ -308,14 +311,18 @@ def tile_attend_gds_kl_kernel(tc, xT, wT, vT, wt, xm, offs, out):
         cast_m("scalar", 0, 1, M_EARLY_COLUMNS, HALF)
         quantize_m(0, 0, "m_codes00")
 
-        teacher_factors(slice(PACK, ROW_TILES - 1))
-        combine(0, 0)
+        combine(0, 0, range(PACK - 1))
+        second = slice(PACK, ROW_TILES)
+        nc.vector.reciprocal(t_inv[:, second], t_sum[:, second])
+        combine(0, 0, [PACK - 1])
         interleave_g(0, 0)
-        teacher_factors(slice(ROW_TILES - 1, ROW_TILES))
+        nc.vector.scalar_tensor_tensor(out=t_fac[:, second], in0=t_inv[:, second], scalar=-1.0,
+                                       in1=weight_cols[:, second], op0=ALU.mult, op1=ALU.mult)
         combine(1, 0)
         interleave_g(1, 0, "scalar", 0, G_SCALAR_SHARE)
         interleave_g(1, 0, "vector", G_SCALAR_SHARE, HALF)
         quantize_g(1, 0)
+        g_planes[0, 1] = placed.tile([P, PACK, HALF], BF16, name="g_planes01", align_bytes=64, offset=0)
         combine(0, 1)
         quantize_g(0, 0)
         quantize_m(1, 0, "m_codes10")

@@ -57,9 +57,10 @@ def tile_attend_gds_kl_kernel(tc, xT, wT, vT, wt, xm, offs, out):
         x_rows = xT[0].rearrange("(p j) r -> p j r", j=PACK)
         m_rows = xm[0].rearrange("(g p j) d -> g p j d", p=P, j=PACK)
 
+        first_plane = load(w_rows[:, 0, :], [P, T], "w0")
         nc.sync.dma_start(offsets[:], offs)
-        first_plane = raw.tile([P, T], F32, name="w0")
-        nc.scalar.dma_start(out=first_plane[:], in_=w_rows[:, 0, :])
+        second_plane = raw.tile([P, T], F32, name="w1")
+        nc.scalar.dma_start(out=second_plane[:], in_=w_rows[:, 1, :])
 
         weight_rows = held.tile([P, K_PASS], F32, name="weight_rows")
         nc.gpsimd.memset(weight_rows[:], 0.0)
@@ -96,7 +97,7 @@ def tile_attend_gds_kl_kernel(tc, xT, wT, vT, wt, xm, offs, out):
 
         w_op = operand("w", "staging")
         nc.scalar.dma_start(out=weight_rows[:ROW_PASSES, :], in_=wt[0].rearrange("(g r) o -> g (r o)", g=ROW_PASSES))
-        w_planes = [first_plane] + [load(w_rows[:, j, :], [P, T], "w%d" % j) for j in range(1, PACK)]
+        w_planes = [first_plane, second_plane] + [load(w_rows[:, j, :], [P, T], "w%d" % j) for j in range(2, PACK)]
         w_listed = held.tile([P, PACK, N], F32, name="w_listed")
         for j in range(PACK - 1):
             nc.vector.tensor_copy(w_listed[:, j, :], w_planes[j][:].indirect(offsets[:]))

@@ -30,7 +30,7 @@ V_SCALAR_SHARE = (128, 96)
 LATE_TILE = 7
 X_SCALAR_SHARE = 48
 M_EARLY_COLUMNS = 128
-G_SCALAR_SHARE = 224
+G_FIRST_PIECE = 128
 SCORE_BANKS = 6
 
 
@@ -140,8 +140,10 @@ def tile_attend_gds_kl_kernel(tc, xT, wT, vT, wt, xm, offs, out):
 
         v_listed = held.tile([P, PACK, N], F32, name="v_listed")
         s_max, s_sum, s_inv = stats("s_max"), stats("s_sum"), stats("s_inv")
-        t_max, t_inv, t_fac = stats("t_max"), stats("t_inv"), stats("t_fac")
-        t_sum = placed.tile([P, ROW_TILES], F32, name="t_sum", align_bytes=64, offset=0)
+        t_max = stats("t_max")
+        t_inv = held.tile([P, 1 + ROW_TILES], F32, name="t_inv", align_bytes=64)
+        t_fac = held.tile([P, 1 + ROW_TILES], F32, name="t_fac", align_bytes=64)
+        t_sum = placed.tile([P, 1 + ROW_TILES], F32, name="t_sum", align_bytes=64, offset=0)
         student, teacher, m_grouped = {}, {}, {}
 
         def student_exps(tiles):
@@ -158,7 +160,7 @@ def tile_attend_gds_kl_kernel(tc, xT, wT, vT, wt, xm, offs, out):
         def teacher_factors(cols):
             nc.vector.reciprocal(t_inv[:, cols], t_sum[:, cols])
             nc.vector.scalar_tensor_tensor(out=t_fac[:, cols], in0=t_inv[:, cols], scalar=-1.0,
-                                           in1=weight_cols[:, cols], op0=ALU.mult, op1=ALU.mult)
+                                           in1=weight[:, cols], op0=ALU.mult, op1=ALU.mult)
 
         def gather_v(j, slots):
             nc.vector.tensor_copy(v_listed[:, j, slots], v_planes[j][:].indirect(listed(slots)))
@@ -196,13 +198,13 @@ def tile_attend_gds_kl_kernel(tc, xT, wT, vT, wt, xm, offs, out):
             nc.vector.quantize_mx(out=m_codes[g, h][:].bitcast(E4M3), scales=m_scales[:, g, HALVES[h]],
                                   in_=m_grouped[g, h])
 
-        def combine(g, h, places=range(PACK)):
+        def combine(g, h, places=range(PACK), cols=slice(0, HALF)):
             for t in places:
                 n = g * PACK + t
-                nc.vector.scalar_tensor_tensor(out=g_planes[g, h][:, t, :], in0=teacher[n][:, HALVES[h]],
-                                               scalar=t_fac[:, n:n + 1],
-                                               in1=late_halves[:, h, :] if n == LATE_TILE else student[n][:, HALVES[h]],
-                                               op0=ALU.mult, op1=ALU.add)
+                scaled = student[n][:, HALVES[h]]
+                nc.vector.scalar_tensor_tensor(out=g_planes[g, h][:, t, cols], in0=teacher[n][:, HALVES[h]][:, cols],
+                                               scalar=t_fac[:, n + 1:n + 2], in1=scaled[:, cols], op0=ALU.mult,
+                                               op1=ALU.subtract if n == LATE_TILE else ALU.add)
 
         def interleave_g(g, h, engine="scalar", lo=0, hi=HALF):
             interleave(engine, g_grouped[g, h].rearrange("p (c j) -> p c j", j=PACK), g_planes[g, h], lo, hi)
@@ -245,9 +247,11 @@ def tile_attend_gds_kl_kernel(tc, xT, wT, vT, wt, xm, offs, out):
         cast_x(0, 1, "vector", P - X_SCALAR_SHARE, P)
         for cols in (slice(0, P), slice(P, HALF), HALVES[1]):
             quantize_e4m3(x_ops[0], cols)
-        weight = raw.tile([P, ROW_PASSES, PACK], F32, name="x0")
-        nc.scalar.copy(out=weight[:], in_=turned[:, :, :ROW_PASSES].rearrange("p t g -> p g t"))
-        weight_cols = weight[:].rearrange("p g t -> p (g t)")
+        weight = raw.tile([P, 1 + ROW_TILES], F32, name="x0")
+        weight_cols = weight[:, 1:]
+        nc.scalar.copy(out=weight_cols.rearrange("p (g t) -> p g t", t=PACK),
+                       in_=turned[:, :, :ROW_PASSES].rearrange("p t g -> p g t"))
+        nc.scalar.copy(out=weight[:, :1], in_=turned[:, PACK - 1, ROW_PASSES - 1:ROW_PASSES])
 
         x_ops.append(operand("x1", "x_grouped"))
         cast_x(1, 0, "scalar")
@@ -283,7 +287,7 @@ def tile_attend_gds_kl_kernel(tc, xT, wT, vT, wt, xm, offs, out):
         for slots in HALVES:
             quantize_e4m3(v_op, slots)
         late_max = v_staging[:, HALF * PACK - 2:HALF * PACK].bitcast(F32)
-        student[LATE_TILE] = exps("s", late_scores, LATE_TILE, late_max, s_sum[:, LATE_TILE:])
+        student[LATE_TILE] = exps("s", late_scores, LATE_TILE, late_max, t_sum[:, :1])
         m_raw = [load(m_rows[g], [P, PACK, D], "w%d" % (g + 2)) for g in range(ROW_PASSES)]
 
         m_grouped[0, 0] = v_staging[:, HALF * PACK:]
@@ -291,37 +295,32 @@ def tile_attend_gds_kl_kernel(tc, xT, wT, vT, wt, xm, offs, out):
         cast_m("gpsimd", 0, 0, 0, HALF)
         cast_m("gpsimd", 1, 0, 0, HALF)
         cast_m("scalar", 0, 1, 0, M_EARLY_COLUMNS)
+        cast_m("gpsimd", 0, 1, M_EARLY_COLUMNS, HALF)
 
-        held_max = {ROW_TILES - 2: m_shared[:, HALF * PACK - 2:HALF * PACK].bitcast(F32),
-                    ROW_TILES - 1: first_planes[:, HALF * PACK - 2:].bitcast(F32)}
+        held_max = {ROW_TILES - 1: first_planes[:, HALF * PACK - 2:].bitcast(F32)}
 
         def teacher_exps(tiles):
             for n in tiles:
                 teacher[n] = exps("t", scores(v_op, n, (n + 2) % SCORE_BANKS, HALVES if n == 0 else (slice(0, N),)), n,
-                                  held_max.get(n, t_max[:, n:n + 1]), t_sum[:, n:n + 1])
+                                  held_max.get(n, t_max[:, n:n + 1]), t_sum[:, n + 1:n + 2])
 
-        teacher_exps([0, 1, 2, 3])
-        late = slice(LATE_TILE, ROW_TILES)
-        nc.vector.reciprocal(s_inv[:, late], s_sum[:, late])
-        late_halves = m_raw[1][:, :2, HALVES[0]]
-        nc.gpsimd.tensor_scalar(out=late_halves, in0=student[LATE_TILE][:].rearrange("p (h c) -> p h c", h=2),
-                                scalar1=s_inv[:, late], scalar2=weight_cols[:, late], op0=ALU.mult, op1=ALU.mult)
-        teacher_exps([4, 5])
-        teacher_factors(slice(0, PACK))
+        teacher_exps([0, 1, 2, 3, 4, 5])
+        teacher_factors(slice(0, 1 + PACK))
         teacher_exps([6, 7])
-        cast_m("scalar", 0, 1, M_EARLY_COLUMNS, HALF)
+        nc.scalar.activation(student[LATE_TILE][:], student[LATE_TILE][:], ACT.Copy, scale=t_fac[:, :1])
         quantize_m(0, 0, "m_codes00")
 
         combine(0, 0, range(PACK - 1))
-        second = slice(PACK, ROW_TILES)
+        second = slice(1 + PACK, 1 + ROW_TILES)
         nc.vector.reciprocal(t_inv[:, second], t_sum[:, second])
         combine(0, 0, [PACK - 1])
         interleave_g(0, 0)
         nc.vector.scalar_tensor_tensor(out=t_fac[:, second], in0=t_inv[:, second], scalar=-1.0,
-                                       in1=weight_cols[:, second], op0=ALU.mult, op1=ALU.mult)
-        combine(1, 0)
-        interleave_g(1, 0, "scalar", 0, G_SCALAR_SHARE)
-        interleave_g(1, 0, "vector", G_SCALAR_SHARE, HALF)
+                                       in1=weight[:, second], op0=ALU.mult, op1=ALU.mult)
+        combine(1, 0, cols=slice(0, G_FIRST_PIECE))
+        interleave_g(1, 0, "scalar", 0, G_FIRST_PIECE)
+        combine(1, 0, cols=slice(G_FIRST_PIECE, HALF))
+        interleave_g(1, 0, "scalar", G_FIRST_PIECE, HALF)
         quantize_g(1, 0)
         g_planes[0, 1] = placed.tile([P, PACK, HALF], BF16, name="g_planes01", align_bytes=64, offset=0)
         combine(0, 1)

@@ -29,7 +29,6 @@ HALVES = [slice(0, HALF), slice(HALF, N)]
 V_SCALAR_SHARE = (128, 96)
 LATE_TILE = 7
 X_SCALAR_SHARE = 48
-M_EARLY_COLUMNS = 128
 G_FIRST_PIECE = 128
 SCORE_BANKS = 6
 
@@ -293,9 +292,8 @@ def tile_attend_gds_kl_kernel(tc, xT, wT, vT, wt, xm, offs, out):
         m_grouped[0, 0] = v_staging[:, HALF * PACK:]
         m_grouped[1, 0] = held.tile([P, HALF * PACK], BF16, name="m_grouped", align_bytes=64)[:]
         cast_m("gpsimd", 0, 0, 0, HALF)
+        cast_m("gpsimd", 0, 1, 0, HALF)
         cast_m("gpsimd", 1, 0, 0, HALF)
-        cast_m("scalar", 0, 1, 0, M_EARLY_COLUMNS)
-        cast_m("gpsimd", 0, 1, M_EARLY_COLUMNS, HALF)
 
         held_max = {ROW_TILES - 1: first_planes[:, HALF * PACK - 2:].bitcast(F32)}
 

@@ -23,14 +23,14 @@ PACK = 4
 K_PASS = P * PACK
 ROW_PASSES = R // K_PASS
 ROW_TILES = R // P
+BLOCKS = D // P
 LIST_ROWS = 16
 HALF = N // 2
 HALVES = [slice(0, HALF), slice(HALF, N)]
-V_SCALAR_SHARE = (128, 96)
-LATE_TILE = 7
+ALL = slice(0, N)
+TABLE_SCALAR_SHARE = 160
 X_SCALAR_SHARE = 48
-G_FIRST_PIECE = 128
-SCORE_BANKS = 6
+GPSIMD_TILES = 3
 
 
 def tile_attend_gds_kl_kernel(tc, xT, wT, vT, wt, xm, offs, out):
@@ -46,304 +46,289 @@ def tile_attend_gds_kl_kernel(tc, xT, wT, vT, wt, xm, offs, out):
         def listed(slots):
             return offsets[:, slots.start // LIST_ROWS:slots.stop // LIST_ROWS]
 
-        def load(source, shape, name):
+        def load(source, shape, name, queue=nc.sync):
             tile = raw.tile(shape, F32, name=name)
-            nc.sync.dma_start(out=tile[:], in_=source)
+            queue.dma_start(out=tile[:], in_=source)
             return tile
+
+        def keep(shape, dtype, name):
+            return held.tile(shape, dtype, name=name, align_bytes=64)
 
         w_rows = wT.rearrange("(p j) t -> p j t", j=PACK)
         v_rows = vT.rearrange("(p j) t -> p j t", j=PACK)
         x_rows = xT[0].rearrange("(p j) r -> p j r", j=PACK)
         m_rows = xm[0].rearrange("(g p j) d -> g p j d", p=P, j=PACK)
 
-        first_plane = load(w_rows[:, 0, :], [P, T], "w0")
+        w_planes = [load(w_rows[:, 0, :], [P, T], "w0")]
         nc.sync.dma_start(offsets[:], offs)
-        second_plane = raw.tile([P, T], F32, name="w1")
-        nc.scalar.dma_start(out=second_plane[:], in_=w_rows[:, 1, :])
+        w_planes.append(load(w_rows[:, 1, :], [P, T], "w1", nc.scalar))
 
         weight_rows = held.tile([P, K_PASS], F32, name="weight_rows")
         nc.gpsimd.memset(weight_rows[:], 0.0)
         identity = held.tile([P, P], F32, name="identity")
         make_identity(nc, identity[:])
+        nc.scalar.dma_start(out=weight_rows[:ROW_PASSES, :], in_=wt[0].rearrange("(g r) o -> g (r o)", g=ROW_PASSES))
 
-        windows = [held.tile([P, T], F32, name="window%d" % c) for c in range(D // P)]
+        windows = [held.tile([P, T], F32, name="window%d" % c) for c in range(BLOCKS)]
         for c, window in enumerate(windows):
-            engine = nc.vector if c < len(windows) // 2 else nc.gpsimd
+            engine = nc.vector if c < BLOCKS // 2 else nc.gpsimd
             engine.memset(window[:].bitcast(I32), 0)
 
-        def operand(name, staging):
-            grouped = held.tile([P, K_PASS, PACK], BF16, name=staging, align_bytes=64)
-            codes = held.tile([P, K_PASS], U32, name=name + "_codes", align_bytes=64)
-            scales = held.tile([P, K_PASS], U8, name=name + "_scales", align_bytes=64)
-            return grouped, codes, scales
-
-        def quantize_e4m3(op, cols):
-            grouped, codes, scales = op
-            nc.vector.quantize_mx(out=codes[:, cols].bitcast(E4M3), scales=scales[:, cols],
-                                  in_=grouped[:, cols, :].rearrange("p c j -> p (c j)"))
+        w_planes.extend(load(w_rows[:, j, :], [P, T], "w%d" % j) for j in range(2, PACK))
+        x_raw = [load(x_rows[:, :, g * K_PASS:(g + 1) * K_PASS], [P, PACK, K_PASS], "x%d" % g)
+                 for g in range(ROW_PASSES)]
+        v_planes = [load(v_rows[:, j, :], [P, T], "v%d" % j) for j in range(PACK)]
 
         def copier(engine):
             return nc.vector.tensor_copy if engine == "vector" else nc.scalar.copy
 
+        def indirect_copy(engine, target, source):
+            if engine == "vector":
+                nc.vector.tensor_copy(target, source)
+            else:
+                nc.scalar.activation(target, source, ACT.Copy)
+
+        def gather(engine, picked, planes, j, slots):
+            indirect_copy(engine, picked[:, j, slots], planes[j][:].indirect(listed(slots)))
+
+        def walk(planes):
+            return planes.rearrange("p j (c i) -> p c j i", i=PACK)
+
+        def woven(grouped):
+            return grouped.rearrange("p (c i) j -> p c j i", i=PACK)
+
         def interleave(engine, grouped, planes, lo, hi):
-            copier(engine)(out=grouped[:, lo:hi, :].rearrange("p (c i) j -> p c j i", i=PACK),
-                           in_=planes[:, :, lo:hi].rearrange("p j (c i) -> p c j i", i=PACK))
+            copier(engine)(out=woven(grouped[:, lo:hi, :]), in_=walk(planes[:, :, lo:hi]))
+
+        def quantize(fmt, codes, scales, grouped):
+            nc.vector.quantize_mx(out=codes.bitcast(fmt), scales=scales, in_=grouped.rearrange("p c j -> p (c j)"))
+
+        def operand(name, width=K_PASS, staging=None):
+            return (keep([P, width, PACK], BF16, staging or name + "_grouped"), keep([P, width], U32, name + "_codes"),
+                    keep([P, width], U8, name + "_scales"))
+
+        def quantize_part(fmt, op, cols):
+            quantize(fmt, op[1][:, cols], op[2][:, cols], op[0][:, cols, :])
+
+        def finish_table(op, picked, planes):
+            gather("vector", picked, planes, PACK - 1, HALVES[0])
+            gather("scalar", picked, planes, PACK - 1, HALVES[1])
+            interleave("vector", op[0], picked, 0, HALF)
+            interleave("scalar", op[0], picked, N - TABLE_SCALAR_SHARE, N)
+            interleave("vector", op[0], picked, HALF, N - TABLE_SCALAR_SHARE)
+            for slots in HALVES:
+                quantize_part(E4M3, op, slots)
+
+        w_op = operand("w")
+        w_picked = keep([P, PACK, N], F32, "w_picked")
+        for j, engine in enumerate(("vector", "scalar", "vector")):
+            gather(engine, w_picked, w_planes, j, ALL)
+        finish_table(w_op, w_picked, w_planes)
+
+        turned = psum.tile([P, PACK, P], F32, name="bank%d" % (ROW_TILES - 1))
+        for t in range(PACK):
+            nc.tensor.transpose(turned[:, t, :], weight_rows[:, t::PACK], identity[:])
+        weight = keep([P, ROW_TILES], F32, "weight")
+        nc.scalar.copy(out=weight[:].rearrange("p (g t) -> p g t", t=PACK),
+                       in_=turned[:, :, :ROW_PASSES].rearrange("p t g -> p g t"))
+
+        x_ops = [operand("x%d" % g) for g in range(ROW_PASSES)]
 
         def cast_x(g, half, engine, lo=0, hi=P):
             tiles = slice(2 * half, 2 * half + 2)
             copier(engine)(out=x_ops[g][0][:].rearrange("p (t m) j -> p m j t", t=PACK)[:, lo:hi, :, tiles],
                            in_=x_raw[g][:].rearrange("p j (m t) -> p m j t", t=PACK)[:, lo:hi, :, tiles])
 
-        w_op = operand("w", "staging")
-        nc.scalar.dma_start(out=weight_rows[:ROW_PASSES, :], in_=wt[0].rearrange("(g r) o -> g (r o)", g=ROW_PASSES))
-        w_planes = [first_plane, second_plane] + [load(w_rows[:, j, :], [P, T], "w%d" % j) for j in range(2, PACK)]
-        w_listed = held.tile([P, PACK, N], F32, name="w_listed")
-        for j in range(PACK - 1):
-            nc.vector.tensor_copy(w_listed[:, j, :], w_planes[j][:].indirect(offsets[:]))
-        for slots in HALVES:
-            nc.vector.tensor_copy(w_listed[:, PACK - 1, slots], w_planes[PACK - 1][:].indirect(listed(slots)))
-        for slots, share in zip(HALVES, V_SCALAR_SHARE):
-            interleave("scalar", w_op[0], w_listed, slots.start, slots.start + share)
-            interleave("vector", w_op[0], w_listed, slots.start + share, slots.stop)
-        for slots in HALVES:
-            quantize_e4m3(w_op, slots)
-
-        turned = psum.tile([P, PACK, P], F32, name="bank%d" % (SCORE_BANKS - 1))
-        for t in range(PACK):
-            nc.tensor.transpose(turned[:, t, :], weight_rows[:, t::PACK], identity[:])
-        x_ops = []
-        x_raw = [load(x_rows[:, :, g * K_PASS:(g + 1) * K_PASS], [P, PACK, K_PASS], "x%d" % g) for g in range(ROW_PASSES)]
-        v_planes = [load(v_rows[:, j, :], [P, T], "v%d" % j) for j in range(PACK)]
-
         def stats(name):
-            return held.tile([P, ROW_TILES], F32, name=name, align_bytes=64)
+            return keep([P, ROW_TILES], F32, name)
 
-        def scores(table, n, bank, parts=(slice(0, N),)):
+        def softmax_tile(table, n, neg_max, total, result, parts=(ALL,)):
             g, t = divmod(n, PACK)
-            acc = psum.tile([P, N], F32, name="bank%d" % bank)
+            acc = psum.tile([P, N], F32, name="bank%d" % n)
             cols = slice(t * P, (t + 1) * P)
             for slots in parts:
                 nc.tensor.matmul_mx(out=acc[:, slots], lhsT=x_ops[g][1][:, cols].bitcast(E4M3),
                                     lhsT_scale=x_ops[g][2][:, cols], rhs=table[1][:, slots].bitcast(E4M3),
                                     rhs_scale=table[2][:, slots], start=True, stop=True)
-            return acc
+            nc.vector.tensor_reduce(out=neg_max[:, n:n + 1], in_=acc[:], axis=AXIS_X, op=ALU.max, negate=True)
+            nc.scalar.activation(result, acc[:], ACT.Exp, bias=neg_max[:, n:n + 1], accum_out=total[:, n:n + 1])
 
-        def student_bank(n):
-            return n % SCORE_BANKS
+        def scale_on_gpsimd(target, plane, inv, n):
+            nc.gpsimd.tensor_scalar(out=target, in0=plane, scalar1=inv, scalar2=weight[:, n:n + 1],
+                                    op0=ALU.mult, op1=ALU.mult)
 
-        def exps(name, acc, n, neg_max, total):
-            nc.vector.tensor_reduce(out=neg_max, in_=acc[:], axis=AXIS_X, op=ALU.max, negate=True)
-            result = held.tile([P, N], F32, name="exp_%s%d" % (name, n), align_bytes=64) if name + str(n) != "s0" else raw.tile([P, N], F32, name="x1")
-            nc.scalar.activation(result[:], acc[:], ACT.Exp, bias=neg_max, accum_out=total)
-            return result
-
-        v_listed = held.tile([P, PACK, N], F32, name="v_listed")
         s_max, s_sum, s_inv = stats("s_max"), stats("s_sum"), stats("s_inv")
-        t_max = stats("t_max")
-        t_inv = held.tile([P, 1 + ROW_TILES], F32, name="t_inv", align_bytes=64)
-        t_fac = held.tile([P, 1 + ROW_TILES], F32, name="t_fac", align_bytes=64)
-        t_sum = placed.tile([P, 1 + ROW_TILES], F32, name="t_sum", align_bytes=64, offset=0)
-        student, teacher, m_grouped = {}, {}, {}
+        t_max, t_sum, t_inv, t_fac = stats("t_max"), stats("t_sum"), stats("t_inv"), stats("t_fac")
+        student = [keep([P, PACK, N], F32, "student%d" % g) for g in range(ROW_PASSES)]
+        teacher = [keep([P, N], F32, "teacher%d" % n) for n in range(ROW_TILES)]
+        first_scaled = keep([P, PACK, N], F32, "first_scaled")
 
-        def student_exps(tiles):
+        def student_tiles(tiles):
             for n in tiles:
-                student[n] = exps("s", scores(w_op, n, student_bank(n)), n, s_max[:, n:n + 1], s_sum[:, n:n + 1])
+                softmax_tile(w_op, n, s_max, s_sum, student[n // PACK][:, n % PACK, :])
 
-        def scale_student(tiles, also=0):
-            cols = slice(tiles[0], tiles[-1] + 1 + also)
+        def scale_student(tiles):
+            cols = slice(tiles[0], tiles[-1] + 1)
             nc.vector.reciprocal(s_inv[:, cols], s_sum[:, cols])
             for n in tiles:
-                nc.gpsimd.tensor_scalar(out=student[n][:], in0=student[n][:], scalar1=s_inv[:, n:n + 1],
-                                        scalar2=weight_cols[:, n:n + 1], op0=ALU.mult, op1=ALU.mult)
+                plane = student[n // PACK][:, n % PACK, :]
+                scale_on_gpsimd(plane, plane, s_inv[:, n:n + 1], n)
 
-        def teacher_factors(cols):
-            nc.vector.reciprocal(t_inv[:, cols], t_sum[:, cols])
-            nc.vector.scalar_tensor_tensor(out=t_fac[:, cols], in0=t_inv[:, cols], scalar=-1.0,
-                                           in1=weight[:, cols], op0=ALU.mult, op1=ALU.mult)
+        v_op = operand("v")
+        v_picked = keep([P, PACK, N], F32, "v_picked")
 
-        def gather_v(j, slots):
-            nc.vector.tensor_copy(v_listed[:, j, slots], v_planes[j][:].indirect(listed(slots)))
+        cast_x(0, 0, "scalar", 0, X_SCALAR_SHARE)
+        cast_x(0, 0, "vector", X_SCALAR_SHARE, P)
+        cast_x(0, 1, "scalar", 0, X_SCALAR_SHARE)
+        cast_x(0, 1, "vector", X_SCALAR_SHARE, P)
+        for cols in (slice(0, P), slice(P, HALF), HALVES[1]):
+            quantize_part(E4M3, x_ops[0], cols)
+        student_tiles([0, 1])
+        cast_x(1, 0, "vector")
+        cast_x(1, 1, "scalar")
+        student_tiles([2])
+        quantize_part(E4M3, x_ops[1], HALVES[0])
+        student_tiles([3])
+        quantize_part(E4M3, x_ops[1], HALVES[1])
+        gather("scalar", v_picked, v_planes, 0, ALL)
+        scale_student([0, 1])
+        student_tiles([4, 5])
+        scale_student([2, 3])
+        student_tiles([6, 7])
+        scale_student([4, 5])
+        gather("vector", v_picked, v_planes, 1, ALL)
+        scale_student([6, 7])
+        gather("vector", v_picked, v_planes, 2, ALL)
+        finish_table(v_op, v_picked, v_planes)
 
-        g_grouped = {(g, h): held.tile([P, HALF * PACK], BF16, name="g_grouped%d%d" % (g, h), align_bytes=64)[:]
-                     for g, h in ((0, 0), (0, 1), (1, 1))}
-        g_shared = held.tile([P, HALF * (PACK + 1)], BF16, name="g_shared", align_bytes=64)
-        g_grouped[1, 0] = g_shared[:, HALF:]
-        g_codes = [held.tile([P, HALF + N], U32, name="g%d_codes" % g, align_bytes=64) for g in range(ROW_PASSES)]
-        g_scales = [held.tile([P, HALF + N], U8, name="g%d_scales" % g, align_bytes=64) for g in range(ROW_PASSES)]
-        for g in range(ROW_PASSES):
-            nc.gpsimd.memset(g_codes[g][:, :HALF], 0)
-            nc.gpsimd.memset(g_scales[g][:, :HALF].bitcast(U32), 0)
-        padded_first_half = slice(0, N)
-        all_slots = slice(HALF, HALF + N)
-        first_planes = held.tile([P, PACK * HALF], BF16, name="g_planes00", align_bytes=64)
-        g_planes = {(0, 0): first_planes[:].rearrange("p (j c) -> p j c", j=PACK)}
-        m_shared = held.tile([P, 2 * HALF * PACK], BF16, name="m_shared", align_bytes=64)
-        g_planes[1, 0] = m_shared[:, HALF * PACK:].rearrange("p (j c) -> p j c", j=PACK)
-        m_grouped[0, 1] = m_shared[:, :HALF * PACK]
-        g_planes[1, 1] = g_shared[:, :HALF * PACK].rearrange("p (j c) -> p j c", j=PACK)
-        m_codes = {}
-        m_scales = held.tile([P, ROW_PASSES, D], U8, name="m_scales", align_bytes=64)
+        m_raw = {(g, h): load(m_rows[g][:, :, HALVES[h]], [P, PACK, HALF], "w%d" % (2 * h + g))
+                 for h in range(2) for g in range(ROW_PASSES)}
+        m_grouped, m_codes = {}, {}
+        m_shape = [P, ROW_PASSES * P]
+        m_scales = keep([P, BLOCKS, ROW_PASSES * P], U8, "m_scales")
 
-        def cast_m(engine, g, h, lo, hi):
-            planes = m_raw[g][:, :, HALVES[h]]
-            target = m_grouped[g, h].rearrange("p (m j) -> p m j", j=PACK)
-            if engine == "gpsimd":
-                nc.gpsimd.tensor_copy(out=target[:, lo:hi, :], in_=planes[:, :, lo:hi].rearrange("p j m -> p m j"))
-            else:
-                interleave(engine, target, planes, lo, hi)
+        def cast_m(engine, c, passes=range(ROW_PASSES)):
+            for g in passes:
+                target = m_grouped[c][:, g * P:(g + 1) * P, :]
+                planes = m_raw[g, c // 2][:, :, c % 2 * P:(c % 2 + 1) * P]
+                if engine == "gpsimd":
+                    nc.gpsimd.tensor_copy(out=target, in_=planes.rearrange("p j m -> p m j"))
+                else:
+                    interleave(engine, target, planes, 0, P)
 
-        def quantize_m(g, h, name):
-            m_codes[g, h] = held.tile([P, HALF], U32, name=name, align_bytes=64)
-            nc.vector.quantize_mx(out=m_codes[g, h][:].bitcast(E4M3), scales=m_scales[:, g, HALVES[h]],
-                                  in_=m_grouped[g, h])
+        def m_staging(c, name):
+            m_grouped[c] = keep([P, ROW_PASSES * P, PACK], BF16, name)[:]
 
-        def combine(g, h, places=range(PACK), cols=slice(0, HALF)):
-            for t in places:
-                n = g * PACK + t
-                scaled = student[n][:, HALVES[h]]
-                nc.vector.scalar_tensor_tensor(out=g_planes[g, h][:, t, cols], in0=teacher[n][:, HALVES[h]][:, cols],
-                                               scalar=t_fac[:, n + 1:n + 2], in1=scaled[:, cols], op0=ALU.mult,
-                                               op1=ALU.subtract if n == LATE_TILE else ALU.add)
+        def place(shape, dtype, name, offset):
+            return placed.tile(shape, dtype, name=name, align_bytes=64, offset=offset)
 
-        def interleave_g(g, h, engine="scalar", lo=0, hi=HALF):
-            interleave(engine, g_grouped[g, h].rearrange("p (c j) -> p c j", j=PACK), g_planes[g, h], lo, hi)
+        def quantize_m(c, codes):
+            m_codes[c] = codes[:]
+            quantize(E4M3, m_codes[c], m_scales[:, c, :], m_grouped[c])
+
+        def teacher_tile(n):
+            softmax_tile(v_op, n, t_max, t_sum, teacher[n][:], HALVES if n == 0 else (ALL,))
+
+        def teacher_inv(lo, hi):
+            nc.vector.reciprocal(t_inv[:, lo:hi], t_sum[:, lo:hi])
+
+        early_inv = [keep([P, 1], F32, "inv%d" % n) for n in range(PACK)]
+        for n in range(ROW_TILES):
+            teacher_tile(n)
+            behind = n - 2
+            if 0 <= behind < PACK:
+                nc.vector.reciprocal(early_inv[behind][:], t_sum[:, behind:behind + 1])
+            if 0 <= behind < GPSIMD_TILES:
+                scale_on_gpsimd(first_scaled[:, behind, :], teacher[behind][:], early_inv[behind][:], behind)
+        m_staging(0, "m0_grouped")
+        m_staging(1, "v_grouped")
+        cast_m("vector", 1, [0])
+        cast_m("scalar", 0)
+        cast_m("scalar", 1, [1])
+
+        g_ops = {}
+        scaled = [keep([P, PACK, HALF], F32, "scaled%d" % h)[:] for h in range(2)]
+
+        def factors(tiles):
+            for n in tiles:
+                nc.scalar.activation(t_fac[:, n:n + 1], t_inv[:, n:n + 1], ACT.Copy, scale=weight[:, n:n + 1])
+
+        def scale_on_scalar(tiles, h):
+            for n in tiles:
+                nc.scalar.activation(scaled[h][:, n % PACK, :], teacher[n][:, HALVES[h]], ACT.Copy,
+                                     scale=t_fac[:, n:n + 1])
+
+        def combine(g, h, staging):
+            g_ops[g, h] = operand("g%d%d" % (g, h), HALF, staging)
+            other = first_scaled[:, :, HALVES[h]] if g == 0 else scaled[h]
+            nc.vector.tensor_tensor(out=woven(g_ops[g, h][0][:]), in0=walk(student[g][:, :, HALVES[h]]),
+                                    in1=walk(other), op=ALU.subtract)
 
         def quantize_g(g, h):
-            cols = slice((h + 1) * HALF, (h + 2) * HALF)
-            nc.vector.quantize_mx(out=g_codes[g][:, cols].bitcast(E5M2), scales=g_scales[g][:, cols],
-                                  in_=g_grouped[g, h])
+            quantize_part(E5M2, g_ops[g, h], slice(0, HALF))
 
-        def product(c, cols, bank):
-            acc = psum.tile([P, N], F32, name="product%d" % bank)
-            block = slice(c * P, (c + 1) * P)
-            for g in range(ROW_PASSES):
-                nc.tensor.matmul_mx(out=acc[:], lhsT=m_codes[g, c // 2][:, c % 2 * P:(c % 2 + 1) * P].bitcast(E4M3), lhsT_scale=m_scales[:, g, block],
-                                    rhs=g_codes[g][:, cols].bitcast(E5M2), rhs_scale=g_scales[g][:, cols],
-                                    start=g == 0, stop=g == ROW_PASSES - 1)
+        def product(c, halves, bank):
+            acc = psum.tile([P, len(halves), HALF], F32, name="bank%d" % bank)
+            for k, h in enumerate(halves):
+                for g in range(ROW_PASSES):
+                    block = slice(g * P, (g + 1) * P)
+                    nc.tensor.matmul_mx(out=acc[:, k, :], lhsT=m_codes[c][:, block].bitcast(E4M3),
+                                        lhsT_scale=m_scales[:, c, block], rhs=g_ops[g, h][1][:].bitcast(E5M2),
+                                        rhs_scale=g_ops[g, h][2][:], start=g == 0, stop=g == ROW_PASSES - 1)
             return acc
 
-        def copy_out(source, width, name):
-            dw = held.tile([P, width], F32, name=name, align_bytes=64)
-            nc.scalar.copy(out=dw[:], in_=source)
+        def copy_out(engine, c, halves, bank, offset=None):
+            acc = product(c, halves, bank)
+            shape, name = [P, len(halves) * HALF], "dw%d%d" % (c, halves[0])
+            dw = keep(shape, F32, name) if offset is None else place(shape, F32, name, offset)
+            copier(engine)(out=dw[:], in_=acc[:].rearrange("p k c -> p (k c)"))
             return dw[:]
 
-        def scatter(c, dw, slots):
-            nc.vector.tensor_copy(windows[c][:].indirect(listed(slots)), dw)
+        def scatter(engine, c, slots, values):
+            indirect_copy(engine, windows[c][:].indirect(listed(slots)), values)
 
-        def finish(c, first_slot):
-            acc = product(c, all_slots, (c + 1) % 2)
-            scatter(c, copy_out(acc[:, first_slot:], N - first_slot, "dw%d" % c), slice(first_slot, N))
-            if c < len(windows) - 1:
+        def store(c):
+            if c < BLOCKS - 1:
                 nc.sync.dma_start(out=out[c * P:(c + 1) * P, :], in_=windows[c][:])
                 return
             for queue, cols in ((nc.sync, slice(0, T // 2)), (nc.scalar, slice(T // 2, T))):
                 queue.dma_start(out=out[c * P:(c + 1) * P, cols], in_=windows[c][:, cols])
 
-        x_ops.append(operand("x0", "x_grouped"))
-        cast_x(0, 0, "scalar", 0, X_SCALAR_SHARE)
-        cast_x(0, 0, "vector", X_SCALAR_SHARE, P)
-        cast_x(0, 1, "scalar", 0, P - X_SCALAR_SHARE)
-        cast_x(0, 1, "vector", P - X_SCALAR_SHARE, P)
-        for cols in (slice(0, P), slice(P, HALF), HALVES[1]):
-            quantize_e4m3(x_ops[0], cols)
-        weight = raw.tile([P, 1 + ROW_TILES], F32, name="x0")
-        weight_cols = weight[:, 1:]
-        nc.scalar.copy(out=weight_cols.rearrange("p (g t) -> p g t", t=PACK),
-                       in_=turned[:, :, :ROW_PASSES].rearrange("p t g -> p g t"))
-        nc.scalar.copy(out=weight[:, :1], in_=turned[:, PACK - 1, ROW_PASSES - 1:ROW_PASSES])
-
-        x_ops.append(operand("x1", "x_grouped"))
-        cast_x(1, 0, "scalar")
-        cast_x(1, 1, "scalar")
-        student_exps([0, 1, 2, 3])
-        for cols in HALVES:
-            quantize_e4m3(x_ops[1], cols)
-        v_staging = held.tile([P, N * PACK], BF16, name="staging", align_bytes=64)
-        v_op = (v_staging[:].rearrange("p (c j) -> p c j", j=PACK),
-                held.tile([P, K_PASS], U32, name="v_codes", align_bytes=64),
-                held.tile([P, K_PASS], U8, name="v_scales", align_bytes=64))
-        gather_v(0, slice(0, N))
-        scale_student([0, 1])
-        student_exps([4, 5])
-        scale_student([2, 3])
-        student_exps([6])
-        late_scores = scores(w_op, LATE_TILE, student_bank(LATE_TILE))
-        gather_v(1, slice(0, N))
-        scalar_tiles = [5, 6]
-        scale_student([4], also=len(scalar_tiles))
-        gather_v(2, slice(0, N))
-        s_fac = stats("s_fac")
-        for n in scalar_tiles:
-            nc.scalar.activation(s_fac[:, n:n + 1], s_inv[:, n:n + 1], ACT.Copy, scale=weight_cols[:, n:n + 1])
-        for n in scalar_tiles:
-            nc.scalar.activation(student[n][:], student[n][:], ACT.Copy, scale=s_fac[:, n:n + 1])
-
-        for slots in HALVES:
-            gather_v(PACK - 1, slots)
-        for slots, share in zip(HALVES, V_SCALAR_SHARE):
-            interleave("scalar", v_op[0], v_listed, slots.start, slots.start + share)
-            interleave("vector", v_op[0], v_listed, slots.start + share, slots.stop)
-        for slots in HALVES:
-            quantize_e4m3(v_op, slots)
-        late_max = v_staging[:, HALF * PACK - 2:HALF * PACK].bitcast(F32)
-        student[LATE_TILE] = exps("s", late_scores, LATE_TILE, late_max, t_sum[:, :1])
-        m_raw = [load(m_rows[g], [P, PACK, D], "w%d" % (g + 2)) for g in range(ROW_PASSES)]
-
-        m_grouped[0, 0] = v_staging[:, HALF * PACK:]
-        m_grouped[1, 0] = held.tile([P, HALF * PACK], BF16, name="m_grouped", align_bytes=64)[:]
-        cast_m("gpsimd", 0, 0, 0, HALF)
-        cast_m("gpsimd", 0, 1, 0, HALF)
-        cast_m("gpsimd", 1, 0, 0, HALF)
-
-        held_max = {ROW_TILES - 1: first_planes[:, HALF * PACK - 2:].bitcast(F32)}
-
-        def teacher_exps(tiles):
-            for n in tiles:
-                teacher[n] = exps("t", scores(v_op, n, (n + 2) % SCORE_BANKS, HALVES if n == 0 else (slice(0, N),)), n,
-                                  held_max.get(n, t_max[:, n:n + 1]), t_sum[:, n + 1:n + 2])
-
-        teacher_exps([0, 1, 2, 3, 4, 5])
-        teacher_factors(slice(0, 1 + PACK))
-        teacher_exps([6, 7])
-        nc.scalar.activation(student[LATE_TILE][:], student[LATE_TILE][:], ACT.Copy, scale=t_fac[:, :1])
-        quantize_m(0, 0, "m_codes00")
-
-        combine(0, 0, range(PACK - 1))
-        second = slice(1 + PACK, 1 + ROW_TILES)
-        nc.vector.reciprocal(t_inv[:, second], t_sum[:, second])
-        combine(0, 0, [PACK - 1])
-        interleave_g(0, 0)
-        nc.vector.scalar_tensor_tensor(out=t_fac[:, second], in0=t_inv[:, second], scalar=-1.0,
-                                       in1=weight[:, second], op0=ALU.mult, op1=ALU.mult)
-        combine(1, 0, cols=slice(0, G_FIRST_PIECE))
-        interleave_g(1, 0, "scalar", 0, G_FIRST_PIECE)
-        combine(1, 0, cols=slice(G_FIRST_PIECE, HALF))
-        interleave_g(1, 0, "scalar", G_FIRST_PIECE, HALF)
-        quantize_g(1, 0)
-        g_planes[0, 1] = placed.tile([P, PACK, HALF], BF16, name="g_planes01", align_bytes=64, offset=0)
-        combine(0, 1)
+        teacher_inv(4, 6)
+        factors([4, 5])
+        scale_on_scalar([4, 5], 0)
+        for n in range(GPSIMD_TILES, PACK):
+            nc.vector.tensor_scalar(out=first_scaled[:, n, :], in0=teacher[n][:], scalar1=early_inv[n][:],
+                                    scalar2=weight[:, n:n + 1], op0=ALU.mult, op1=ALU.mult)
+        quantize_m(0, keep(m_shape, U32, "v_codes"))
+        combine(0, 0, "g_staging0")
+        teacher_inv(6, 8)
+        factors([6, 7])
+        scale_on_scalar([6, 7], 0)
+        combine(0, 1, "g_staging1")
+        scale_on_scalar([4, 5, 6, 7], 1)
         quantize_g(0, 0)
-        quantize_m(1, 0, "m_codes10")
-
-        early = product(0, padded_first_half, 0)
-        interleave_g(0, 1)
-        dw_early = copy_out(early[:, HALF:], HALF, "dw_early")
-        combine(1, 1)
-        interleave_g(1, 1)
+        combine(1, 0, "g_staging2")
         quantize_g(0, 1)
-        quantize_m(0, 1, "exp_s6")
+        quantize_g(1, 0)
+        m_staging(2, "g_staging0")
+        cast_m("scalar", 2)
+        scatter("scalar", 0, HALVES[0], copy_out("scalar", 0, [0], 0))
+        quantize_m(1, keep(m_shape, U32, "first_scaled"))
+        combine(1, 1, "g_staging2")
+        quantize_m(2, keep(m_shape, U32, "m2_codes"))
         quantize_g(1, 1)
-        scatter(0, dw_early, HALVES[0])
-
-        early = product(1, padded_first_half, 0)
-        after_g = held.tile([P, HALF + N], F32, name="g_shared", align_bytes=64)
-        nc.scalar.copy(out=after_g[:, :HALF], in_=early[:, HALF:])
-        scatter(1, after_g[:, :HALF], HALVES[0])
-        finish(0, HALF)
-        m_grouped[1, 1] = after_g[:, HALF:].bitcast(BF16)
-        for lo in (0, P):
-            cast_m("scalar", 1, 1, lo, lo + P)
-        quantize_m(1, 1, "m_codes11")
-        finish(1, HALF)
-        finish(2, 0)
-        finish(3, 0)
+        scatter("vector", 0, HALVES[1], copy_out("vector", 0, [1], 1, 512))
+        store(0)
+        m_staging(3, "g_staging2")
+        cast_m("gpsimd", 3)
+        for h in range(2):
+            scatter("scalar", 1, HALVES[h], copy_out("scalar", 1, [h], 2 + h))
+        store(1)
+        both = copy_out("vector", 2, [0, 1], 2, 1024)
+        quantize_m(3, place(m_shape, U32, "m3_codes", 0))
+        scatter("vector", 2, ALL, both)
+        store(2)
+        for h in range(2):
+            scatter("scalar", 3, HALVES[h], copy_out("scalar", 3, [h], 4 + h))
+        store(3)

@@ -31,6 +31,7 @@ ALL = slice(0, N)
 TABLE_SCALAR_SHARE = 160
 X_SCALAR_SHARE = 48
 GPSIMD_TILES = 3
+V_VECTOR_SHARE = 128
 
 
 def tile_attend_gds_kl_kernel(tc, xT, wT, vT, wt, xm, offs, out):
@@ -183,22 +184,23 @@ def tile_attend_gds_kl_kernel(tc, xT, wT, vT, wt, xm, offs, out):
         cast_x(0, 1, "vector", X_SCALAR_SHARE, P)
         for cols in (slice(0, P), slice(P, HALF), HALVES[1]):
             quantize_part(E4M3, x_ops[0], cols)
-        student_tiles([0, 1])
         cast_x(1, 0, "vector")
-        cast_x(1, 1, "scalar")
-        student_tiles([2])
-        quantize_part(E4M3, x_ops[1], HALVES[0])
-        student_tiles([3])
-        quantize_part(E4M3, x_ops[1], HALVES[1])
-        gather("scalar", v_picked, v_planes, 0, ALL)
+        for t in (2, 3):
+            nc.gpsimd.tensor_copy(out=x_ops[1][0][:, t * P:(t + 1) * P, :],
+                                  in_=x_raw[1][:].rearrange("p j (m t) -> p t m j", t=PACK)[:, t])
+        student_tiles([0, 1, 2, 3])
+        for cols in HALVES:
+            quantize_part(E4M3, x_ops[1], cols)
         scale_student([0, 1])
-        student_tiles([4, 5])
+        student_tiles([4])
         scale_student([2, 3])
-        student_tiles([6, 7])
+        gather("scalar", v_picked, v_planes, 0, ALL)
+        student_tiles([5, 6, 7])
         scale_student([4, 5])
-        gather("vector", v_picked, v_planes, 1, ALL)
-        scale_student([6, 7])
+        gather("scalar", v_picked, v_planes, 1, slice(V_VECTOR_SHARE, N))
+        gather("vector", v_picked, v_planes, 1, slice(0, V_VECTOR_SHARE))
         gather("vector", v_picked, v_planes, 2, ALL)
+        scale_student([6, 7])
         finish_table(v_op, v_picked, v_planes)
 
         m_raw = {(g, h): load(m_rows[g][:, :, HALVES[h]], [P, PACK, HALF], "w%d" % (2 * h + g))
@@ -320,10 +322,10 @@ def tile_attend_gds_kl_kernel(tc, xT, wT, vT, wt, xm, offs, out):
         quantize_g(1, 1)
         scatter("vector", 0, HALVES[1], copy_out("vector", 0, [1], 1, 512))
         store(0)
+        scatter("scalar", 1, HALVES[0], copy_out("vector", 1, [0], 2))
         m_staging(3, "g_staging2")
         cast_m("gpsimd", 3)
-        for h in range(2):
-            scatter("scalar", 1, HALVES[h], copy_out("scalar", 1, [h], 2 + h))
+        scatter("scalar", 1, HALVES[1], copy_out("scalar", 1, [1], 3))
         store(1)
         both = copy_out("vector", 2, [0, 1], 2, 1024)
         quantize_m(3, place(m_shape, U32, "m3_codes", 0))

@@ -31,7 +31,6 @@ ALL = slice(0, N)
 TABLE_SCALAR_SHARE = 160
 X_SCALAR_SHARE = 48
 GPSIMD_TILES = 3
-V_VECTOR_SHARE = 128
 
 
 def tile_attend_gds_kl_kernel(tc, xT, wT, vT, wt, xm, offs, out):
@@ -54,6 +53,9 @@ def tile_attend_gds_kl_kernel(tc, xT, wT, vT, wt, xm, offs, out):
 
         def keep(shape, dtype, name):
             return held.tile(shape, dtype, name=name, align_bytes=64)
+
+        def place(shape, dtype, name, offset):
+            return placed.tile(shape, dtype, name=name, align_bytes=64, offset=offset)
 
         w_rows = wT.rearrange("(p j) t -> p j t", j=PACK)
         v_rows = vT.rearrange("(p j) t -> p j t", j=PACK)
@@ -168,14 +170,14 @@ def tile_attend_gds_kl_kernel(tc, xT, wT, vT, wt, xm, offs, out):
             for n in tiles:
                 softmax_tile(w_op, n, s_max, s_sum, student[n // PACK][:, n % PACK, :])
 
-        def scale_student(tiles):
+        def scale_student(tiles, inv=s_inv):
             cols = slice(tiles[0], tiles[-1] + 1)
-            nc.vector.reciprocal(s_inv[:, cols], s_sum[:, cols])
+            nc.vector.reciprocal(inv[:, cols], s_sum[:, cols])
             for n in tiles:
                 plane = student[n // PACK][:, n % PACK, :]
-                scale_on_gpsimd(plane, plane, s_inv[:, n:n + 1], n)
+                scale_on_gpsimd(plane, plane, inv[:, n:n + 1], n)
 
-        v_op = operand("v")
+        v_op = (place([P, N, PACK], BF16, "v_grouped", 4096), keep([P, N], U32, "v_codes"), keep([P, N], U8, "v_scales"))
         v_picked = keep([P, PACK, N], F32, "v_picked")
 
         cast_x(0, 0, "scalar", 0, X_SCALAR_SHARE)
@@ -184,23 +186,22 @@ def tile_attend_gds_kl_kernel(tc, xT, wT, vT, wt, xm, offs, out):
         cast_x(0, 1, "vector", X_SCALAR_SHARE, P)
         for cols in (slice(0, P), slice(P, HALF), HALVES[1]):
             quantize_part(E4M3, x_ops[0], cols)
-        cast_x(1, 0, "vector")
+        cast_x(1, 0, "scalar")
         for t in (2, 3):
             nc.gpsimd.tensor_copy(out=x_ops[1][0][:, t * P:(t + 1) * P, :],
                                   in_=x_raw[1][:].rearrange("p j (m t) -> p t m j", t=PACK)[:, t])
-        student_tiles([0, 1, 2, 3])
-        for cols in HALVES:
-            quantize_part(E4M3, x_ops[1], cols)
+        student_tiles([0, 1, 2])
+        quantize_part(E4M3, x_ops[1], ALL)
         scale_student([0, 1])
+        student_tiles([3])
+        gather("scalar", v_picked, v_planes, 0, ALL)
         student_tiles([4])
         scale_student([2, 3])
-        gather("scalar", v_picked, v_planes, 0, ALL)
         student_tiles([5, 6, 7])
         scale_student([4, 5])
-        gather("scalar", v_picked, v_planes, 1, slice(V_VECTOR_SHARE, N))
-        gather("vector", v_picked, v_planes, 1, slice(0, V_VECTOR_SHARE))
+        gather("vector", v_picked, v_planes, 1, ALL)
+        scale_student([6])
         gather("vector", v_picked, v_planes, 2, ALL)
-        scale_student([6, 7])
         finish_table(v_op, v_picked, v_planes)
 
         m_raw = {(g, h): load(m_rows[g][:, :, HALVES[h]], [P, PACK, HALF], "w%d" % (2 * h + g))
@@ -221,9 +222,6 @@ def tile_attend_gds_kl_kernel(tc, xT, wT, vT, wt, xm, offs, out):
         def m_staging(c, name):
             m_grouped[c] = keep([P, ROW_PASSES * P, PACK], BF16, name)[:]
 
-        def place(shape, dtype, name, offset):
-            return placed.tile(shape, dtype, name=name, align_bytes=64, offset=offset)
-
         def quantize_m(c, codes):
             m_codes[c] = codes[:]
             quantize(E4M3, m_codes[c], m_scales[:, c, :], m_grouped[c])
@@ -234,6 +232,9 @@ def tile_attend_gds_kl_kernel(tc, xT, wT, vT, wt, xm, offs, out):
         def teacher_inv(lo, hi):
             nc.vector.reciprocal(t_inv[:, lo:hi], t_sum[:, lo:hi])
 
+        m_grouped[1] = place([P, ROW_PASSES * P, PACK], BF16, "m1_grouped", 4096)[:]
+        cast_m("vector", 1, [0])
+        scale_student([7], place([P, ROW_TILES], F32, "late_inv", 6144))
         early_inv = [keep([P, 1], F32, "inv%d" % n) for n in range(PACK)]
         for n in range(ROW_TILES):
             teacher_tile(n)
@@ -243,8 +244,6 @@ def tile_attend_gds_kl_kernel(tc, xT, wT, vT, wt, xm, offs, out):
             if 0 <= behind < GPSIMD_TILES:
                 scale_on_gpsimd(first_scaled[:, behind, :], teacher[behind][:], early_inv[behind][:], behind)
         m_staging(0, "m0_grouped")
-        m_staging(1, "v_grouped")
-        cast_m("vector", 1, [0])
         cast_m("scalar", 0)
         cast_m("scalar", 1, [1])
 

@@ -31,6 +31,7 @@ ALL = slice(0, N)
 TABLE_SCALAR_SHARE = 160
 X_SCALAR_SHARE = 48
 GPSIMD_TILES = 3
+V_VECTOR_SHARE = 320
 
 
 def tile_attend_gds_kl_kernel(tc, xT, wT, vT, wt, xm, offs, out):
@@ -114,9 +115,11 @@ def tile_attend_gds_kl_kernel(tc, xT, wT, vT, wt, xm, offs, out):
             quantize(fmt, op[1][:, cols], op[2][:, cols], op[0][:, cols, :])
 
         def finish_table(op, picked, planes):
-            gather("vector", picked, planes, PACK - 1, HALVES[0])
+            for lo in (0, P):
+                gather("vector", picked, planes, PACK - 1, slice(lo, lo + P))
             gather("scalar", picked, planes, PACK - 1, HALVES[1])
-            interleave("vector", op[0], picked, 0, HALF)
+            for lo in (0, P):
+                interleave("vector", op[0], picked, lo, lo + P)
             interleave("scalar", op[0], picked, N - TABLE_SCALAR_SHARE, N)
             interleave("vector", op[0], picked, HALF, N - TABLE_SCALAR_SHARE)
             for slots in HALVES:
@@ -199,7 +202,8 @@ def tile_attend_gds_kl_kernel(tc, xT, wT, vT, wt, xm, offs, out):
         scale_student([2, 3])
         student_tiles([5, 6, 7])
         scale_student([4, 5])
-        gather("vector", v_picked, v_planes, 1, ALL)
+        gather("vector", v_picked, v_planes, 1, slice(0, V_VECTOR_SHARE))
+        gather("scalar", v_picked, v_planes, 1, slice(V_VECTOR_SHARE, N))
         scale_student([6])
         gather("vector", v_picked, v_planes, 2, ALL)
         finish_table(v_op, v_picked, v_planes)

@@ -204,7 +204,6 @@ def tile_attend_gds_kl_kernel(tc, xT, wT, vT, wt, xm, offs, out):
         scale_student([4, 5])
         gather("vector", v_picked, v_planes, 1, slice(0, V_VECTOR_SHARE))
         gather("scalar", v_picked, v_planes, 1, slice(V_VECTOR_SHARE, N))
-        scale_student([6])
         gather("vector", v_picked, v_planes, 2, ALL)
         finish_table(v_op, v_picked, v_planes)
 
@@ -238,7 +237,7 @@ def tile_attend_gds_kl_kernel(tc, xT, wT, vT, wt, xm, offs, out):
 
         m_grouped[1] = place([P, ROW_PASSES * P, PACK], BF16, "m1_grouped", 4096)[:]
         cast_m("vector", 1, [0])
-        scale_student([7], place([P, ROW_TILES], F32, "late_inv", 6144))
+        scale_student([6, 7], place([P, ROW_TILES], F32, "late_inv", 6144))
         early_inv = [keep([P, 1], F32, "inv%d" % n) for n in range(PACK)]
         for n in range(ROW_TILES):
             teacher_tile(n)

@@ -180,7 +180,7 @@ def tile_attend_gds_kl_kernel(tc, xT, wT, vT, wt, xm, offs, out):
                 plane = student[n // PACK][:, n % PACK, :]
                 scale_on_gpsimd(plane, plane, inv[:, n:n + 1], n)
 
-        v_op = (place([P, N, PACK], BF16, "v_grouped", 4096), keep([P, N], U32, "v_codes"), keep([P, N], U8, "v_scales"))
+        v_op = operand("v")
         v_picked = keep([P, PACK, N], F32, "v_picked")
 
         cast_x(0, 0, "scalar", 0, X_SCALAR_SHARE)
@@ -235,12 +235,16 @@ def tile_attend_gds_kl_kernel(tc, xT, wT, vT, wt, xm, offs, out):
         def teacher_inv(lo, hi):
             nc.vector.reciprocal(t_inv[:, lo:hi], t_sum[:, lo:hi])
 
-        m_grouped[1] = place([P, ROW_PASSES * P, PACK], BF16, "m1_grouped", 4096)[:]
+        m_staging(1, "v_picked")
         cast_m("vector", 1, [0])
-        scale_student([6, 7], place([P, ROW_TILES], F32, "late_inv", 6144))
+        v_flat = v_op[0][:].rearrange("p c j -> p (c j)")
+        late_inv = v_flat[:, HALF * PACK - 2 * ROW_TILES:HALF * PACK].bitcast(F32)
+        scale_student([6], late_inv)
         early_inv = [keep([P, 1], F32, "inv%d" % n) for n in range(PACK)]
         for n in range(ROW_TILES):
             teacher_tile(n)
+            if n == 0:
+                scale_student([7], late_inv)
             behind = n - 2
             if 0 <= behind < PACK:
                 nc.vector.reciprocal(early_inv[behind][:], t_sum[:, behind:behind + 1])

from contextlib import ExitStack

import concourse.mybir as mybir
from concourse.masks import make_identity

N, T, D, R = 512, 2048, 512, 1024
FLOPS = 3 * 2 * R * N * D

F32 = mybir.dt.float32
BF16 = mybir.dt.bfloat16
U32 = mybir.dt.uint32
I32 = mybir.dt.int32
U16 = mybir.dt.uint16
U8 = mybir.dt.uint8
E4M3 = mybir.dt.float8_e4m3fn_x4
E5M2 = mybir.dt.float8_e5m2_x4
ALU = mybir.AluOpType
ACT = mybir.ActivationFunctionType
AXIS_X = mybir.AxisListType.X

P = 128
PACK = 4
K_PASS = P * PACK
ROW_PASSES = R // K_PASS
ROW_TILES = R // P
BLOCKS = D // P
LIST_ROWS = 16
HALF = N // 2
HALVES = [slice(0, HALF), slice(HALF, N)]
ALL = slice(0, N)
TABLE_SCALAR_SHARE = 160
X_SCALAR_SHARE = 48
GPSIMD_TILES = 3
V_VECTOR_SHARE = 320


def tile_attend_gds_kl_kernel(tc, xT, wT, vT, wt, xm, offs, out):
    nc = tc.nc
    with ExitStack() as ctx:
        held = ctx.enter_context(tc.tile_pool(name="held", bufs=1))
        raw = ctx.enter_context(tc.tile_pool(name="raw", bufs=1))
        placed = ctx.enter_context(tc.tile_pool(name="placed", bufs=1))
        psum = ctx.enter_context(tc.psum_pool(name="psum", bufs=1))

        offsets = held.tile([P, N // LIST_ROWS], U16, name="offsets")

        def listed(slots):
            return offsets[:, slots.start // LIST_ROWS:slots.stop // LIST_ROWS]

        def load(source, shape, name, queue=nc.sync):
            tile = raw.tile(shape, F32, name=name)
            queue.dma_start(out=tile[:], in_=source)
            return tile

        def keep(shape, dtype, name):
            return held.tile(shape, dtype, name=name, align_bytes=64)

        def place(shape, dtype, name, offset):
            return placed.tile(shape, dtype, name=name, align_bytes=64, offset=offset)

        w_rows = wT.rearrange("(p j) t -> p j t", j=PACK)
        v_rows = vT.rearrange("(p j) t -> p j t", j=PACK)
        x_rows = xT[0].rearrange("(p j) r -> p j r", j=PACK)
        m_rows = xm[0].rearrange("(g p j) d -> g p j d", p=P, j=PACK)

        w_planes = [load(w_rows[:, 0, :], [P, T], "w0")]
        nc.sync.dma_start(offsets[:], offs)
        w_planes.append(load(w_rows[:, 1, :], [P, T], "w1", nc.scalar))

        weight_rows = held.tile([P, K_PASS], F32, name="weight_rows")
        nc.gpsimd.memset(weight_rows[:], 0.0)
        identity = held.tile([P, P], F32, name="identity")
        make_identity(nc, identity[:])
        nc.scalar.dma_start(out=weight_rows[:ROW_PASSES, :], in_=wt[0].rearrange("(g r) o -> g (r o)", g=ROW_PASSES))

        windows = [held.tile([P, T], F32, name="window%d" % c) for c in range(BLOCKS)]
        for c, window in enumerate(windows):
            engine = nc.vector if c < BLOCKS // 2 else nc.gpsimd
            engine.memset(window[:].bitcast(I32), 0)

        w_planes.extend(load(w_rows[:, j, :], [P, T], "w%d" % j) for j in range(2, PACK))
        x_raw = [load(x_rows[:, :, g * K_PASS:(g + 1) * K_PASS], [P, PACK, K_PASS], "x%d" % g)
                 for g in range(ROW_PASSES)]
        v_planes = [load(v_rows[:, j, :], [P, T], "v%d" % j) for j in range(PACK)]

        def copier(engine):
            return nc.vector.tensor_copy if engine == "vector" else nc.scalar.copy

        def indirect_copy(engine, target, source):
            if engine == "vector":
                nc.vector.tensor_copy(target, source)
            else:
                nc.scalar.activation(target, source, ACT.Copy)

        def gather(engine, picked, planes, j, slots):
            indirect_copy(engine, picked[:, j, slots], planes[j][:].indirect(listed(slots)))

        def walk(planes):
            return planes.rearrange("p j (c i) -> p c j i", i=PACK)

        def woven(grouped):
            return grouped.rearrange("p (c i) j -> p c j i", i=PACK)

        def interleave(engine, grouped, planes, lo, hi):
            copier(engine)(out=woven(grouped[:, lo:hi, :]), in_=walk(planes[:, :, lo:hi]))

        def quantize(fmt, codes, scales, grouped):
            nc.vector.quantize_mx(out=codes.bitcast(fmt), scales=scales, in_=grouped.rearrange("p c j -> p (c j)"))

        def operand(name, width=K_PASS, staging=None):
            return (keep([P, width, PACK], BF16, staging or name + "_grouped"), keep([P, width], U32, name + "_codes"),
                    keep([P, width], U8, name + "_scales"))

        def quantize_part(fmt, op, cols):
            quantize(fmt, op[1][:, cols], op[2][:, cols], op[0][:, cols, :])

        def finish_table(op, picked, planes):
            for lo in (0, P):
                gather("vector", picked, planes, PACK - 1, slice(lo, lo + P))
            gather("scalar", picked, planes, PACK - 1, HALVES[1])
            for lo in (0, P):
                interleave("vector", op[0], picked, lo, lo + P)
            interleave("scalar", op[0], picked, N - TABLE_SCALAR_SHARE, N)
            interleave("vector", op[0], picked, HALF, N - TABLE_SCALAR_SHARE)
            for slots in HALVES:
                quantize_part(E4M3, op, slots)

        w_op = operand("w")
        w_picked = keep([P, PACK, N], F32, "w_picked")
        for j, engine in enumerate(("vector", "scalar", "vector")):
            gather(engine, w_picked, w_planes, j, ALL)
        finish_table(w_op, w_picked, w_planes)

        turned = psum.tile([P, PACK, P], F32, name="bank%d" % (ROW_TILES - 1))
        for t in range(PACK):
            nc.tensor.transpose(turned[:, t, :], weight_rows[:, t::PACK], identity[:])
        weight = keep([P, ROW_TILES], F32, "weight")
        nc.scalar.copy(out=weight[:].rearrange("p (g t) -> p g t", t=PACK),
                       in_=turned[:, :, :ROW_PASSES].rearrange("p t g -> p g t"))

        x_ops = [operand("x%d" % g) for g in range(ROW_PASSES)]

        def cast_x(g, half, engine, lo=0, hi=P):
            tiles = slice(2 * half, 2 * half + 2)
            copier(engine)(out=x_ops[g][0][:].rearrange("p (t m) j -> p m j t", t=PACK)[:, lo:hi, :, tiles],
                           in_=x_raw[g][:].rearrange("p j (m t) -> p m j t", t=PACK)[:, lo:hi, :, tiles])

        def stats(name):
            return keep([P, ROW_TILES], F32, name)

        def softmax_tile(table, n, neg_max, total, result, parts=(ALL,)):
            g, t = divmod(n, PACK)
            acc = psum.tile([P, N], F32, name="bank%d" % n)
            cols = slice(t * P, (t + 1) * P)
            for slots in parts:
                nc.tensor.matmul_mx(out=acc[:, slots], lhsT=x_ops[g][1][:, cols].bitcast(E4M3),
                                    lhsT_scale=x_ops[g][2][:, cols], rhs=table[1][:, slots].bitcast(E4M3),
                                    rhs_scale=table[2][:, slots], start=True, stop=True)
            nc.vector.tensor_reduce(out=neg_max[:, n:n + 1], in_=acc[:], axis=AXIS_X, op=ALU.max, negate=True)
            nc.scalar.activation(result, acc[:], ACT.Exp, bias=neg_max[:, n:n + 1], accum_out=total[:, n:n + 1])

        def scale_on_gpsimd(target, plane, inv, n):
            nc.gpsimd.tensor_scalar(out=target, in0=plane, scalar1=inv, scalar2=weight[:, n:n + 1],
                                    op0=ALU.mult, op1=ALU.mult)

        s_max, s_sum, s_inv = stats("s_max"), stats("s_sum"), stats("s_inv")
        t_max, t_sum, t_inv, t_fac = stats("t_max"), stats("t_sum"), stats("t_inv"), stats("t_fac")
        student = [keep([P, PACK, N], F32, "student%d" % g) for g in range(ROW_PASSES)]
        teacher = [keep([P, N], F32, "teacher%d" % n) for n in range(ROW_TILES)]
        first_scaled = keep([P, PACK, N], F32, "first_scaled")

        def student_tiles(tiles):
            for n in tiles:
                softmax_tile(w_op, n, s_max, s_sum, student[n // PACK][:, n % PACK, :])

        def scale_student(tiles, inv=s_inv):
            cols = slice(tiles[0], tiles[-1] + 1)
            nc.vector.reciprocal(inv[:, cols], s_sum[:, cols])
            for n in tiles:
                plane = student[n // PACK][:, n % PACK, :]
                scale_on_gpsimd(plane, plane, inv[:, n:n + 1], n)

        v_op = operand("v")
        v_picked = keep([P, PACK, N], F32, "v_picked")

        cast_x(0, 0, "scalar", 0, X_SCALAR_SHARE)
        cast_x(0, 0, "vector", X_SCALAR_SHARE, P)
        cast_x(0, 1, "scalar", 0, X_SCALAR_SHARE)
        cast_x(0, 1, "vector", X_SCALAR_SHARE, P)
        for cols in (slice(0, P), slice(P, HALF), HALVES[1]):
            quantize_part(E4M3, x_ops[0], cols)
        cast_x(1, 0, "scalar")
        for t in (2, 3):
            nc.gpsimd.tensor_copy(out=x_ops[1][0][:, t * P:(t + 1) * P, :],
                                  in_=x_raw[1][:].rearrange("p j (m t) -> p t m j", t=PACK)[:, t])
        student_tiles([0, 1, 2])
        quantize_part(E4M3, x_ops[1], ALL)
        scale_student([0, 1])
        student_tiles([3])
        gather("scalar", v_picked, v_planes, 0, ALL)
        student_tiles([4])
        scale_student([2, 3])
        student_tiles([5, 6, 7])
        scale_student([4, 5])
        gather("vector", v_picked, v_planes, 1, slice(0, V_VECTOR_SHARE))
        gather("scalar", v_picked, v_planes, 1, slice(V_VECTOR_SHARE, N))
        gather("vector", v_picked, v_planes, 2, ALL)
        finish_table(v_op, v_picked, v_planes)

        m_raw = {(g, h): load(m_rows[g][:, :, HALVES[h]], [P, PACK, HALF], "w%d" % (2 * h + g))
                 for h in range(2) for g in range(ROW_PASSES)}
        m_grouped, m_codes = {}, {}
        m_shape = [P, ROW_PASSES * P]
        m_scales = keep([P, BLOCKS, ROW_PASSES * P], U8, "m_scales")

        def cast_m(engine, c, passes=range(ROW_PASSES)):
            for g in passes:
                target = m_grouped[c][:, g * P:(g + 1) * P, :]
                planes = m_raw[g, c // 2][:, :, c % 2 * P:(c % 2 + 1) * P]
                if engine == "gpsimd":
                    nc.gpsimd.tensor_copy(out=target, in_=planes.rearrange("p j m -> p m j"))
                else:
                    interleave(engine, target, planes, 0, P)

        def m_staging(c, name):
            m_grouped[c] = keep([P, ROW_PASSES * P, PACK], BF16, name)[:]

        def quantize_m(c, codes):
            m_codes[c] = codes[:]
            quantize(E4M3, m_codes[c], m_scales[:, c, :], m_grouped[c])

        def teacher_tile(n):
            softmax_tile(v_op, n, t_max, t_sum, teacher[n][:], HALVES if n == 0 else (ALL,))

        def teacher_inv(lo, hi):
            nc.vector.reciprocal(t_inv[:, lo:hi], t_sum[:, lo:hi])

        m_staging(1, "v_picked")
        cast_m("vector", 1, [0])
        v_flat = v_op[0][:].rearrange("p c j -> p (c j)")
        late_inv = v_flat[:, HALF * PACK - 2 * ROW_TILES:HALF * PACK].bitcast(F32)
        scale_student([6], late_inv)
        early_inv = [keep([P, 1], F32, "inv%d" % n) for n in range(PACK)]
        for n in range(ROW_TILES):
            teacher_tile(n)
            if n == 0:
                scale_student([7], late_inv)
            behind = n - 2
            if 0 <= behind < PACK:
                nc.vector.reciprocal(early_inv[behind][:], t_sum[:, behind:behind + 1])
            if 0 <= behind < GPSIMD_TILES:
                scale_on_gpsimd(first_scaled[:, behind, :], teacher[behind][:], early_inv[behind][:], behind)
        m_staging(0, "m0_grouped")
        cast_m("scalar", 0)
        cast_m("scalar", 1, [1])

        g_ops = {}
        scaled = [keep([P, PACK, HALF], F32, "scaled%d" % h)[:] for h in range(2)]

        def factors(tiles):
            for n in tiles:
                nc.scalar.activation(t_fac[:, n:n + 1], t_inv[:, n:n + 1], ACT.Copy, scale=weight[:, n:n + 1])

        def scale_on_scalar(tiles, h):
            for n in tiles:
                nc.scalar.activation(scaled[h][:, n % PACK, :], teacher[n][:, HALVES[h]], ACT.Copy,
                                     scale=t_fac[:, n:n + 1])

        def combine(g, h, staging):
            g_ops[g, h] = operand("g%d%d" % (g, h), HALF, staging)
            other = first_scaled[:, :, HALVES[h]] if g == 0 else scaled[h]
            nc.vector.tensor_tensor(out=woven(g_ops[g, h][0][:]), in0=walk(student[g][:, :, HALVES[h]]),
                                    in1=walk(other), op=ALU.subtract)

        def quantize_g(g, h):
            quantize_part(E5M2, g_ops[g, h], slice(0, HALF))

        def product(c, halves, bank):
            acc = psum.tile([P, len(halves), HALF], F32, name="bank%d" % bank)
            for k, h in enumerate(halves):
                for g in range(ROW_PASSES):
                    block = slice(g * P, (g + 1) * P)
                    nc.tensor.matmul_mx(out=acc[:, k, :], lhsT=m_codes[c][:, block].bitcast(E4M3),
                                        lhsT_scale=m_scales[:, c, block], rhs=g_ops[g, h][1][:].bitcast(E5M2),
                                        rhs_scale=g_ops[g, h][2][:], start=g == 0, stop=g == ROW_PASSES - 1)
            return acc

        def copy_out(engine, c, halves, bank, offset=None):
            acc = product(c, halves, bank)
            shape, name = [P, len(halves) * HALF], "dw%d%d" % (c, halves[0])
            dw = keep(shape, F32, name) if offset is None else place(shape, F32, name, offset)
            copier(engine)(out=dw[:], in_=acc[:].rearrange("p k c -> p (k c)"))
            return dw[:]

        def scatter(engine, c, slots, values):
            indirect_copy(engine, windows[c][:].indirect(listed(slots)), values)

        def store(c):
            if c < BLOCKS - 1:
                nc.sync.dma_start(out=out[c * P:(c + 1) * P, :], in_=windows[c][:])
                return
            for queue, cols in ((nc.sync, slice(0, T // 2)), (nc.scalar, slice(T // 2, T))):
                queue.dma_start(out=out[c * P:(c + 1) * P, cols], in_=windows[c][:, cols])

        teacher_inv(4, 6)
        factors([4, 5])
        scale_on_scalar([4, 5], 0)
        for n in range(GPSIMD_TILES, PACK):
            nc.vector.tensor_scalar(out=first_scaled[:, n, :], in0=teacher[n][:], scalar1=early_inv[n][:],
                                    scalar2=weight[:, n:n + 1], op0=ALU.mult, op1=ALU.mult)
        quantize_m(0, keep(m_shape, U32, "v_codes"))
        combine(0, 0, "g_staging0")
        teacher_inv(6, 8)
        factors([6, 7])
        scale_on_scalar([6, 7], 0)
        combine(0, 1, "g_staging1")
        scale_on_scalar([4, 5, 6, 7], 1)
        quantize_g(0, 0)
        combine(1, 0, "g_staging2")
        quantize_g(0, 1)
        quantize_g(1, 0)
        m_staging(2, "g_staging0")
        cast_m("scalar", 2)
        scatter("scalar", 0, HALVES[0], copy_out("scalar", 0, [0], 0))
        quantize_m(1, keep(m_shape, U32, "first_scaled"))
        combine(1, 1, "g_staging2")
        quantize_m(2, keep(m_shape, U32, "m2_codes"))
        quantize_g(1, 1)
        scatter("vector", 0, HALVES[1], copy_out("vector", 0, [1], 1, 512))
        store(0)
        scatter("scalar", 1, HALVES[0], copy_out("vector", 1, [0], 2))
        m_staging(3, "g_staging2")
        cast_m("gpsimd", 3)
        scatter("scalar", 1, HALVES[1], copy_out("scalar", 1, [1], 3))
        store(1)
        both = copy_out("vector", 2, [0, 1], 2, 1024)
        quantize_m(3, place(m_shape, U32, "m3_codes", 0))
        scatter("vector", 2, ALL, both)
        store(2)
        for h in range(2):
            scatter("scalar", 3, HALVES[h], copy_out("scalar", 3, [h], 4 + h))
        store(3)
